import numpy as np
import ml_dtypes


def mxq(x, axis, fmt="e4m3"):
    dtype, down = {"e4m3": (ml_dtypes.float8_e4m3fn, 7), "e5m2": (ml_dtypes.float8_e5m2, 14)}[fmt]
    v = np.moveaxis(np.asarray(x, np.float32).astype(ml_dtypes.bfloat16).astype(np.float64), axis, -1)
    blocks = v.reshape(v.shape[:-1] + (-1, 32))
    amax = np.abs(blocks).max(-1, keepdims=True)
    byte = np.maximum(np.where(amax > 0, np.frexp(amax)[1] - 1 + 127, 0) - down, 1)
    scale = np.exp2(byte - 127.0)
    codes = (blocks / scale).astype(np.float32).astype(dtype).astype(np.float64)
    return np.moveaxis((codes * scale).reshape(v.shape), -1, axis)


WIDE = False


def mx_kscale(k):
    if not WIDE:
        return np.ones(k)
    levels = np.array([10, -10, 5, -5, 0])
    if k % 512:
        return np.exp2(np.random.permutation(np.resize(levels, k // 32))).repeat(32)
    a = np.empty((k // 512, 16))
    for p in range(k // 512):
        a[p, :8] = np.random.permutation(np.resize(levels, 8))
        for g in range(8):
            far = levels[np.abs(levels - a[p, g]) >= 10]
            a[p, g + 8] = far[np.random.randint(len(far))]
    return np.exp2(a.ravel()).repeat(32)


def f64(x):
    return np.asarray(x).astype(np.float64)


def striped(idx):
    return np.tile(idx.reshape(-1, 16).T, (8, 1)).astype(np.uint16)


def unstriped(offs):
    return offs[:16].T.reshape(-1).astype(np.int64)


E2M1 = np.array([0.0, 0.5, 1.0, 1.5, 2.0, 3.0, 4.0, 6.0, -0.0, -0.5, -1.0, -1.5, -2.0, -3.0, -4.0, -6.0])


def pack_weight(w, fmt):
    k, n = w.shape
    w = f64(np.asarray(w, np.float32).astype(ml_dtypes.bfloat16)).reshape(k // 32, 32, n)
    amax = np.abs(w).max(1)
    if fmt == "e4m3":
        byte = np.frexp(amax)[1] - 1 + 127 - 7
    else:
        mant, ex = np.frexp(amax / 6.0)
        byte = np.where(mant > 0.5, ex, ex - 1) + 127
    byte = np.clip(np.where(amax > 0, byte, 1), 1, 254)
    scaled = (w * np.exp2(127.0 - byte)[:, None, :]).reshape(k, n).astype(np.float32)
    by_word = np.ascontiguousarray(scaled.reshape(k // 512, 128, 4, n).transpose(0, 1, 3, 2))
    if fmt == "e4m3":
        words = by_word.astype(ml_dtypes.float8_e4m3fn).view(np.uint8)
    else:
        c = by_word.astype(ml_dtypes.float4_e2m1fn).view(np.uint8) & 0xF
        words = (c[..., 0::2] | (c[..., 1::2] << 4)).reshape(k // 512, 128, 2 * n)
    return np.ascontiguousarray(words), np.ascontiguousarray(byte.astype(np.uint8).reshape(k // 512, 16, n))


def unpack_weight(words, scales, fmt):
    g, _, n = scales.shape
    words = np.ascontiguousarray(words).reshape(g, 128, n, -1)
    if fmt == "e4m3":
        vals = words.view(ml_dtypes.float8_e4m3fn).astype(np.float64)
    else:
        nib = np.empty((g, 128, n, 4), np.uint8)
        nib[..., 0::2] = words & 0xF
        nib[..., 1::2] = words >> 4
        vals = E2M1[nib]
    vals = vals * np.repeat(np.exp2(scales.astype(np.float64) - 127.0), 8, axis=1)[..., None]
    return vals.transpose(0, 1, 3, 2).reshape(g * 512, n)


def gelu(v):
    return 0.5 * v * (1.0 + np.tanh(np.sqrt(2.0 / np.pi) * (v + 0.044715 * v**3)))


T, S, K, H, N = 4096, 1024, 1024, 1024, 512

def setup_inputs():
    n = np.random.standard_normal
    s = mx_kscale(K)[:, None]
    u = mx_kscale(H)[:, None]
    tab_words, tab_scales = pack_weight(n((K, T)) * s, "e4m3")
    w4_words, w4_scales = pack_weight(n((K, H)) / np.sqrt(K) / s * u.T, "e2m1")
    w8_words, w8_scales = pack_weight(n((H, N)) / np.sqrt(H) / u, "e4m3")
    return {
        "tab_words": tab_words, "tab_scales": tab_scales,
        "offs": striped(np.random.permutation(T)[:S]),
        "w1": (n((K, H)) / np.sqrt(K) / s * u.T).astype(np.float32),
        "w4_words": w4_words, "w4_scales": w4_scales,
        "rel": (n((H, S)) * u).astype(np.float32),
        "w8_words": w8_words, "w8_scales": w8_scales,
        "offs2": striped(np.random.permutation(S)),
        "wgo": np.exp(0.3 * n((128, S))).astype(np.float32),
        "x0": n((N, S)).astype(np.float32),
    }

def reference(tab_words, tab_scales, offs, w1, w4_words, w4_scales, rel,
              w8_words, w8_scales, offs2, wgo, x0):
    v = unpack_weight(tab_words, tab_scales, "e4m3")[:, unstriped(offs)]
    mould = mxq(f64(w1), 0, "e4m3").T @ v
    melt = unpack_weight(w4_words, w4_scales, "e2m1").T @ v
    h = np.maximum(mould, melt) - f64(rel)
    y = unpack_weight(w8_words, w8_scales, "e4m3").T @ mxq(h, 0, "e4m3")
    page = np.zeros((N, S))
    page[:, unstriped(offs2)] = np.tile(f64(wgo), (N // 128, 1)) * y
    return np.maximum(page, f64(x0))

@@ -1,0 +1,284 @@
+from contextlib import ExitStack
+
+import concourse.mybir as mybir
+
+T, S, K, H, N = 4096, 1024, 1024, 1024, 512
+FLOPS = 2 * S * (2 * K * H + H * N)
+
+F32 = mybir.dt.float32
+BF16 = mybir.dt.bfloat16
+I32 = mybir.dt.int32
+U32 = mybir.dt.uint32
+U16 = mybir.dt.uint16
+U8 = mybir.dt.uint8
+FP8X4 = mybir.dt.float8_e4m3fn_x4
+FP4X4 = mybir.dt.float4_e2m1fn_x4
+ALU = mybir.AluOpType
+
+P = 128
+PACK = 4
+KP = P * PACK
+HALF = 512
+QW = 256
+NQ = S // QW
+
+
+def tile_list_foundry_job_dispatch_kernel(
+    tc, tab_words, tab_scales, offs, w1, w4_words, w4_scales, rel, w8_words, w8_scales, offs2, wgo, x0, out
+):
+    nc = tc.nc
+    with ExitStack() as ctx:
+        keep = ctx.enter_context(tc.tile_pool(name="keep", bufs=1))
+        ring = ctx.enter_context(tc.tile_pool(name="ring", bufs=2))
+        psum = ctx.enter_context(tc.psum_pool(name="psum", bufs=2))
+
+        def held(shape, dtype, name):
+            return keep.tile(shape, dtype, name=name, align_bytes=64)
+
+        picks = keep.tile([P, S // 16], U16, name="picks")
+        places = keep.tile([P, S // 16], U16, name="places")
+        tab_w = [held([P, T], I32, f"tab_w{a}") for a in range(2)]
+        tab_s = held([P, T], U8, "tab_s")
+        v_w = [held([P, S], U32, f"v_w{a}") for a in range(2)]
+        v_s = [held([P, S], U8, f"v_s{a}") for a in range(2)]
+        w4_raw = held([P, 2, 2 * H], U8, "w4_raw")
+        w4_w = held([P, 2, 2 * H], U8, "w4_w")
+        w4_sraw = held([P, 2, H], U8, "w4_sraw")
+        w4_s = held([P, 2, H], U8, "w4_s")
+        w8_w = held([P, 2, N], I32, "w8_w")
+        w8_s = held([P, N], U8, "w8_s")
+        gains = held([P, S], F32, "gains")
+        page = [held([P, S], F32, f"page{n}") for n in range(N // P)]
+
+        nc.vector.memset(tab_s[:].bitcast(I32), 0)
+        nc.vector.memset(w4_sraw[:].bitcast(I32), 0)
+        nc.vector.memset(v_s[1][:].bitcast(I32), 0)
+        nc.vector.memset(w8_s[:].bitcast(I32), 0)
+        for g in range(4):
+            nc.scalar.dma_start(
+                out=tab_s[32 * g : 32 * g + 8, :].bitcast(I32), in_=tab_scales[:, 4 * g : 4 * g + 4, :].bitcast(I32)
+            )
+        for g in range(4):
+            nc.gpsimd.dma_start(
+                out=w4_sraw[32 * g : 32 * g + 4, :, :].bitcast(I32),
+                in_=w4_scales[:, 4 * g : 4 * g + 4, :].rearrange("a r c -> r a c").bitcast(I32),
+            )
+
+        nc.sync.dma_start(picks[:], offs)
+        nc.sync.dma_start(places[:], offs2)
+
+        def load_table(a, pieces):
+            words = tab_words[a].rearrange("p t i -> p (t i)").bitcast(I32)
+            for c in range(0, T, T // pieces):
+                nc.sync.dma_start(out=tab_w[a][:, c : c + T // pieces], in_=words[:, c : c + T // pieces])
+
+        load_table(0, 8)
+        nc.sync.dma_start(out=w4_raw[:].bitcast(I32), in_=w4_words.rearrange("a p c -> p a c").bitcast(I32))
+        load_table(1, 4)
+        w1_raw = {}
+        for b in range(2):
+            for a in range(2):
+                raw = ring.tile([P, PACK, KP], F32, name="raw", bufs=4, align_bytes=64)
+                rows = w1[a * KP : (a + 1) * KP, b * KP : (b + 1) * KP].rearrange("(p j) c -> p j c", j=PACK)
+                for j in range(0, PACK, 2):
+                    nc.sync.dma_start(out=raw[:, j : j + 2, :], in_=rows[:, j : j + 2, :])
+                w1_raw[a, b] = raw
+        rel_sb = {}
+
+        def load_rel(q):
+            for b in range(2):
+                rel_sb[b, q] = held([P, PACK, QW], F32, f"rel{b}{q}")
+                nc.sync.dma_start(
+                    out=rel_sb[b, q][:],
+                    in_=rel[b * KP : (b + 1) * KP, q * QW : (q + 1) * QW].rearrange("(p t) j -> p t j", t=PACK),
+                )
+
+        load_rel(0)
+        nc.sync.dma_start(out=w8_w[:], in_=w8_words.rearrange("a p c i -> p a (c i)").bitcast(I32))
+        load_rel(1)
+        nc.sync.dma_start(out=gains[:], in_=wgo)
+        load_rel(2)
+        load_rel(3)
+
+        nc.vector.tensor_copy(v_s[0][:], tab_s[:].indirect(picks[:]))
+        for g in range(4):
+            nc.scalar.dma_start(
+                out=v_s[1][32 * g : 32 * g + 4, :].bitcast(I32), in_=v_s[0][32 * g + 4 : 32 * g + 8, :].bitcast(I32)
+            )
+        for g in range(4):
+            nc.gpsimd.dma_start(
+                out=w8_s[32 * g : 32 * g + 8, :].bitcast(I32), in_=w8_scales[:, 4 * g : 4 * g + 4, :].bitcast(I32)
+            )
+        nc.vector.tensor_copy(v_w[0][:], tab_w[0][:].bitcast(U32).indirect(picks[:]))
+        nc.vector.tensor_copy(
+            w4_w[:].bitcast(U16).rearrange("p a (b t m) -> p (a b) t m", t=PACK, m=P),
+            w4_raw[:].bitcast(U16).rearrange("p a (b m t) -> p (a b) t m", t=PACK, m=P),
+        )
+        nc.vector.tensor_copy(
+            w4_s[:].rearrange("p a (b t m) -> p (a b) t m", t=PACK, m=P),
+            w4_sraw[:].rearrange("p a (b m t) -> p (a b) t m", t=PACK, m=P),
+        )
+        for h in range(2):
+            nc.vector.tensor_copy(
+                v_w[1][:, h * HALF : (h + 1) * HALF],
+                tab_w[1][:].bitcast(U32).indirect(picks[:, h * HALF // 16 : (h + 1) * HALF // 16]),
+            )
+
+        melt = {}
+
+        def melt_block(b, h):
+            melt[b, h] = held([P, PACK, HALF], F32, f"melt{b}{h}")
+            cols = slice(h * HALF, (h + 1) * HALF)
+            for t in range(PACK):
+                acc = psum.tile([P, HALF], F32, name="melt_acc", bufs=2)
+                c0 = b * KP + t * P
+                for a in range(2):
+                    nc.tensor.matmul_mx(
+                        out=acc[:],
+                        lhsT=w4_w[:, a, 2 * c0 : 2 * (c0 + P)].bitcast(FP4X4),
+                        lhsT_scale=w4_s[:, a, c0 : c0 + P],
+                        rhs=v_w[a][:, cols].bitcast(FP8X4),
+                        rhs_scale=v_s[a][:, cols],
+                        start=(a == 0),
+                        stop=(a == 1),
+                    )
+                nc.scalar.copy(out=melt[b, h][:, t, :], in_=acc[:])
+
+        w1_bf = {}
+        w1_w = {}
+        w1_s = {}
+
+        def cast_w1(a, b, on_vector):
+            w1_bf[a, b] = ring.tile([P, PACK, P, PACK], BF16, name="w1_bf", bufs=2, align_bytes=64)
+            dst = w1_bf[a, b][:].rearrange("p t m j -> p m j t")
+            src = w1_raw[a, b][:].rearrange("p j (m t) -> p m j t", t=PACK)
+            if on_vector:
+                nc.vector.tensor_copy(out=dst, in_=src)
+            else:
+                nc.scalar.copy(out=dst, in_=src)
+
+        def quantise_w1(a, b):
+            w1_w[a, b] = held([P, KP], U32, f"w1_w{a}{b}")
+            w1_s[a, b] = held([P, KP], U8, f"w1_s{a}{b}")
+            nc.vector.quantize_mx(
+                out=w1_w[a, b][:].bitcast(FP8X4),
+                scales=w1_s[a, b][:],
+                in_=w1_bf[a, b][:].rearrange("p t m j -> p (t m j)"),
+            )
+
+        later = {}
+
+        def mould_and_max(b, q):
+            later[b, q] = ring.tile([P, PACK, QW], F32, name="later", bufs=3, align_bytes=64)
+            cols = slice(q * QW, (q + 1) * QW)
+            h, within = divmod(q * QW, HALF)
+            for pair in range(2):
+                acc = psum.tile([P, 2, QW], F32, name="mould_acc", bufs=3)
+                for i in range(2):
+                    t = 2 * pair + i
+                    for a in range(2):
+                        nc.tensor.matmul_mx(
+                            out=acc[:, i, :],
+                            lhsT=w1_w[a, b][:, t * P : (t + 1) * P].bitcast(FP8X4),
+                            lhsT_scale=w1_s[a, b][:, t * P : (t + 1) * P],
+                            rhs=v_w[a][:, cols].bitcast(FP8X4),
+                            rhs_scale=v_s[a][:, cols],
+                            start=(a == 0),
+                            stop=(a == 1),
+                        )
+                nc.vector.tensor_tensor(
+                    later[b, q][:, 2 * pair : 2 * pair + 2, :],
+                    acc[:],
+                    melt[b, h][:, 2 * pair : 2 * pair + 2, within : within + QW],
+                    ALU.max,
+                )
+
+        h_bf = {}
+        h_w = {}
+        h_s = {}
+
+        def subtract(b, q):
+            h_bf[b, q] = ring.tile([P, QW, PACK], BF16, name="h_bf", bufs=3, align_bytes=64)
+            nc.vector.tensor_tensor(
+                h_bf[b, q][:].rearrange("p (c i) t -> p c t i", i=4),
+                later[b, q][:].rearrange("p t (c i) -> p c t i", i=4),
+                rel_sb[b, q][:].rearrange("p t (c i) -> p c t i", i=4),
+                ALU.subtract,
+            )
+
+        def quantise_h(b, q):
+            h_w[b, q] = ring.tile([P, QW], U32, name="h_w", bufs=4, align_bytes=64)
+            h_s[b, q] = ring.tile([P, QW], U8, name="h_s", bufs=4, align_bytes=64)
+            nc.vector.quantize_mx(
+                out=h_w[b, q][:].bitcast(FP8X4), scales=h_s[b, q][:], in_=h_bf[b, q][:].rearrange("p j t -> p (j t)")
+            )
+
+        def finish(q):
+            cols = slice(q * QW, (q + 1) * QW)
+            for pair in range(2):
+                acc = psum.tile([P, 2, QW], F32, name="y_acc", bufs=2)
+                for i in range(2):
+                    n = 2 * pair + i
+                    for b in range(2):
+                        nc.tensor.matmul_mx(
+                            out=acc[:, i, :],
+                            lhsT=w8_w[:, b, n * P : (n + 1) * P].bitcast(FP8X4),
+                            lhsT_scale=w8_s[4 * b :, n * P : (n + 1) * P],
+                            rhs=h_w[b, q][:].bitcast(FP8X4),
+                            rhs_scale=h_s[b, q][:],
+                            start=(b == 0),
+                            stop=(b == 1),
+                        )
+                y = ring.tile([P, 2, QW], F32, name="y", bufs=4, align_bytes=64)
+                nc.scalar.copy(out=y[:], in_=acc[:])
+                for i in range(2):
+                    nc.vector.tensor_tensor(
+                        page[2 * pair + i][:].indirect(places[:, q * QW // 16 : (q + 1) * QW // 16]),
+                        y[:, i, :],
+                        gains[:, cols],
+                        ALU.mult,
+                    )
+
+        melt_block(0, 0)
+        cast_w1(0, 0, True)
+        cast_w1(1, 0, False)
+        quantise_w1(0, 0)
+        quantise_w1(1, 0)
+        melt_block(1, 0)
+        cast_w1(0, 1, False)
+        cast_w1(1, 1, True)
+        mould_and_max(0, 0)
+        quantise_w1(0, 1)
+        quantise_w1(1, 1)
+        subtract(0, 0)
+        mould_and_max(1, 0)
+        quantise_h(0, 0)
+        subtract(1, 0)
+        mould_and_max(0, 1)
+        quantise_h(1, 0)
+        melt_block(0, 1)
+        melt_block(1, 1)
+
+        promised = []
+        for pair in range(2):
+            both = ring.tile([P, 2, S], F32, name="raw", bufs=4, align_bytes=64)
+            nc.sync.dma_start(
+                out=both[:], in_=x0[2 * pair * P : 2 * (pair + 1) * P, :].rearrange("(i p) m -> p i m", p=P)
+            )
+            promised.append(both)
+
+        for q in range(NQ):
+            if q + 1 < NQ:
+                if q > 0:
+                    mould_and_max(0, q + 1)
+                subtract(0, q + 1)
+                mould_and_max(1, q + 1)
+                quantise_h(0, q + 1)
+                subtract(1, q + 1)
+                quantise_h(1, q + 1)
+            finish(q)
+
+        for n in range(N // P):
+            result = promised[n // 2][:, n % 2, :]
+            nc.vector.tensor_tensor(result, page[n][:], result, ALU.max)
+            nc.sync.dma_start(out=out[n * P : (n + 1) * P, :], in_=result)

@@ -1,6 +1,7 @@
 from contextlib import ExitStack
 
 import concourse.mybir as mybir
+from concourse.masks import make_identity
 
 T, S, K, H, N = 4096, 1024, 1024, 1024, 512
 FLOPS = 2 * S * (2 * K * H + H * N)
@@ -14,6 +15,7 @@ U8 = mybir.dt.uint8
 FP8X4 = mybir.dt.float8_e4m3fn_x4
 FP4X4 = mybir.dt.float4_e2m1fn_x4
 ALU = mybir.AluOpType
+COPY = mybir.ActivationFunctionType.Copy
 
 P = 128
 PACK = 4
@@ -21,6 +23,10 @@ KP = P * PACK
 HALF = 512
 QW = 256
 NQ = S // QW
+ON_VECTOR = (0, 1)
+MELTB = (0, 1, 5)
+MOULDB = (2, 3, 4)
+TURNB = (5, 0, 1)
 
 
 def tile_list_foundry_job_dispatch_kernel(
@@ -40,7 +46,8 @@ def tile_list_foundry_job_dispatch_kernel(
         tab_w = [held([P, T], I32, f"tab_w{a}") for a in range(2)]
         tab_s = held([P, T], U8, "tab_s")
         v_w = [held([P, S], U32, f"v_w{a}") for a in range(2)]
-        v_s = [held([P, S], U8, f"v_s{a}") for a in range(2)]
+        picked_s = held([P, S], U8, "picked_s")
+        v_s = held([P, 2, S], U8, "v_s")
         w4_raw = held([P, 2, 2 * H], U8, "w4_raw")
         w4_w = held([P, 2, 2 * H], U8, "w4_w")
         w4_sraw = held([P, 2, H], U8, "w4_sraw")
@@ -50,31 +57,40 @@ def tile_list_foundry_job_dispatch_kernel(
         gains = held([P, S], F32, "gains")
         page = [held([P, S], F32, f"page{n}") for n in range(N // P)]
 
-        nc.vector.memset(tab_s[:].bitcast(I32), 0)
+        ident = held([P, P], F32, "ident")
         nc.vector.memset(w4_sraw[:].bitcast(I32), 0)
-        nc.vector.memset(v_s[1][:].bitcast(I32), 0)
+        for g in range(4):
+            nc.vector.memset(tab_s[32 * g : 32 * g + 24, :].bitcast(I32), 0)
+        nc.vector.memset(v_s[:].bitcast(I32), 0)
         nc.vector.memset(w8_s[:].bitcast(I32), 0)
-        for g in range(4):
-            nc.scalar.dma_start(
-                out=tab_s[32 * g : 32 * g + 8, :].bitcast(I32), in_=tab_scales[:, 4 * g : 4 * g + 4, :].bitcast(I32)
-            )
-        for g in range(4):
-            nc.gpsimd.dma_start(
-                out=w4_sraw[32 * g : 32 * g + 4, :, :].bitcast(I32),
-                in_=w4_scales[:, 4 * g : 4 * g + 4, :].rearrange("a r c -> r a c").bitcast(I32),
-            )
 
+        make_identity(nc, ident[:])
         nc.sync.dma_start(picks[:], offs)
-        nc.sync.dma_start(places[:], offs2)
+        for g in range(4):
+            nc.sync.dma_start(
+                out=tab_s[32 * g + 24 : 32 * g + 32, :].bitcast(I32),
+                in_=tab_scales[:, 4 * g : 4 * g + 4, :].bitcast(I32),
+            )
 
         def load_table(a, pieces):
             words = tab_words[a].rearrange("p t i -> p (t i)").bitcast(I32)
             for c in range(0, T, T // pieces):
                 nc.sync.dma_start(out=tab_w[a][:, c : c + T // pieces], in_=words[:, c : c + T // pieces])
 
-        load_table(0, 8)
+        load_table(0, 2)
         nc.sync.dma_start(out=w4_raw[:].bitcast(I32), in_=w4_words.rearrange("a p c -> p a c").bitcast(I32))
-        load_table(1, 4)
+        for g in range(4):
+            nc.sync.dma_start(
+                out=w4_sraw[32 * g : 32 * g + 4, :, :].bitcast(I32),
+                in_=w4_scales[:, 4 * g : 4 * g + 4, :].rearrange("a r c -> r a c").bitcast(I32),
+            )
+        nc.vector.tensor_copy(picked_s[:], tab_s[:].indirect(picks[:]))
+        for a in range(2):
+            first = 24 + 4 * a
+            nc.scalar.dma_start(
+                out=v_s[0:100, a, :].bitcast(I32), in_=picked_s[first : first + 100, :].bitcast(I32)
+            )
+        load_table(1, 2)
         w1_raw = {}
         for b in range(2):
             for a in range(2):
@@ -94,21 +110,17 @@ def tile_list_foundry_job_dispatch_kernel(
                 )
 
         load_rel(0)
-        nc.sync.dma_start(out=w8_w[:], in_=w8_words.rearrange("a p c i -> p a (c i)").bitcast(I32))
+        for g in range(4):
+            nc.sync.dma_start(
+                out=w8_s[32 * g : 32 * g + 8, :].bitcast(I32), in_=w8_scales[:, 4 * g : 4 * g + 4, :].bitcast(I32)
+            )
         load_rel(1)
+        nc.sync.dma_start(out=w8_w[:], in_=w8_words.rearrange("a p c i -> p a (c i)").bitcast(I32))
+        nc.sync.dma_start(places[:], offs2)
         nc.sync.dma_start(out=gains[:], in_=wgo)
         load_rel(2)
         load_rel(3)
 
-        nc.vector.tensor_copy(v_s[0][:], tab_s[:].indirect(picks[:]))
-        for g in range(4):
-            nc.scalar.dma_start(
-                out=v_s[1][32 * g : 32 * g + 4, :].bitcast(I32), in_=v_s[0][32 * g + 4 : 32 * g + 8, :].bitcast(I32)
-            )
-        for g in range(4):
-            nc.gpsimd.dma_start(
-                out=w8_s[32 * g : 32 * g + 8, :].bitcast(I32), in_=w8_scales[:, 4 * g : 4 * g + 4, :].bitcast(I32)
-            )
         nc.vector.tensor_copy(v_w[0][:], tab_w[0][:].bitcast(U32).indirect(picks[:]))
         nc.vector.tensor_copy(
             w4_w[:].bitcast(U16).rearrange("p a (b t m) -> p (a b) t m", t=PACK, m=P),
@@ -124,13 +136,21 @@ def tile_list_foundry_job_dispatch_kernel(
                 tab_w[1][:].bitcast(U32).indirect(picks[:, h * HALF // 16 : (h + 1) * HALF // 16]),
             )
 
+        banks = [psum.tile([P, HALF], F32, name=f"bank{i}", bufs=1) for i in range(8)]
+        bank_x, bank_z = banks[6], banks[7]
+        taken = []
+
+        def next_bank(choices):
+            taken.append(choices)
+            return banks[choices[(len([c for c in taken if c == choices]) - 1) % len(choices)]]
+
         melt = {}
 
         def melt_block(b, h):
-            melt[b, h] = held([P, PACK, HALF], F32, f"melt{b}{h}")
+            melt[b, h] = held([P, HALF // QW, PACK, QW], F32, f"melt{b}{h}")
             cols = slice(h * HALF, (h + 1) * HALF)
             for t in range(PACK):
-                acc = psum.tile([P, HALF], F32, name="melt_acc", bufs=2)
+                acc = next_bank(MELTB)
                 c0 = b * KP + t * P
                 for a in range(2):
                     nc.tensor.matmul_mx(
@@ -138,18 +158,18 @@ def tile_list_foundry_job_dispatch_kernel(
                         lhsT=w4_w[:, a, 2 * c0 : 2 * (c0 + P)].bitcast(FP4X4),
                         lhsT_scale=w4_s[:, a, c0 : c0 + P],
                         rhs=v_w[a][:, cols].bitcast(FP8X4),
-                        rhs_scale=v_s[a][:, cols],
+                        rhs_scale=v_s[:, a, cols],
                         start=(a == 0),
                         stop=(a == 1),
                     )
-                nc.scalar.copy(out=melt[b, h][:, t, :], in_=acc[:])
+                nc.scalar.activation(out=melt[b, h][:, :, t, :], in_=acc[:].rearrange("p (q j) -> p q j", j=QW), func=COPY, scale=-1.0)
 
         w1_bf = {}
         w1_w = {}
         w1_s = {}
 
         def cast_w1(a, b, on_vector):
-            w1_bf[a, b] = ring.tile([P, PACK, P, PACK], BF16, name="w1_bf", bufs=2, align_bytes=64)
+            w1_bf[a, b] = ring.tile([P, PACK, P, PACK], BF16, name="w1_bf", bufs=3, align_bytes=64)
             dst = w1_bf[a, b][:].rearrange("p t m j -> p m j t")
             src = w1_raw[a, b][:].rearrange("p j (m t) -> p m j t", t=PACK)
             if on_vector:
@@ -169,11 +189,11 @@ def tile_list_foundry_job_dispatch_kernel(
         later = {}
 
         def mould_and_max(b, q):
-            later[b, q] = ring.tile([P, PACK, QW], F32, name="later", bufs=3, align_bytes=64)
             cols = slice(q * QW, (q + 1) * QW)
-            h, within = divmod(q * QW, HALF)
+            h, within = divmod(q, HALF // QW)
+            later[b, q] = melt[b, h][:, within]
             for pair in range(2):
-                acc = psum.tile([P, 2, QW], F32, name="mould_acc", bufs=3)
+                acc = next_bank(MOULDB)[:].rearrange("p (i j) -> p i j", i=2)
                 for i in range(2):
                     t = 2 * pair + i
                     for a in range(2):
@@ -182,33 +202,60 @@ def tile_list_foundry_job_dispatch_kernel(
                             lhsT=w1_w[a, b][:, t * P : (t + 1) * P].bitcast(FP8X4),
                             lhsT_scale=w1_s[a, b][:, t * P : (t + 1) * P],
                             rhs=v_w[a][:, cols].bitcast(FP8X4),
-                            rhs_scale=v_s[a][:, cols],
+                            rhs_scale=v_s[:, a, cols],
                             start=(a == 0),
                             stop=(a == 1),
                         )
-                nc.vector.tensor_tensor(
-                    later[b, q][:, 2 * pair : 2 * pair + 2, :],
-                    acc[:],
-                    melt[b, h][:, 2 * pair : 2 * pair + 2, within : within + QW],
-                    ALU.max,
-                )
+                dst = later[b, q][:, 2 * pair : 2 * pair + 2, :]
+                neg_melt = dst
+                if q in ON_VECTOR:
+                    nc.vector.scalar_tensor_tensor(dst, neg_melt, -1.0, acc, ALU.mult, ALU.max)
+                else:
+                    nc.vector.scalar_tensor_tensor(dst, acc, -1.0, neg_melt, ALU.mult, ALU.min)
 
         h_bf = {}
         h_w = {}
         h_s = {}
 
         def subtract(b, q):
-            h_bf[b, q] = ring.tile([P, QW, PACK], BF16, name="h_bf", bufs=3, align_bytes=64)
+            h_bf[b, q] = ring.tile([P, QW, PACK], BF16, name="h_bf", bufs=4, align_bytes=64)
+            if q not in ON_VECTOR:
+                turned = []
+                for jb in range(QW // P):
+                    acc = next_bank(TURNB)[:].rearrange("j (t p) -> j t p", t=PACK)
+                    jcols = slice(jb * P, (jb + 1) * P)
+                    for t in range(PACK):
+                        nc.tensor.matmul(
+                            acc[:, t, :], later[b, q][:, t, jcols], ident[:], start=True, stop=False, is_transpose=True
+                        )
+                        nc.tensor.matmul(
+                            acc[:, t, :], rel_sb[b, q][:, t, jcols], ident[:], start=False, stop=True, is_transpose=True
+                        )
+                    rows = ring.tile([P, 2, P, 2], BF16, name="h_rows", bufs=3, align_bytes=64)
+                    nc.scalar.activation(
+                        out=rows[:], in_=acc.rearrange("j (u e) p -> j u p e", e=2), func=COPY, scale=-1.0
+                    )
+                    turned.append(rows)
+                back = (bank_z, bank_x)[b][:].rearrange("p (jb u j) -> p jb u j", u=2, j=P)
+                for jb in range(QW // P):
+                    words = turned[jb][:].rearrange("j u p e -> j u (p e)").bitcast(F32)
+                    for u in range(2):
+                        nc.tensor.transpose(back[:, jb, u, :], words[:, u, :], ident[:])
+                nc.scalar.copy(
+                    out=h_bf[b, q][:].bitcast(F32).rearrange("p (jb j) u -> p jb j u", j=P),
+                    in_=back.rearrange("p jb u j -> p jb j u"),
+                )
+                return
             nc.vector.tensor_tensor(
                 h_bf[b, q][:].rearrange("p (c i) t -> p c t i", i=4),
-                later[b, q][:].rearrange("p t (c i) -> p c t i", i=4),
+                later[b, q].rearrange("p t (c i) -> p c t i", i=4),
                 rel_sb[b, q][:].rearrange("p t (c i) -> p c t i", i=4),
                 ALU.subtract,
             )
 
         def quantise_h(b, q):
-            h_w[b, q] = ring.tile([P, QW], U32, name="h_w", bufs=4, align_bytes=64)
-            h_s[b, q] = ring.tile([P, QW], U8, name="h_s", bufs=4, align_bytes=64)
+            h_w[b, q] = ring.tile([P, QW], U32, name="h_w", bufs=6, align_bytes=64)
+            h_s[b, q] = ring.tile([P, QW], U8, name="h_s", bufs=6, align_bytes=64)
             nc.vector.quantize_mx(
                 out=h_w[b, q][:].bitcast(FP8X4), scales=h_s[b, q][:], in_=h_bf[b, q][:].rearrange("p j t -> p (j t)")
             )
@@ -216,21 +263,21 @@ def tile_list_foundry_job_dispatch_kernel(
         def finish(q):
             cols = slice(q * QW, (q + 1) * QW)
             for pair in range(2):
-                acc = psum.tile([P, 2, QW], F32, name="y_acc", bufs=2)
+                acc = (next_bank(MOULDB) if (q, pair) < (1, 1) else bank_z if (q, pair) == (NQ - 1, 1) else bank_x)[:].rearrange("p (i j) -> p i j", i=2)
                 for i in range(2):
                     n = 2 * pair + i
-                    for b in range(2):
+                    for b in (1, 0):
                         nc.tensor.matmul_mx(
                             out=acc[:, i, :],
                             lhsT=w8_w[:, b, n * P : (n + 1) * P].bitcast(FP8X4),
                             lhsT_scale=w8_s[4 * b :, n * P : (n + 1) * P],
                             rhs=h_w[b, q][:].bitcast(FP8X4),
                             rhs_scale=h_s[b, q][:],
-                            start=(b == 0),
-                            stop=(b == 1),
+                            start=(b == 1),
+                            stop=(b == 0),
                         )
-                y = ring.tile([P, 2, QW], F32, name="y", bufs=4, align_bytes=64)
-                nc.scalar.copy(out=y[:], in_=acc[:])
+                y = ring.tile([P, 2, QW], F32, name="y", bufs=6, align_bytes=64)
+                nc.scalar.copy(out=y[:], in_=acc)
                 for i in range(2):
                     nc.vector.tensor_tensor(
                         page[2 * pair + i][:].indirect(places[:, q * QW // 16 : (q + 1) * QW // 16]),
@@ -241,23 +288,33 @@ def tile_list_foundry_job_dispatch_kernel(
 
         melt_block(0, 0)
         cast_w1(0, 0, True)
-        cast_w1(1, 0, False)
         quantise_w1(0, 0)
+        cast_w1(1, 0, True)
         quantise_w1(1, 0)
-        melt_block(1, 0)
-        cast_w1(0, 1, False)
-        cast_w1(1, 1, True)
         mould_and_max(0, 0)
+        mould_and_max(0, 1)
+        cast_w1(0, 1, False)
+        melt_block(0, 1)
+        cast_w1(1, 1, False)
+        melt_block(1, 0)
         quantise_w1(0, 1)
         quantise_w1(1, 1)
-        subtract(0, 0)
-        mould_and_max(1, 0)
-        quantise_h(0, 0)
-        subtract(1, 0)
-        mould_and_max(0, 1)
-        quantise_h(1, 0)
-        melt_block(0, 1)
+        mould_and_max(0, 2)
+        mould_and_max(0, 3)
         melt_block(1, 1)
+        mould_and_max(1, 0)
+        mould_and_max(1, 1)
+        subtract(0, 0)
+        subtract(1, 0)
+        quantise_h(0, 0)
+        quantise_h(1, 0)
+        mould_and_max(1, 2)
+        mould_and_max(1, 3)
+        subtract(0, 1)
+        quantise_h(0, 1)
+        subtract(1, 1)
+        quantise_h(1, 1)
+        finish(0)
 
         promised = []
         for pair in range(2):
@@ -267,16 +324,17 @@ def tile_list_foundry_job_dispatch_kernel(
             )
             promised.append(both)
 
-        for q in range(NQ):
-            if q + 1 < NQ:
-                if q > 0:
-                    mould_and_max(0, q + 1)
-                subtract(0, q + 1)
-                mould_and_max(1, q + 1)
-                quantise_h(0, q + 1)
-                subtract(1, q + 1)
-                quantise_h(1, q + 1)
-            finish(q)
+        subtract(0, 2)
+        quantise_h(0, 2)
+        subtract(1, 2)
+        quantise_h(1, 2)
+        finish(1)
+        subtract(0, 3)
+        quantise_h(0, 3)
+        subtract(1, 3)
+        quantise_h(1, 3)
+        finish(2)
+        finish(3)
 
         for n in range(N // P):
             result = promised[n // 2][:, n % 2, :]

@@ -23,7 +23,7 @@ KP = P * PACK
 HALF = 512
 QW = 256
 NQ = S // QW
-ON_VECTOR = (0, 1)
+ON_VECTOR = ((0, 0), (1, 0), (0, 1), (1, 1))
 MELTB = (0, 1, 5)
 MOULDB = (2, 3, 4)
 TURNB = (5, 0, 1)
@@ -101,25 +101,26 @@ def tile_list_foundry_job_dispatch_kernel(
                 w1_raw[a, b] = raw
         rel_sb = {}
 
-        def load_rel(q):
-            for b in range(2):
-                rel_sb[b, q] = held([P, PACK, QW], F32, f"rel{b}{q}")
-                nc.sync.dma_start(
-                    out=rel_sb[b, q][:],
-                    in_=rel[b * KP : (b + 1) * KP, q * QW : (q + 1) * QW].rearrange("(p t) j -> p t j", t=PACK),
-                )
+        def load_rel(b, h):
+            both = held([P, PACK, HALF], F32, f"rel{b}{h}")
+            nc.sync.dma_start(
+                out=both[:],
+                in_=rel[b * KP : (b + 1) * KP, h * HALF : (h + 1) * HALF].rearrange("(p t) j -> p t j", t=PACK),
+            )
+            for i in range(HALF // QW):
+                rel_sb[b, h * (HALF // QW) + i] = both[:, :, i * QW : (i + 1) * QW]
 
-        load_rel(0)
+        load_rel(0, 0)
         for g in range(4):
             nc.sync.dma_start(
                 out=w8_s[32 * g : 32 * g + 8, :].bitcast(I32), in_=w8_scales[:, 4 * g : 4 * g + 4, :].bitcast(I32)
             )
-        load_rel(1)
+        load_rel(1, 0)
         nc.sync.dma_start(out=w8_w[:], in_=w8_words.rearrange("a p c i -> p a (c i)").bitcast(I32))
         nc.sync.dma_start(places[:], offs2)
         nc.sync.dma_start(out=gains[:], in_=wgo)
-        load_rel(2)
-        load_rel(3)
+        load_rel(0, 1)
+        load_rel(1, 1)
 
         nc.vector.tensor_copy(v_w[0][:], tab_w[0][:].bitcast(U32).indirect(picks[:]))
         nc.vector.tensor_copy(
@@ -168,14 +169,14 @@ def tile_list_foundry_job_dispatch_kernel(
         w1_w = {}
         w1_s = {}
 
-        def cast_w1(a, b, on_vector):
+        def cast_w1(a, b, share):
             w1_bf[a, b] = ring.tile([P, PACK, P, PACK], BF16, name="w1_bf", bufs=3, align_bytes=64)
             dst = w1_bf[a, b][:].rearrange("p t m j -> p m j t")
             src = w1_raw[a, b][:].rearrange("p j (m t) -> p m j t", t=PACK)
-            if on_vector:
-                nc.vector.tensor_copy(out=dst, in_=src)
-            else:
-                nc.scalar.copy(out=dst, in_=src)
+            if share > 0:
+                nc.vector.tensor_scalar(dst[:, :share], src[:, :share], -1.0, None, ALU.mult)
+            if share < P:
+                nc.scalar.activation(out=dst[:, share:], in_=src[:, share:], func=COPY, scale=-1.0)
 
         def quantise_w1(a, b):
             w1_w[a, b] = held([P, KP], U32, f"w1_w{a}{b}")
@@ -207,19 +208,16 @@ def tile_list_foundry_job_dispatch_kernel(
                             stop=(a == 1),
                         )
                 dst = later[b, q][:, 2 * pair : 2 * pair + 2, :]
-                neg_melt = dst
-                if q in ON_VECTOR:
-                    nc.vector.scalar_tensor_tensor(dst, neg_melt, -1.0, acc, ALU.mult, ALU.max)
-                else:
-                    nc.vector.scalar_tensor_tensor(dst, acc, -1.0, neg_melt, ALU.mult, ALU.min)
+                nc.vector.tensor_tensor(dst, acc, dst, ALU.min)
 
         h_bf = {}
+        last_rows = {}
         h_w = {}
         h_s = {}
 
         def subtract(b, q):
             h_bf[b, q] = ring.tile([P, QW, PACK], BF16, name="h_bf", bufs=4, align_bytes=64)
-            if q not in ON_VECTOR:
+            if (b, q) not in ON_VECTOR:
                 turned = []
                 for jb in range(QW // P):
                     acc = next_bank(TURNB)[:].rearrange("j (t p) -> j t p", t=PACK)
@@ -231,11 +229,10 @@ def tile_list_foundry_job_dispatch_kernel(
                         nc.tensor.matmul(
                             acc[:, t, :], rel_sb[b, q][:, t, jcols], ident[:], start=False, stop=True, is_transpose=True
                         )
-                    rows = ring.tile([P, 2, P, 2], BF16, name="h_rows", bufs=3, align_bytes=64)
-                    nc.scalar.activation(
-                        out=rows[:], in_=acc.rearrange("j (u e) p -> j u p e", e=2), func=COPY, scale=-1.0
-                    )
+                    rows = ring.tile([P, 2, P, 2], BF16, name="h_rows", bufs=8, align_bytes=64)
+                    nc.scalar.copy(out=rows[:], in_=acc.rearrange("j (u e) p -> j u p e", e=2))
                     turned.append(rows)
+                    last_rows[b, q] = rows
                 back = (bank_z, bank_x)[b][:].rearrange("p (jb u j) -> p jb u j", u=2, j=P)
                 for jb in range(QW // P):
                     words = turned[jb][:].rearrange("j u p e -> j u (p e)").bitcast(F32)
@@ -249,8 +246,8 @@ def tile_list_foundry_job_dispatch_kernel(
             nc.vector.tensor_tensor(
                 h_bf[b, q][:].rearrange("p (c i) t -> p c t i", i=4),
                 later[b, q].rearrange("p t (c i) -> p c t i", i=4),
-                rel_sb[b, q][:].rearrange("p t (c i) -> p c t i", i=4),
-                ALU.subtract,
+                rel_sb[b, q].rearrange("p t (c i) -> p c t i", i=4),
+                ALU.add,
             )
 
         def quantise_h(b, q):
@@ -263,7 +260,7 @@ def tile_list_foundry_job_dispatch_kernel(
         def finish(q):
             cols = slice(q * QW, (q + 1) * QW)
             for pair in range(2):
-                acc = (next_bank(MOULDB) if (q, pair) < (1, 1) else bank_z if (q, pair) == (NQ - 1, 1) else bank_x)[:].rearrange("p (i j) -> p i j", i=2)
+                acc = (next_bank(MOULDB) if q < 2 else bank_x if (q, pair) == (3, 0) else bank_z)[:].rearrange("p (i j) -> p i j", i=2)
                 for i in range(2):
                     n = 2 * pair + i
                     for b in (1, 0):
@@ -276,34 +273,40 @@ def tile_list_foundry_job_dispatch_kernel(
                             start=(b == 1),
                             stop=(b == 0),
                         )
-                y = ring.tile([P, 2, QW], F32, name="y", bufs=6, align_bytes=64)
-                nc.scalar.copy(out=y[:], in_=acc)
+                y = ring.tile([P, 2, QW], F32, name="y", bufs=5, align_bytes=64)
+                sources = [y[:, 0, :], y[:, 1, :]]
+                if pair == 1 and (1, q + 1) in last_rows:
+                    sources[1] = last_rows[1, q + 1][:].rearrange("j u p e -> j (u p e)").bitcast(F32)
+                    for i in range(2):
+                        nc.scalar.activation(out=sources[i], in_=acc[:, i, :], func=COPY, scale=-1.0)
+                else:
+                    nc.scalar.activation(out=y[:], in_=acc, func=COPY, scale=-1.0)
                 for i in range(2):
                     nc.vector.tensor_tensor(
                         page[2 * pair + i][:].indirect(places[:, q * QW // 16 : (q + 1) * QW // 16]),
-                        y[:, i, :],
+                        sources[i],
                         gains[:, cols],
                         ALU.mult,
                     )
 
         melt_block(0, 0)
-        cast_w1(0, 0, True)
+        cast_w1(0, 0, 128)
         quantise_w1(0, 0)
-        cast_w1(1, 0, True)
+        cast_w1(1, 0, 128)
         quantise_w1(1, 0)
+        cast_w1(0, 1, 128)
         mould_and_max(0, 0)
         mould_and_max(0, 1)
-        cast_w1(0, 1, False)
         melt_block(0, 1)
-        cast_w1(1, 1, False)
         melt_block(1, 0)
+        cast_w1(1, 1, 0)
         quantise_w1(0, 1)
         quantise_w1(1, 1)
         mould_and_max(0, 2)
         mould_and_max(0, 3)
-        melt_block(1, 1)
         mould_and_max(1, 0)
         mould_and_max(1, 1)
+        melt_block(1, 1)
         subtract(0, 0)
         subtract(1, 0)
         quantise_h(0, 0)
@@ -337,6 +340,8 @@ def tile_list_foundry_job_dispatch_kernel(
         finish(3)
 
         for n in range(N // P):
-            result = promised[n // 2][:, n % 2, :]
-            nc.vector.tensor_tensor(result, page[n][:], result, ALU.max)
-            nc.sync.dma_start(out=out[n * P : (n + 1) * P, :], in_=result)
+            width = S // 2 if n == N // P - 1 else S
+            for c in range(0, S, width):
+                result = promised[n // 2][:, n % 2, c : c + width]
+                nc.vector.tensor_tensor(result, page[n][:, c : c + width], result, ALU.max)
+                nc.sync.dma_start(out=out[n * P : (n + 1) * P, c : c + width], in_=result)

@@ -19,14 +19,19 @@ COPY = mybir.ActivationFunctionType.Copy
 
 P = 128
 PACK = 4
-KP = P * PACK
-HALF = 512
-QW = 256
-NQ = S // QW
-ON_VECTOR = ((0, 0), (1, 0), (0, 1), (1, 1))
-MELTB = (0, 1, 5)
-MOULDB = (2, 3, 4)
-TURNB = (5, 0, 1)
+PASS = P * PACK
+QUADRANTS = 4
+HALF = S // 2
+QUARTER = S // 4
+PER_COLUMN = 16
+SCALE_ROW = 24
+PLANE_ROWS = 100
+RUN = 2
+
+MELT_BANKS = (0, 1, 5)
+MOULD_BANKS = ((2, 3, 4), (6, 2, 3, 4))
+TURN_BANKS = (5, 0, 1)
+BACK_BANKS = (7, 6)
 
 
 def tile_list_foundry_job_dispatch_kernel(
@@ -36,13 +41,16 @@ def tile_list_foundry_job_dispatch_kernel(
     with ExitStack() as ctx:
         keep = ctx.enter_context(tc.tile_pool(name="keep", bufs=1))
         ring = ctx.enter_context(tc.tile_pool(name="ring", bufs=2))
-        psum = ctx.enter_context(tc.psum_pool(name="psum", bufs=2))
+        psum = ctx.enter_context(tc.psum_pool(name="psum", bufs=1))
 
         def held(shape, dtype, name):
             return keep.tile(shape, dtype, name=name, align_bytes=64)
 
-        picks = keep.tile([P, S // 16], U16, name="picks")
-        places = keep.tile([P, S // 16], U16, name="places")
+        def rotating(shape, dtype, name, bufs):
+            return ring.tile(shape, dtype, name=name, bufs=bufs, align_bytes=64)
+
+        picks = keep.tile([P, S // PER_COLUMN], U16, name="picks")
+        places = keep.tile([P, S // PER_COLUMN], U16, name="places")
         tab_w = [held([P, T], I32, f"tab_w{a}") for a in range(2)]
         tab_s = held([P, T], U8, "tab_s")
         v_w = [held([P, S], U32, f"v_w{a}") for a in range(2)]
@@ -56,62 +64,63 @@ def tile_list_foundry_job_dispatch_kernel(
         w8_s = held([P, N], U8, "w8_s")
         gains = held([P, S], F32, "gains")
         page = [held([P, S], F32, f"page{n}") for n in range(N // P)]
-
         ident = held([P, P], F32, "ident")
+
         nc.vector.memset(w4_sraw[:].bitcast(I32), 0)
-        for g in range(4):
-            nc.vector.memset(tab_s[32 * g : 32 * g + 24, :].bitcast(I32), 0)
+        for g in range(QUADRANTS):
+            nc.vector.memset(tab_s[32 * g : 32 * g + SCALE_ROW, :].bitcast(I32), 0)
         nc.vector.memset(v_s[:].bitcast(I32), 0)
         nc.vector.memset(w8_s[:].bitcast(I32), 0)
-
         make_identity(nc, ident[:])
+
         nc.sync.dma_start(picks[:], offs)
-        for g in range(4):
+        for g in range(QUADRANTS):
             nc.sync.dma_start(
-                out=tab_s[32 * g + 24 : 32 * g + 32, :].bitcast(I32),
+                out=tab_s[32 * g + SCALE_ROW : 32 * (g + 1), :].bitcast(I32),
                 in_=tab_scales[:, 4 * g : 4 * g + 4, :].bitcast(I32),
             )
 
-        def load_table(a, pieces):
+        def load_table(a):
             words = tab_words[a].rearrange("p t i -> p (t i)").bitcast(I32)
-            for c in range(0, T, T // pieces):
-                nc.sync.dma_start(out=tab_w[a][:, c : c + T // pieces], in_=words[:, c : c + T // pieces])
+            for c in range(0, T, T // 2):
+                nc.sync.dma_start(out=tab_w[a][:, c : c + T // 2], in_=words[:, c : c + T // 2])
 
-        load_table(0, 2)
+        load_table(0)
         nc.sync.dma_start(out=w4_raw[:].bitcast(I32), in_=w4_words.rearrange("a p c -> p a c").bitcast(I32))
-        for g in range(4):
+        for g in range(QUADRANTS):
             nc.sync.dma_start(
                 out=w4_sraw[32 * g : 32 * g + 4, :, :].bitcast(I32),
                 in_=w4_scales[:, 4 * g : 4 * g + 4, :].rearrange("a r c -> r a c").bitcast(I32),
             )
         nc.vector.tensor_copy(picked_s[:], tab_s[:].indirect(picks[:]))
         for a in range(2):
-            first = 24 + 4 * a
+            first = SCALE_ROW + 4 * a
             nc.scalar.dma_start(
-                out=v_s[0:100, a, :].bitcast(I32), in_=picked_s[first : first + 100, :].bitcast(I32)
+                out=v_s[0:PLANE_ROWS, a, :].bitcast(I32), in_=picked_s[first : first + PLANE_ROWS, :].bitcast(I32)
             )
-        load_table(1, 2)
+        load_table(1)
+
         w1_raw = {}
         for b in range(2):
             for a in range(2):
-                raw = ring.tile([P, PACK, KP], F32, name="raw", bufs=4, align_bytes=64)
-                rows = w1[a * KP : (a + 1) * KP, b * KP : (b + 1) * KP].rearrange("(p j) c -> p j c", j=PACK)
+                w1_raw[a, b] = rotating([P, PACK, PASS], F32, "raw", 4)
+                rows = w1[a * PASS : (a + 1) * PASS, b * PASS : (b + 1) * PASS].rearrange("(p j) c -> p j c", j=PACK)
                 for j in range(0, PACK, 2):
-                    nc.sync.dma_start(out=raw[:, j : j + 2, :], in_=rows[:, j : j + 2, :])
-                w1_raw[a, b] = raw
+                    nc.sync.dma_start(out=w1_raw[a, b][:, j : j + 2, :], in_=rows[:, j : j + 2, :])
+
         rel_sb = {}
 
         def load_rel(b, h):
             both = held([P, PACK, HALF], F32, f"rel{b}{h}")
             nc.sync.dma_start(
                 out=both[:],
-                in_=rel[b * KP : (b + 1) * KP, h * HALF : (h + 1) * HALF].rearrange("(p t) j -> p t j", t=PACK),
+                in_=rel[b * PASS : (b + 1) * PASS, h * HALF : (h + 1) * HALF].rearrange("(p t) j -> p t j", t=PACK),
             )
-            for i in range(HALF // QW):
-                rel_sb[b, h * (HALF // QW) + i] = both[:, :, i * QW : (i + 1) * QW]
+            for i in range(2):
+                rel_sb[b, 2 * h + i] = both[:, :, i * QUARTER : (i + 1) * QUARTER]
 
         load_rel(0, 0)
-        for g in range(4):
+        for g in range(QUADRANTS):
             nc.sync.dma_start(
                 out=w8_s[32 * g : 32 * g + 8, :].bitcast(I32), in_=w8_scales[:, 4 * g : 4 * g + 4, :].bitcast(I32)
             )
@@ -134,25 +143,24 @@ def tile_list_foundry_job_dispatch_kernel(
         for h in range(2):
             nc.vector.tensor_copy(
                 v_w[1][:, h * HALF : (h + 1) * HALF],
-                tab_w[1][:].bitcast(U32).indirect(picks[:, h * HALF // 16 : (h + 1) * HALF // 16]),
+                tab_w[1][:].bitcast(U32).indirect(picks[:, h * HALF // PER_COLUMN : (h + 1) * HALF // PER_COLUMN]),
             )
 
-        banks = [psum.tile([P, HALF], F32, name=f"bank{i}", bufs=1) for i in range(8)]
-        bank_x, bank_z = banks[6], banks[7]
+        banks = [psum.tile([P, HALF], F32, name=f"bank{i}") for i in range(8)]
         taken = []
 
         def next_bank(choices):
             taken.append(choices)
             return banks[choices[(len([c for c in taken if c == choices]) - 1) % len(choices)]]
 
-        melt = {}
+        later = {}
 
-        def melt_block(b, h):
-            melt[b, h] = held([P, HALF // QW, PACK, QW], F32, f"melt{b}{h}")
+        def melt_half(b, h):
+            neg_melt = held([P, 2, PACK, QUARTER], F32, f"melt{b}{h}")
             cols = slice(h * HALF, (h + 1) * HALF)
             for t in range(PACK):
-                acc = next_bank(MELTB)
-                c0 = b * KP + t * P
+                acc = next_bank(MELT_BANKS)
+                c0 = b * PASS + t * P
                 for a in range(2):
                     nc.tensor.matmul_mx(
                         out=acc[:],
@@ -163,38 +171,44 @@ def tile_list_foundry_job_dispatch_kernel(
                         start=(a == 0),
                         stop=(a == 1),
                     )
-                nc.scalar.activation(out=melt[b, h][:, :, t, :], in_=acc[:].rearrange("p (q j) -> p q j", j=QW), func=COPY, scale=-1.0)
+                nc.scalar.activation(
+                    out=neg_melt[:, :, t, :], in_=acc[:].rearrange("p (i j) -> p i j", i=2), func=COPY, scale=-1.0
+                )
+            for i in range(2):
+                later[b, 2 * h + i] = neg_melt[:, i]
 
         w1_bf = {}
         w1_w = {}
         w1_s = {}
 
-        def cast_w1(a, b, share):
-            w1_bf[a, b] = ring.tile([P, PACK, P, PACK], BF16, name="w1_bf", bufs=3, align_bytes=64)
-            dst = w1_bf[a, b][:].rearrange("p t m j -> p m j t")
-            src = w1_raw[a, b][:].rearrange("p j (m t) -> p m j t", t=PACK)
-            if share > 0:
-                nc.vector.tensor_scalar(dst[:, :share], src[:, :share], -1.0, None, ALU.mult)
-            if share < P:
-                nc.scalar.activation(out=dst[:, share:], in_=src[:, share:], func=COPY, scale=-1.0)
+        def w1_views(a, b):
+            w1_bf[a, b] = rotating([P, PACK, P, PACK], BF16, "w1_bf", 3)
+            return (
+                w1_bf[a, b][:].rearrange("p t m j -> p m j t"),
+                w1_raw[a, b][:].rearrange("p j (m t) -> p m j t", t=PACK),
+            )
+
+        def round_w1_on_vector(a, b):
+            dst, src = w1_views(a, b)
+            nc.vector.tensor_scalar(dst, src, -1.0, None, ALU.mult)
+
+        def round_w1_on_scalar(a, b):
+            dst, src = w1_views(a, b)
+            nc.scalar.activation(out=dst, in_=src, func=COPY, scale=-1.0)
 
         def quantise_w1(a, b):
-            w1_w[a, b] = held([P, KP], U32, f"w1_w{a}{b}")
-            w1_s[a, b] = held([P, KP], U8, f"w1_s{a}{b}")
+            w1_w[a, b] = held([P, PASS], U32, f"w1_w{a}{b}")
+            w1_s[a, b] = held([P, PASS], U8, f"w1_s{a}{b}")
             nc.vector.quantize_mx(
                 out=w1_w[a, b][:].bitcast(FP8X4),
                 scales=w1_s[a, b][:],
                 in_=w1_bf[a, b][:].rearrange("p t m j -> p (t m j)"),
             )
 
-        later = {}
-
-        def mould_and_max(b, q):
-            cols = slice(q * QW, (q + 1) * QW)
-            h, within = divmod(q, HALF // QW)
-            later[b, q] = melt[b, h][:, within]
+        def mould_and_min(b, q):
+            cols = slice(q * QUARTER, (q + 1) * QUARTER)
             for pair in range(2):
-                acc = next_bank(MOULDB)[:].rearrange("p (i j) -> p i j", i=2)
+                acc = next_bank(MOULD_BANKS[b])[:].rearrange("p (i j) -> p i j", i=2)
                 for i in range(2):
                     t = 2 * pair + i
                     for a in range(2):
@@ -211,56 +225,57 @@ def tile_list_foundry_job_dispatch_kernel(
                 nc.vector.tensor_tensor(dst, acc, dst, ALU.min)
 
         h_bf = {}
-        last_rows = {}
         h_w = {}
         h_s = {}
+        last_rows = {}
 
-        def subtract(b, q):
-            h_bf[b, q] = ring.tile([P, QW, PACK], BF16, name="h_bf", bufs=4, align_bytes=64)
-            if (b, q) not in ON_VECTOR:
-                turned = []
-                for jb in range(QW // P):
-                    acc = next_bank(TURNB)[:].rearrange("j (t p) -> j t p", t=PACK)
-                    jcols = slice(jb * P, (jb + 1) * P)
-                    for t in range(PACK):
-                        nc.tensor.matmul(
-                            acc[:, t, :], later[b, q][:, t, jcols], ident[:], start=True, stop=False, is_transpose=True
-                        )
-                        nc.tensor.matmul(
-                            acc[:, t, :], rel_sb[b, q][:, t, jcols], ident[:], start=False, stop=True, is_transpose=True
-                        )
-                    rows = ring.tile([P, 2, P, 2], BF16, name="h_rows", bufs=8, align_bytes=64)
-                    nc.scalar.copy(out=rows[:], in_=acc.rearrange("j (u e) p -> j u p e", e=2))
-                    turned.append(rows)
-                    last_rows[b, q] = rows
-                back = (bank_z, bank_x)[b][:].rearrange("p (jb u j) -> p jb u j", u=2, j=P)
-                for jb in range(QW // P):
-                    words = turned[jb][:].rearrange("j u p e -> j u (p e)").bitcast(F32)
-                    for u in range(2):
-                        nc.tensor.transpose(back[:, jb, u, :], words[:, u, :], ident[:])
-                nc.scalar.copy(
-                    out=h_bf[b, q][:].bitcast(F32).rearrange("p (jb j) u -> p jb j u", j=P),
-                    in_=back.rearrange("p jb u j -> p jb j u"),
-                )
-                return
+        def add_rel_on_vector(b, q):
+            h_bf[b, q] = rotating([P, QUARTER, PACK], BF16, "h_bf", 4)
             nc.vector.tensor_tensor(
-                h_bf[b, q][:].rearrange("p (c i) t -> p c t i", i=4),
-                later[b, q].rearrange("p t (c i) -> p c t i", i=4),
-                rel_sb[b, q].rearrange("p t (c i) -> p c t i", i=4),
+                h_bf[b, q][:].rearrange("p (c i) t -> p c t i", i=RUN),
+                later[b, q].rearrange("p t (c i) -> p c t i", i=RUN),
+                rel_sb[b, q].rearrange("p t (c i) -> p c t i", i=RUN),
                 ALU.add,
             )
 
+        def add_rel_on_tensor(b, q):
+            h_bf[b, q] = rotating([P, QUARTER, PACK], BF16, "h_bf", 4)
+            turned = []
+            for jb in range(QUARTER // P):
+                acc = next_bank(TURN_BANKS)[:].rearrange("j (t p) -> j t p", t=PACK)
+                jcols = slice(jb * P, (jb + 1) * P)
+                for t in range(PACK):
+                    nc.tensor.matmul(
+                        acc[:, t, :], later[b, q][:, t, jcols], ident[:], start=True, stop=False, is_transpose=True
+                    )
+                    nc.tensor.matmul(
+                        acc[:, t, :], rel_sb[b, q][:, t, jcols], ident[:], start=False, stop=True, is_transpose=True
+                    )
+                rows = rotating([P, 2, P, 2], BF16, "h_rows", 8)
+                nc.scalar.copy(out=rows[:], in_=acc.rearrange("j (u e) p -> j u p e", e=2))
+                turned.append(rows)
+            last_rows[b, q] = turned[-1]
+            back = banks[BACK_BANKS[b]][:].rearrange("p (jb u j) -> p jb u j", u=2, j=P)
+            for jb in range(QUARTER // P):
+                words = turned[jb][:].rearrange("j u p e -> j u (p e)").bitcast(F32)
+                for u in range(2):
+                    nc.tensor.transpose(back[:, jb, u, :], words[:, u, :], ident[:])
+            nc.scalar.copy(
+                out=h_bf[b, q][:].bitcast(F32).rearrange("p (jb j) u -> p jb j u", j=P),
+                in_=back.rearrange("p jb u j -> p jb j u"),
+            )
+
         def quantise_h(b, q):
-            h_w[b, q] = ring.tile([P, QW], U32, name="h_w", bufs=6, align_bytes=64)
-            h_s[b, q] = ring.tile([P, QW], U8, name="h_s", bufs=6, align_bytes=64)
+            h_w[b, q] = rotating([P, QUARTER], U32, "h_w", 6)
+            h_s[b, q] = rotating([P, QUARTER], U8, "h_s", 6)
             nc.vector.quantize_mx(
                 out=h_w[b, q][:].bitcast(FP8X4), scales=h_s[b, q][:], in_=h_bf[b, q][:].rearrange("p j t -> p (j t)")
             )
 
-        def finish(q):
-            cols = slice(q * QW, (q + 1) * QW)
+        def finish(q, pair_banks):
+            cols = slice(q * QUARTER, (q + 1) * QUARTER)
             for pair in range(2):
-                acc = (next_bank(MOULDB) if q < 2 else bank_x if (q, pair) == (3, 0) else bank_z)[:].rearrange("p (i j) -> p i j", i=2)
+                acc = pair_banks[pair][:].rearrange("p (i j) -> p i j", i=2)
                 for i in range(2):
                     n = 2 * pair + i
                     for b in (1, 0):
@@ -273,7 +288,7 @@ def tile_list_foundry_job_dispatch_kernel(
                             start=(b == 1),
                             stop=(b == 0),
                         )
-                y = ring.tile([P, 2, QW], F32, name="y", bufs=5, align_bytes=64)
+                y = rotating([P, 2, QUARTER], F32, "y", 5)
                 sources = [y[:, 0, :], y[:, 1, :]]
                 if pair == 1 and (1, q + 1) in last_rows:
                     sources[1] = last_rows[1, q + 1][:].rearrange("j u p e -> j (u p e)").bitcast(F32)
@@ -283,61 +298,63 @@ def tile_list_foundry_job_dispatch_kernel(
                     nc.scalar.activation(out=y[:], in_=acc, func=COPY, scale=-1.0)
                 for i in range(2):
                     nc.vector.tensor_tensor(
-                        page[2 * pair + i][:].indirect(places[:, q * QW // 16 : (q + 1) * QW // 16]),
+                        page[2 * pair + i][:].indirect(
+                            places[:, q * QUARTER // PER_COLUMN : (q + 1) * QUARTER // PER_COLUMN]
+                        ),
                         sources[i],
                         gains[:, cols],
                         ALU.mult,
                     )
 
-        melt_block(0, 0)
-        cast_w1(0, 0, 128)
-        quantise_w1(0, 0)
-        cast_w1(1, 0, 128)
-        quantise_w1(1, 0)
-        cast_w1(0, 1, 128)
-        mould_and_max(0, 0)
-        mould_and_max(0, 1)
-        melt_block(0, 1)
-        melt_block(1, 0)
-        cast_w1(1, 1, 0)
-        quantise_w1(0, 1)
-        quantise_w1(1, 1)
-        mould_and_max(0, 2)
-        mould_and_max(0, 3)
-        mould_and_max(1, 0)
-        mould_and_max(1, 1)
-        melt_block(1, 1)
-        subtract(0, 0)
-        subtract(1, 0)
-        quantise_h(0, 0)
-        quantise_h(1, 0)
-        mould_and_max(1, 2)
-        mould_and_max(1, 3)
-        subtract(0, 1)
-        quantise_h(0, 1)
-        subtract(1, 1)
-        quantise_h(1, 1)
-        finish(0)
+        def after_moulds():
+            return [next_bank(MOULD_BANKS[0]) for pair in range(2)]
+
+        melt_half(0, 0)
+        for a in range(2):
+            round_w1_on_vector(a, 0)
+            quantise_w1(a, 0)
+        round_w1_on_vector(0, 1)
+        for q in (0, 1):
+            mould_and_min(0, q)
+        melt_half(0, 1)
+        melt_half(1, 0)
+        round_w1_on_scalar(1, 1)
+        for a in range(2):
+            quantise_w1(a, 1)
+        for q in (2, 3):
+            mould_and_min(0, q)
+        for q in (0, 1):
+            mould_and_min(1, q)
+        melt_half(1, 1)
+
+        for b in range(2):
+            add_rel_on_vector(b, 0)
+        for b in range(2):
+            quantise_h(b, 0)
+        for q in (2, 3):
+            mould_and_min(1, q)
+        for b in range(2):
+            add_rel_on_vector(b, 1)
+            quantise_h(b, 1)
+        finish(0, after_moulds())
 
         promised = []
         for pair in range(2):
-            both = ring.tile([P, 2, S], F32, name="raw", bufs=4, align_bytes=64)
+            both = rotating([P, 2, S], F32, "raw", 4)
             nc.sync.dma_start(
                 out=both[:], in_=x0[2 * pair * P : 2 * (pair + 1) * P, :].rearrange("(i p) m -> p i m", p=P)
             )
             promised.append(both)
 
-        subtract(0, 2)
-        quantise_h(0, 2)
-        subtract(1, 2)
-        quantise_h(1, 2)
-        finish(1)
-        subtract(0, 3)
-        quantise_h(0, 3)
-        subtract(1, 3)
-        quantise_h(1, 3)
-        finish(2)
-        finish(3)
+        for b in range(2):
+            add_rel_on_tensor(b, 2)
+            quantise_h(b, 2)
+        finish(1, after_moulds())
+        for b in range(2):
+            add_rel_on_tensor(b, 3)
+            quantise_h(b, 3)
+        finish(2, [banks[BACK_BANKS[0]], banks[BACK_BANKS[0]]])
+        finish(3, [banks[BACK_BANKS[1]], banks[BACK_BANKS[0]]])
 
         for n in range(N // P):
             width = S // 2 if n == N // P - 1 else S

@@ -24,8 +24,6 @@ QUADRANTS = 4
 HALF = S // 2
 QUARTER = S // 4
 PER_COLUMN = 16
-SCALE_ROW = 24
-PLANE_ROWS = 100
 RUN = 2
 
 MELT_BANKS = (0, 1, 5)
@@ -67,38 +65,35 @@ def tile_list_foundry_job_dispatch_kernel(
         ident = held([P, P], F32, "ident")
 
         nc.vector.memset(w4_sraw[:].bitcast(I32), 0)
-        for g in range(QUADRANTS):
-            nc.vector.memset(tab_s[32 * g : 32 * g + SCALE_ROW, :].bitcast(I32), 0)
+        nc.vector.memset(tab_s[32:64, :].bitcast(I32), 0)
+        nc.vector.memset(tab_s[64:128, :].bitcast(I32), 0)
         nc.vector.memset(v_s[:].bitcast(I32), 0)
         nc.vector.memset(w8_s[:].bitcast(I32), 0)
         make_identity(nc, ident[:])
 
         nc.sync.dma_start(picks[:], offs)
-        for g in range(QUADRANTS):
-            nc.sync.dma_start(
-                out=tab_s[32 * g + SCALE_ROW : 32 * (g + 1), :].bitcast(I32),
-                in_=tab_scales[:, 4 * g : 4 * g + 4, :].bitcast(I32),
-            )
+        nc.sync.dma_start(out=tab_s[0:32, :].bitcast(I32), in_=tab_scales.rearrange("a q t -> (a q) t").bitcast(I32))
 
-        def load_table(a):
+        def load_table(a, pieces):
             words = tab_words[a].rearrange("p t i -> p (t i)").bitcast(I32)
-            for c in range(0, T, T // 2):
-                nc.sync.dma_start(out=tab_w[a][:, c : c + T // 2], in_=words[:, c : c + T // 2])
+            for c in range(0, T, T // pieces):
+                nc.sync.dma_start(out=tab_w[a][:, c : c + T // pieces], in_=words[:, c : c + T // pieces])
 
-        load_table(0)
+        load_table(0, 4)
         nc.sync.dma_start(out=w4_raw[:].bitcast(I32), in_=w4_words.rearrange("a p c -> p a c").bitcast(I32))
         for g in range(QUADRANTS):
-            nc.sync.dma_start(
+            nc.scalar.dma_start(
                 out=w4_sraw[32 * g : 32 * g + 4, :, :].bitcast(I32),
                 in_=w4_scales[:, 4 * g : 4 * g + 4, :].rearrange("a r c -> r a c").bitcast(I32),
             )
+        load_table(1, 2)
         nc.vector.tensor_copy(picked_s[:], tab_s[:].indirect(picks[:]))
         for a in range(2):
-            first = SCALE_ROW + 4 * a
-            nc.scalar.dma_start(
-                out=v_s[0:PLANE_ROWS, a, :].bitcast(I32), in_=picked_s[first : first + PLANE_ROWS, :].bitcast(I32)
-            )
-        load_table(1)
+            for g in range(QUADRANTS):
+                first = 16 * a + 4 * g
+                nc.scalar.dma_start(
+                    out=v_s[32 * g : 32 * g + 4, a, :].bitcast(I32), in_=picked_s[first : first + 4, :].bitcast(I32)
+                )
 
         w1_raw = {}
         for b in range(2):

@@ -24,12 +24,8 @@ QUADRANTS = 4
 HALF = S // 2
 QUARTER = S // 4
 PER_COLUMN = 16
+SCALE_ROW = P - 16
 RUN = 2
-
-MELT_BANKS = (0, 1, 5)
-MOULD_BANKS = ((2, 3, 4), (6, 2, 3, 4))
-TURN_BANKS = (5, 0, 1)
-BACK_BANKS = (7, 6)
 
 
 def tile_list_foundry_job_dispatch_kernel(
@@ -50,9 +46,9 @@ def tile_list_foundry_job_dispatch_kernel(
         picks = keep.tile([P, S // PER_COLUMN], U16, name="picks")
         places = keep.tile([P, S // PER_COLUMN], U16, name="places")
         tab_w = [held([P, T], I32, f"tab_w{a}") for a in range(2)]
-        tab_s = held([P, T], U8, "tab_s")
+        tab_s = held([P, 2, T], U8, "tab_s")
         v_w = [held([P, S], U32, f"v_w{a}") for a in range(2)]
-        picked_s = held([P, S], U8, "picked_s")
+        picked_s = held([P, 2, S], U8, "picked_s")
         v_s = held([P, 2, S], U8, "v_s")
         w4_raw = held([P, 2, 2 * H], U8, "w4_raw")
         w4_w = held([P, 2, 2 * H], U8, "w4_w")
@@ -64,44 +60,45 @@ def tile_list_foundry_job_dispatch_kernel(
         page = [held([P, S], F32, f"page{n}") for n in range(N // P)]
         ident = held([P, P], F32, "ident")
 
-        nc.vector.memset(w4_sraw[:].bitcast(I32), 0)
-        nc.vector.memset(tab_s[32:64, :].bitcast(I32), 0)
-        nc.vector.memset(tab_s[64:128, :].bitcast(I32), 0)
-        nc.vector.memset(v_s[:].bitcast(I32), 0)
-        nc.vector.memset(w8_s[:].bitcast(I32), 0)
+        nc.gpsimd.memset(w4_sraw[:].bitcast(I32), 0)
+        nc.vector.memset(tab_s[:SCALE_ROW, 0, :].bitcast(I32), 0)
+        nc.vector.memset(tab_s[:SCALE_ROW, 1, :].bitcast(I32), 0)
+        nc.gpsimd.memset(v_s[:].bitcast(I32), 0)
+        nc.gpsimd.memset(w8_s[:].bitcast(I32), 0)
         make_identity(nc, ident[:])
 
         nc.sync.dma_start(picks[:], offs)
-        nc.sync.dma_start(out=tab_s[0:32, :].bitcast(I32), in_=tab_scales.rearrange("a q t -> (a q) t").bitcast(I32))
+        nc.sync.dma_start(
+            out=tab_s[SCALE_ROW:, :, :].bitcast(I32), in_=tab_scales.rearrange("a q t -> q a t").bitcast(I32)
+        )
 
         def load_table(a, pieces):
             words = tab_words[a].rearrange("p t i -> p (t i)").bitcast(I32)
-            for c in range(0, T, T // pieces):
-                nc.sync.dma_start(out=tab_w[a][:, c : c + T // pieces], in_=words[:, c : c + T // pieces])
+            for c0, c1 in zip(pieces, pieces[1:]):
+                nc.sync.dma_start(out=tab_w[a][:, c0:c1], in_=words[:, c0:c1])
 
-        load_table(0, 4)
         nc.sync.dma_start(out=w4_raw[:].bitcast(I32), in_=w4_words.rearrange("a p c -> p a c").bitcast(I32))
         for g in range(QUADRANTS):
-            nc.scalar.dma_start(
+            nc.sync.dma_start(
                 out=w4_sraw[32 * g : 32 * g + 4, :, :].bitcast(I32),
                 in_=w4_scales[:, 4 * g : 4 * g + 4, :].rearrange("a r c -> r a c").bitcast(I32),
             )
-        load_table(1, 2)
-        nc.vector.tensor_copy(picked_s[:], tab_s[:].indirect(picks[:]))
+        load_table(0, (0, T))
+        load_table(1, (0, 1536, 2816, T))
         for a in range(2):
-            for g in range(QUADRANTS):
-                first = 16 * a + 4 * g
-                nc.scalar.dma_start(
-                    out=v_s[32 * g : 32 * g + 4, a, :].bitcast(I32), in_=picked_s[first : first + 4, :].bitcast(I32)
-                )
+            nc.vector.tensor_copy(picked_s[:, a, :], tab_s[:, a, :].indirect(picks[:]))
+        for g in range(QUADRANTS):
+            first = SCALE_ROW + 4 * g
+            nc.scalar.dma_start(
+                out=v_s[32 * g : 32 * g + 4, :, :].bitcast(I32), in_=picked_s[first : first + 4, :, :].bitcast(I32)
+            )
 
         w1_raw = {}
         for b in range(2):
             for a in range(2):
                 w1_raw[a, b] = rotating([P, PACK, PASS], F32, "raw", 4)
                 rows = w1[a * PASS : (a + 1) * PASS, b * PASS : (b + 1) * PASS].rearrange("(p j) c -> p j c", j=PACK)
-                for j in range(0, PACK, 2):
-                    nc.sync.dma_start(out=w1_raw[a, b][:, j : j + 2, :], in_=rows[:, j : j + 2, :])
+                nc.sync.dma_start(out=w1_raw[a, b][:], in_=rows)
 
         rel_sb = {}
 
@@ -126,7 +123,6 @@ def tile_list_foundry_job_dispatch_kernel(
         load_rel(0, 1)
         load_rel(1, 1)
 
-        nc.vector.tensor_copy(v_w[0][:], tab_w[0][:].bitcast(U32).indirect(picks[:]))
         nc.vector.tensor_copy(
             w4_w[:].bitcast(U16).rearrange("p a (b t m) -> p (a b) t m", t=PACK, m=P),
             w4_raw[:].bitcast(U16).rearrange("p a (b m t) -> p (a b) t m", t=PACK, m=P),
@@ -135,6 +131,7 @@ def tile_list_foundry_job_dispatch_kernel(
             w4_s[:].rearrange("p a (b t m) -> p (a b) t m", t=PACK, m=P),
             w4_sraw[:].rearrange("p a (b m t) -> p (a b) t m", t=PACK, m=P),
         )
+        nc.vector.tensor_copy(v_w[0][:], tab_w[0][:].bitcast(U32).indirect(picks[:]))
         for h in range(2):
             nc.vector.tensor_copy(
                 v_w[1][:, h * HALF : (h + 1) * HALF],
@@ -142,32 +139,43 @@ def tile_list_foundry_job_dispatch_kernel(
             )
 
         banks = [psum.tile([P, HALF], F32, name=f"bank{i}") for i in range(8)]
-        taken = []
-
-        def next_bank(choices):
-            taken.append(choices)
-            return banks[choices[(len([c for c in taken if c == choices]) - 1) % len(choices)]]
 
         later = {}
 
-        def melt_half(b, h):
-            neg_melt = held([P, 2, PACK, QUARTER], F32, f"melt{b}{h}")
+        def melt_pass(b, h, t, a, acc):
             cols = slice(h * HALF, (h + 1) * HALF)
+            c0 = b * PASS + t * P
+            nc.tensor.matmul_mx(
+                out=acc[:],
+                lhsT=w4_w[:, a, 2 * c0 : 2 * (c0 + P)].bitcast(FP4X4),
+                lhsT_scale=w4_s[:, a, c0 : c0 + P],
+                rhs=v_w[a][:, cols].bitcast(FP8X4),
+                rhs_scale=v_s[:, a, cols],
+                start=(a == 0),
+                stop=(a == 1),
+            )
+
+        def melt_open(b, h, group):
             for t in range(PACK):
-                acc = next_bank(MELT_BANKS)
-                c0 = b * PASS + t * P
-                for a in range(2):
-                    nc.tensor.matmul_mx(
-                        out=acc[:],
-                        lhsT=w4_w[:, a, 2 * c0 : 2 * (c0 + P)].bitcast(FP4X4),
-                        lhsT_scale=w4_s[:, a, c0 : c0 + P],
-                        rhs=v_w[a][:, cols].bitcast(FP8X4),
-                        rhs_scale=v_s[:, a, cols],
-                        start=(a == 0),
-                        stop=(a == 1),
-                    )
+                melt_pass(b, h, t, 0, group[t])
+
+        def melt_close(b, h, group):
+            neg_melt = held([P, 2, PACK, QUARTER], F32, f"melt{b}{h}")
+            for t in range(PACK):
+                melt_pass(b, h, t, 1, group[t])
                 nc.scalar.activation(
-                    out=neg_melt[:, :, t, :], in_=acc[:].rearrange("p (i j) -> p i j", i=2), func=COPY, scale=-1.0
+                    out=neg_melt[:, :, t, :], in_=group[t][:].rearrange("p (i j) -> p i j", i=2), func=COPY, scale=-1.0
+                )
+            for i in range(2):
+                later[b, 2 * h + i] = neg_melt[:, i]
+
+        def melt_half(b, h, group):
+            neg_melt = held([P, 2, PACK, QUARTER], F32, f"melt{b}{h}")
+            for t in range(PACK):
+                for a in range(2):
+                    melt_pass(b, h, t, a, group[t])
+                nc.scalar.activation(
+                    out=neg_melt[:, :, t, :], in_=group[t][:].rearrange("p (i j) -> p i j", i=2), func=COPY, scale=-1.0
                 )
             for i in range(2):
                 later[b, 2 * h + i] = neg_melt[:, i]
@@ -200,10 +208,10 @@ def tile_list_foundry_job_dispatch_kernel(
                 in_=w1_bf[a, b][:].rearrange("p t m j -> p (t m j)"),
             )
 
-        def mould_and_min(b, q):
+        def mould_and_min(b, q, group):
             cols = slice(q * QUARTER, (q + 1) * QUARTER)
             for pair in range(2):
-                acc = next_bank(MOULD_BANKS[b])[:].rearrange("p (i j) -> p i j", i=2)
+                acc = group[pair][:].rearrange("p (i j) -> p i j", i=2)
                 for i in range(2):
                     t = 2 * pair + i
                     for a in range(2):
@@ -222,7 +230,6 @@ def tile_list_foundry_job_dispatch_kernel(
         h_bf = {}
         h_w = {}
         h_s = {}
-        last_rows = {}
 
         def add_rel_on_vector(b, q):
             h_bf[b, q] = rotating([P, QUARTER, PACK], BF16, "h_bf", 4)
@@ -233,11 +240,11 @@ def tile_list_foundry_job_dispatch_kernel(
                 ALU.add,
             )
 
-        def add_rel_on_tensor(b, q):
+        def add_rel_on_tensor(b, q, group, back_bank):
             h_bf[b, q] = rotating([P, QUARTER, PACK], BF16, "h_bf", 4)
             turned = []
             for jb in range(QUARTER // P):
-                acc = next_bank(TURN_BANKS)[:].rearrange("j (t p) -> j t p", t=PACK)
+                acc = group[jb][:].rearrange("j (t p) -> j t p", t=PACK)
                 jcols = slice(jb * P, (jb + 1) * P)
                 for t in range(PACK):
                     nc.tensor.matmul(
@@ -246,11 +253,10 @@ def tile_list_foundry_job_dispatch_kernel(
                     nc.tensor.matmul(
                         acc[:, t, :], rel_sb[b, q][:, t, jcols], ident[:], start=False, stop=True, is_transpose=True
                     )
-                rows = rotating([P, 2, P, 2], BF16, "h_rows", 8)
+                rows = rotating([P, 2, P, 2], BF16, "h_rows", 6)
                 nc.scalar.copy(out=rows[:], in_=acc.rearrange("j (u e) p -> j u p e", e=2))
                 turned.append(rows)
-            last_rows[b, q] = turned[-1]
-            back = banks[BACK_BANKS[b]][:].rearrange("p (jb u j) -> p jb u j", u=2, j=P)
+            back = back_bank[:].rearrange("p (jb u j) -> p jb u j", u=2, j=P)
             for jb in range(QUARTER // P):
                 words = turned[jb][:].rearrange("j u p e -> j u (p e)").bitcast(F32)
                 for u in range(2):
@@ -267,71 +273,59 @@ def tile_list_foundry_job_dispatch_kernel(
                 out=h_w[b, q][:].bitcast(FP8X4), scales=h_s[b, q][:], in_=h_bf[b, q][:].rearrange("p j t -> p (j t)")
             )
 
-        def finish(q, pair_banks):
+        def finish(q, blocks, bank):
             cols = slice(q * QUARTER, (q + 1) * QUARTER)
-            for pair in range(2):
-                acc = pair_banks[pair][:].rearrange("p (i j) -> p i j", i=2)
-                for i in range(2):
-                    n = 2 * pair + i
-                    for b in (1, 0):
-                        nc.tensor.matmul_mx(
-                            out=acc[:, i, :],
-                            lhsT=w8_w[:, b, n * P : (n + 1) * P].bitcast(FP8X4),
-                            lhsT_scale=w8_s[4 * b :, n * P : (n + 1) * P],
-                            rhs=h_w[b, q][:].bitcast(FP8X4),
-                            rhs_scale=h_s[b, q][:],
-                            start=(b == 1),
-                            stop=(b == 0),
-                        )
-                y = rotating([P, 2, QUARTER], F32, "y", 5)
-                sources = [y[:, 0, :], y[:, 1, :]]
-                if pair == 1 and (1, q + 1) in last_rows:
-                    sources[1] = last_rows[1, q + 1][:].rearrange("j u p e -> j (u p e)").bitcast(F32)
-                    for i in range(2):
-                        nc.scalar.activation(out=sources[i], in_=acc[:, i, :], func=COPY, scale=-1.0)
-                else:
-                    nc.scalar.activation(out=y[:], in_=acc, func=COPY, scale=-1.0)
-                for i in range(2):
-                    nc.vector.tensor_tensor(
-                        page[2 * pair + i][:].indirect(
-                            places[:, q * QUARTER // PER_COLUMN : (q + 1) * QUARTER // PER_COLUMN]
-                        ),
-                        sources[i],
-                        gains[:, cols],
-                        ALU.mult,
+            acc = bank[:].rearrange("p (i j) -> p i j", i=2)[:, : len(blocks), :]
+            for i, n in enumerate(blocks):
+                for b in (1, 0):
+                    nc.tensor.matmul_mx(
+                        out=acc[:, i, :],
+                        lhsT=w8_w[:, b, n * P : (n + 1) * P].bitcast(FP8X4),
+                        lhsT_scale=w8_s[4 * b :, n * P : (n + 1) * P],
+                        rhs=h_w[b, q][:].bitcast(FP8X4),
+                        rhs_scale=h_s[b, q][:],
+                        start=(b == 1),
+                        stop=(b == 0),
                     )
+            y = rotating([P, 2, QUARTER], F32, "y", 4)
+            nc.scalar.activation(out=y[:, : len(blocks), :], in_=acc, func=COPY, scale=-1.0)
+            for i, n in enumerate(blocks):
+                nc.vector.tensor_tensor(
+                    page[n][:].indirect(
+                        places[:, q * QUARTER // PER_COLUMN : (q + 1) * QUARTER // PER_COLUMN]
+                    ),
+                    y[:, i, :],
+                    gains[:, cols],
+                    ALU.mult,
+                )
 
-        def after_moulds():
-            return [next_bank(MOULD_BANKS[0]) for pair in range(2)]
-
-        melt_half(0, 0)
+        low, high = banks[:4], banks[4:]
+        melt_open(0, 0, low)
+        melt_open(1, 0, high)
+        melt_close(0, 0, low)
+        melt_close(1, 0, high)
         for a in range(2):
             round_w1_on_vector(a, 0)
             quantise_w1(a, 0)
         round_w1_on_vector(0, 1)
-        for q in (0, 1):
-            mould_and_min(0, q)
-        melt_half(0, 1)
-        melt_half(1, 0)
+        quantise_w1(0, 1)
+        melt_half(0, 1, low)
+        mould_and_min(0, 0, high[:2])
+        mould_and_min(0, 1, high[2:])
         round_w1_on_scalar(1, 1)
-        for a in range(2):
-            quantise_w1(a, 1)
-        for q in (2, 3):
-            mould_and_min(0, q)
-        for q in (0, 1):
-            mould_and_min(1, q)
-        melt_half(1, 1)
-
-        for b in range(2):
-            add_rel_on_vector(b, 0)
-        for b in range(2):
-            quantise_h(b, 0)
-        for q in (2, 3):
-            mould_and_min(1, q)
-        for b in range(2):
-            add_rel_on_vector(b, 1)
-            quantise_h(b, 1)
-        finish(0, after_moulds())
+        quantise_w1(1, 1)
+        mould_and_min(0, 2, low[:2])
+        mould_and_min(0, 3, low[2:])
+        add_rel_on_vector(0, 0)
+        mould_and_min(1, 0, low[:2])
+        melt_half(1, 1, high)
+        add_rel_on_vector(1, 0)
+        quantise_h(0, 0)
+        mould_and_min(1, 1, low[2:])
+        quantise_h(1, 0)
+        mould_and_min(1, 2, high[:2])
+        mould_and_min(1, 3, high[2:])
+        finish(0, (0, 1), low[0])
 
         promised = []
         for pair in range(2):
@@ -341,19 +335,22 @@ def tile_list_foundry_job_dispatch_kernel(
             )
             promised.append(both)
 
-        for b in range(2):
-            add_rel_on_tensor(b, 2)
-            quantise_h(b, 2)
-        finish(1, after_moulds())
-        for b in range(2):
-            add_rel_on_tensor(b, 3)
-            quantise_h(b, 3)
-        finish(2, [banks[BACK_BANKS[0]], banks[BACK_BANKS[0]]])
-        finish(3, [banks[BACK_BANKS[1]], banks[BACK_BANKS[0]]])
+        for q in range(1, 4):
+            add_rel_on_tensor(0, q, low[1:3], banks[4])
+            add_rel_on_tensor(1, q, [banks[3], banks[5]], banks[6])
+            for b in range(2):
+                quantise_h(b, q)
+            if q == 1:
+                finish(0, (2,), banks[7])
+                finish(0, (3,), banks[6])
+            else:
+                finish(q - 1, (2, 3), banks[6])
+            finish(q, (0, 1), banks[0 if q % 2 else 7])
+        finish(3, (2, 3), banks[4])
 
         for n in range(N // P):
-            width = S // 2 if n == N // P - 1 else S
-            for c in range(0, S, width):
-                result = promised[n // 2][:, n % 2, c : c + width]
-                nc.vector.tensor_tensor(result, page[n][:, c : c + width], result, ALU.max)
-                nc.sync.dma_start(out=out[n * P : (n + 1) * P, c : c + width], in_=result)
+            cuts = (0, HALF, HALF + QUARTER, S) if n == N // P - 1 else (0, S)
+            for c0, c1 in zip(cuts, cuts[1:]):
+                result = promised[n // 2][:, n % 2, c0:c1]
+                nc.vector.tensor_tensor(result, page[n][:, c0:c1], result, ALU.max)
+                nc.sync.dma_start(out=out[n * P : (n + 1) * P, c0:c1], in_=result)

@@ -301,31 +301,37 @@ def tile_list_foundry_job_dispatch_kernel(
 
         low, high = banks[:4], banks[4:]
         melt_open(0, 0, low)
-        melt_open(1, 0, high)
+        melt_open(0, 1, high)
         melt_close(0, 0, low)
-        melt_close(1, 0, high)
+        melt_close(0, 1, high)
         for a in range(2):
             round_w1_on_vector(a, 0)
             quantise_w1(a, 0)
         round_w1_on_vector(0, 1)
         quantise_w1(0, 1)
-        melt_half(0, 1, low)
+        round_w1_on_scalar(1, 1)
+        melt_half(1, 0, low)
         mould_and_min(0, 0, high[:2])
         mould_and_min(0, 1, high[2:])
-        round_w1_on_scalar(1, 1)
         quantise_w1(1, 1)
-        mould_and_min(0, 2, low[:2])
-        mould_and_min(0, 3, low[2:])
+        mould_and_min(0, 2, high[:2])
+        mould_and_min(0, 3, high[2:])
         add_rel_on_vector(0, 0)
-        mould_and_min(1, 0, low[:2])
-        melt_half(1, 1, high)
+        mould_and_min(1, 0, high[:2])
+        melt_half(1, 1, low)
         add_rel_on_vector(1, 0)
         quantise_h(0, 0)
-        mould_and_min(1, 1, low[2:])
+        mould_and_min(1, 1, high[2:])
         quantise_h(1, 0)
         mould_and_min(1, 2, high[:2])
         mould_and_min(1, 3, high[2:])
-        finish(0, (0, 1), low[0])
+        for b in range(2):
+            add_rel_on_vector(b, 1)
+        for b in range(2):
+            quantise_h(b, 1)
+        finish(0, (0, 1), banks[5])
+        finish(0, (2, 3), banks[6])
+        finish(1, (0, 1), banks[7])
 
         promised = []
         for pair in range(2):
@@ -335,17 +341,13 @@ def tile_list_foundry_job_dispatch_kernel(
             )
             promised.append(both)
 
-        for q in range(1, 4):
-            add_rel_on_tensor(0, q, low[1:3], banks[4])
-            add_rel_on_tensor(1, q, [banks[3], banks[5]], banks[6])
+        for q in range(2, 4):
+            add_rel_on_tensor(0, q, low[:2], banks[4])
+            add_rel_on_tensor(1, q, low[2:], banks[6])
             for b in range(2):
                 quantise_h(b, q)
-            if q == 1:
-                finish(0, (2,), banks[7])
-                finish(0, (3,), banks[6])
-            else:
-                finish(q - 1, (2, 3), banks[6])
-            finish(q, (0, 1), banks[0 if q % 2 else 7])
+            finish(q - 1, (2, 3), banks[6])
+            finish(q, (0, 1), banks[7 if q % 2 else 5])
         finish(3, (2, 3), banks[4])
 
         for n in range(N // P):

@@ -60,11 +60,11 @@ def tile_list_foundry_job_dispatch_kernel(
         page = [held([P, S], F32, f"page{n}") for n in range(N // P)]
         ident = held([P, P], F32, "ident")
 
-        nc.gpsimd.memset(w4_sraw[:].bitcast(I32), 0)
+        nc.vector.memset(w4_sraw[:].bitcast(I32), 0)
         nc.vector.memset(tab_s[:SCALE_ROW, 0, :].bitcast(I32), 0)
         nc.vector.memset(tab_s[:SCALE_ROW, 1, :].bitcast(I32), 0)
-        nc.gpsimd.memset(v_s[:].bitcast(I32), 0)
-        nc.gpsimd.memset(w8_s[:].bitcast(I32), 0)
+        nc.vector.memset(v_s[:].bitcast(I32), 0)
+        nc.vector.memset(w8_s[:].bitcast(I32), 0)
         make_identity(nc, ident[:])
 
         nc.sync.dma_start(picks[:], offs)
@@ -112,15 +112,15 @@ def tile_list_foundry_job_dispatch_kernel(
                 rel_sb[b, 2 * h + i] = both[:, :, i * QUARTER : (i + 1) * QUARTER]
 
         load_rel(0, 0)
+        load_rel(1, 0)
+        load_rel(0, 1)
         for g in range(QUADRANTS):
             nc.sync.dma_start(
                 out=w8_s[32 * g : 32 * g + 8, :].bitcast(I32), in_=w8_scales[:, 4 * g : 4 * g + 4, :].bitcast(I32)
             )
-        load_rel(1, 0)
         nc.sync.dma_start(out=w8_w[:], in_=w8_words.rearrange("a p c i -> p a (c i)").bitcast(I32))
         nc.sync.dma_start(places[:], offs2)
         nc.sync.dma_start(out=gains[:], in_=wgo)
-        load_rel(0, 1)
         load_rel(1, 1)
 
         nc.vector.tensor_copy(
@@ -253,7 +253,7 @@ def tile_list_foundry_job_dispatch_kernel(
                     nc.tensor.matmul(
                         acc[:, t, :], rel_sb[b, q][:, t, jcols], ident[:], start=False, stop=True, is_transpose=True
                     )
-                rows = rotating([P, 2, P, 2], BF16, "h_rows", 6)
+                rows = rotating([P, 2, P, 2], BF16, "h_rows", 5)
                 nc.scalar.copy(out=rows[:], in_=acc.rearrange("j (u e) p -> j u p e", e=2))
                 turned.append(rows)
             back = back_bank[:].rearrange("p (jb u j) -> p jb u j", u=2, j=P)
@@ -267,8 +267,8 @@ def tile_list_foundry_job_dispatch_kernel(
             )
 
         def quantise_h(b, q):
-            h_w[b, q] = rotating([P, QUARTER], U32, "h_w", 6)
-            h_s[b, q] = rotating([P, QUARTER], U8, "h_s", 6)
+            h_w[b, q] = rotating([P, QUARTER], U32, "h_w", 8)
+            h_s[b, q] = rotating([P, QUARTER], U8, "h_s", 8)
             nc.vector.quantize_mx(
                 out=h_w[b, q][:].bitcast(FP8X4), scales=h_s[b, q][:], in_=h_bf[b, q][:].rearrange("p j t -> p (j t)")
             )
@@ -332,6 +332,11 @@ def tile_list_foundry_job_dispatch_kernel(
         finish(0, (0, 1), banks[5])
         finish(0, (2, 3), banks[6])
         finish(1, (0, 1), banks[7])
+        finish(1, (2,), banks[4])
+        add_rel_on_tensor(0, 2, low[:2], low[1])
+        add_rel_on_tensor(0, 3, low[2:], low[3])
+        for q in (2, 3):
+            quantise_h(0, q)
 
         promised = []
         for pair in range(2):
@@ -341,14 +346,16 @@ def tile_list_foundry_job_dispatch_kernel(
             )
             promised.append(both)
 
-        for q in range(2, 4):
-            add_rel_on_tensor(0, q, low[:2], banks[4])
-            add_rel_on_tensor(1, q, low[2:], banks[6])
-            for b in range(2):
-                quantise_h(b, q)
-            finish(q - 1, (2, 3), banks[6])
-            finish(q, (0, 1), banks[7 if q % 2 else 5])
-        finish(3, (2, 3), banks[4])
+        add_rel_on_tensor(1, 2, low[:2], banks[5])
+        quantise_h(1, 2)
+        finish(1, (3,), banks[5])
+        add_rel_on_tensor(1, 3, low[2:], banks[6])
+        finish(2, (0, 1), banks[7])
+        finish(2, (2,), banks[4])
+        quantise_h(1, 3)
+        finish(2, (3,), banks[6])
+        finish(3, (0, 1), banks[5])
+        finish(3, (2, 3), banks[7])
 
         for n in range(N // P):
             cuts = (0, HALF, HALF + QUARTER, S) if n == N // P - 1 else (0, S)

@@ -24,7 +24,7 @@ QUADRANTS = 4
 HALF = S // 2
 QUARTER = S // 4
 PER_COLUMN = 16
-SCALE_ROW = P - 16
+SCALE_ROW = P - 32
 RUN = 2
 
 
@@ -46,9 +46,9 @@ def tile_list_foundry_job_dispatch_kernel(
         picks = keep.tile([P, S // PER_COLUMN], U16, name="picks")
         places = keep.tile([P, S // PER_COLUMN], U16, name="places")
         tab_w = [held([P, T], I32, f"tab_w{a}") for a in range(2)]
-        tab_s = held([P, 2, T], U8, "tab_s")
+        tab_s = held([P, T], U8, "tab_s")
         v_w = [held([P, S], U32, f"v_w{a}") for a in range(2)]
-        picked_s = held([P, 2, S], U8, "picked_s")
+        picked_s = held([P, S], U8, "picked_s")
         v_s = held([P, 2, S], U8, "v_s")
         w4_raw = held([P, 2, 2 * H], U8, "w4_raw")
         w4_w = held([P, 2, 2 * H], U8, "w4_w")
@@ -61,44 +61,44 @@ def tile_list_foundry_job_dispatch_kernel(
         ident = held([P, P], F32, "ident")
 
         nc.vector.memset(w4_sraw[:].bitcast(I32), 0)
-        nc.vector.memset(tab_s[:SCALE_ROW, 0, :].bitcast(I32), 0)
-        nc.vector.memset(tab_s[:SCALE_ROW, 1, :].bitcast(I32), 0)
+        nc.vector.memset(tab_s[:SCALE_ROW, :].bitcast(I32), 0)
         nc.vector.memset(v_s[:].bitcast(I32), 0)
         nc.vector.memset(w8_s[:].bitcast(I32), 0)
         make_identity(nc, ident[:])
 
         nc.sync.dma_start(picks[:], offs)
         nc.sync.dma_start(
-            out=tab_s[SCALE_ROW:, :, :].bitcast(I32), in_=tab_scales.rearrange("a q t -> q a t").bitcast(I32)
+            out=tab_s[SCALE_ROW:, :].bitcast(I32), in_=tab_scales.rearrange("a q t -> (a q) t").bitcast(I32)
         )
 
         def load_table(a, pieces):
             words = tab_words[a].rearrange("p t i -> p (t i)").bitcast(I32)
-            for c0, c1 in zip(pieces, pieces[1:]):
-                nc.sync.dma_start(out=tab_w[a][:, c0:c1], in_=words[:, c0:c1])
+            for c in range(0, T, T // pieces):
+                nc.sync.dma_start(out=tab_w[a][:, c : c + T // pieces], in_=words[:, c : c + T // pieces])
 
+        load_table(0, 2)
         nc.sync.dma_start(out=w4_raw[:].bitcast(I32), in_=w4_words.rearrange("a p c -> p a c").bitcast(I32))
         for g in range(QUADRANTS):
-            nc.sync.dma_start(
+            nc.scalar.dma_start(
                 out=w4_sraw[32 * g : 32 * g + 4, :, :].bitcast(I32),
                 in_=w4_scales[:, 4 * g : 4 * g + 4, :].rearrange("a r c -> r a c").bitcast(I32),
             )
-        load_table(0, (0, T))
-        load_table(1, (0, 1536, 2816, T))
-        for a in range(2):
-            nc.vector.tensor_copy(picked_s[:, a, :], tab_s[:, a, :].indirect(picks[:]))
-        for g in range(QUADRANTS):
-            first = SCALE_ROW + 4 * g
-            nc.scalar.dma_start(
-                out=v_s[32 * g : 32 * g + 4, :, :].bitcast(I32), in_=picked_s[first : first + 4, :, :].bitcast(I32)
-            )
+        load_table(1, 2)
+        nc.vector.tensor_copy(picked_s[:], tab_s[:].indirect(picks[:]))
+        for a, queue in enumerate((nc.scalar, nc.sync)):
+            for g in range(QUADRANTS):
+                first = SCALE_ROW + 16 * a + 4 * g
+                queue.dma_start(
+                    out=v_s[32 * g : 32 * g + 4, a, :].bitcast(I32), in_=picked_s[first : first + 4, :].bitcast(I32)
+                )
 
         w1_raw = {}
         for b in range(2):
             for a in range(2):
                 w1_raw[a, b] = rotating([P, PACK, PASS], F32, "raw", 4)
                 rows = w1[a * PASS : (a + 1) * PASS, b * PASS : (b + 1) * PASS].rearrange("(p j) c -> p j c", j=PACK)
-                nc.sync.dma_start(out=w1_raw[a, b][:], in_=rows)
+                for j in range(0, PACK, 2):
+                    nc.sync.dma_start(out=w1_raw[a, b][:, j : j + 2, :], in_=rows[:, j : j + 2, :])
 
         rel_sb = {}
 
@@ -123,6 +123,7 @@ def tile_list_foundry_job_dispatch_kernel(
         nc.sync.dma_start(out=gains[:], in_=wgo)
         load_rel(1, 1)
 
+        nc.vector.tensor_copy(v_w[0][:], tab_w[0][:].bitcast(U32).indirect(picks[:]))
         nc.vector.tensor_copy(
             w4_w[:].bitcast(U16).rearrange("p a (b t m) -> p (a b) t m", t=PACK, m=P),
             w4_raw[:].bitcast(U16).rearrange("p a (b m t) -> p (a b) t m", t=PACK, m=P),
@@ -131,7 +132,6 @@ def tile_list_foundry_job_dispatch_kernel(
             w4_s[:].rearrange("p a (b t m) -> p (a b) t m", t=PACK, m=P),
             w4_sraw[:].rearrange("p a (b m t) -> p (a b) t m", t=PACK, m=P),
         )
-        nc.vector.tensor_copy(v_w[0][:], tab_w[0][:].bitcast(U32).indirect(picks[:]))
         for h in range(2):
             nc.vector.tensor_copy(
                 v_w[1][:, h * HALF : (h + 1) * HALF],
@@ -317,18 +317,18 @@ def tile_list_foundry_job_dispatch_kernel(
         mould_and_min(0, 2, high[:2])
         mould_and_min(0, 3, high[2:])
         add_rel_on_vector(0, 0)
+        add_rel_on_vector(0, 1)
         mould_and_min(1, 0, high[:2])
         melt_half(1, 1, low)
         add_rel_on_vector(1, 0)
         quantise_h(0, 0)
         mould_and_min(1, 1, high[2:])
         quantise_h(1, 0)
+        quantise_h(0, 1)
         mould_and_min(1, 2, high[:2])
         mould_and_min(1, 3, high[2:])
-        for b in range(2):
-            add_rel_on_vector(b, 1)
-        for b in range(2):
-            quantise_h(b, 1)
+        add_rel_on_vector(1, 1)
+        quantise_h(1, 1)
         finish(0, (0, 1), banks[5])
         finish(0, (2, 3), banks[6])
         finish(1, (0, 1), banks[7])
@@ -358,8 +358,8 @@ def tile_list_foundry_job_dispatch_kernel(
         finish(3, (2, 3), banks[7])
 
         for n in range(N // P):
-            cuts = (0, HALF, HALF + QUARTER, S) if n == N // P - 1 else (0, S)
-            for c0, c1 in zip(cuts, cuts[1:]):
-                result = promised[n // 2][:, n % 2, c0:c1]
-                nc.vector.tensor_tensor(result, page[n][:, c0:c1], result, ALU.max)
-                nc.sync.dma_start(out=out[n * P : (n + 1) * P, c0:c1], in_=result)
+            width = S // 2 if n == N // P - 1 else S
+            for c in range(0, S, width):
+                result = promised[n // 2][:, n % 2, c : c + width]
+                nc.vector.tensor_tensor(result, page[n][:, c : c + width], result, ALU.max)
+                nc.sync.dma_start(out=out[n * P : (n + 1) * P, c : c + width], in_=result)

@@ -26,6 +26,7 @@ QUARTER = S // 4
 PER_COLUMN = 16
 SCALE_ROW = P - 32
 RUN = 2
+TABLE_PIECES = 2
 
 
 def tile_list_foundry_job_dispatch_kernel(
@@ -71,34 +72,44 @@ def tile_list_foundry_job_dispatch_kernel(
             out=tab_s[SCALE_ROW:, :].bitcast(I32), in_=tab_scales.rearrange("a q t -> (a q) t").bitcast(I32)
         )
 
-        def load_table(a, pieces):
+        def load_table(a):
             words = tab_words[a].rearrange("p t i -> p (t i)").bitcast(I32)
-            for c in range(0, T, T // pieces):
-                nc.sync.dma_start(out=tab_w[a][:, c : c + T // pieces], in_=words[:, c : c + T // pieces])
+            piece = T // TABLE_PIECES
+            for c in range(0, T, piece):
+                nc.sync.dma_start(out=tab_w[a][:, c : c + piece], in_=words[:, c : c + piece])
 
-        load_table(0, 2)
+        load_table(0)
         nc.sync.dma_start(out=w4_raw[:].bitcast(I32), in_=w4_words.rearrange("a p c -> p a c").bitcast(I32))
         for g in range(QUADRANTS):
             nc.scalar.dma_start(
                 out=w4_sraw[32 * g : 32 * g + 4, :, :].bitcast(I32),
                 in_=w4_scales[:, 4 * g : 4 * g + 4, :].rearrange("a r c -> r a c").bitcast(I32),
             )
-        load_table(1, 2)
+        load_table(1)
         nc.vector.tensor_copy(picked_s[:], tab_s[:].indirect(picks[:]))
-        for a, queue in enumerate((nc.scalar, nc.sync)):
+
+        def move_plane(a, queue):
             for g in range(QUADRANTS):
                 first = SCALE_ROW + 16 * a + 4 * g
                 queue.dma_start(
                     out=v_s[32 * g : 32 * g + 4, a, :].bitcast(I32), in_=picked_s[first : first + 4, :].bitcast(I32)
                 )
 
+        move_plane(0, nc.scalar)
+
         w1_raw = {}
-        for b in range(2):
-            for a in range(2):
-                w1_raw[a, b] = rotating([P, PACK, PASS], F32, "raw", 4)
-                rows = w1[a * PASS : (a + 1) * PASS, b * PASS : (b + 1) * PASS].rearrange("(p j) c -> p j c", j=PACK)
-                for j in range(0, PACK, 2):
-                    nc.sync.dma_start(out=w1_raw[a, b][:, j : j + 2, :], in_=rows[:, j : j + 2, :])
+
+        def load_w1(a, b):
+            w1_raw[a, b] = rotating([P, PACK, PASS], F32, "raw", 4)
+            rows = w1[a * PASS : (a + 1) * PASS, b * PASS : (b + 1) * PASS].rearrange("(p j) c -> p j c", j=PACK)
+            for j in range(0, PACK, 2):
+                nc.sync.dma_start(out=w1_raw[a, b][:, j : j + 2, :], in_=rows[:, j : j + 2, :])
+
+        load_w1(0, 0)
+        move_plane(1, nc.sync)
+        load_w1(1, 0)
+        load_w1(0, 1)
+        load_w1(1, 1)
 
         rel_sb = {}
 
@@ -155,24 +166,14 @@ def tile_list_foundry_job_dispatch_kernel(
                 stop=(a == 1),
             )
 
-        def melt_open(b, h, group):
+        def open_melt(b, h, group):
             for t in range(PACK):
                 melt_pass(b, h, t, 0, group[t])
 
-        def melt_close(b, h, group):
+        def close_melt(b, h, group, first_pass):
             neg_melt = held([P, 2, PACK, QUARTER], F32, f"melt{b}{h}")
             for t in range(PACK):
-                melt_pass(b, h, t, 1, group[t])
-                nc.scalar.activation(
-                    out=neg_melt[:, :, t, :], in_=group[t][:].rearrange("p (i j) -> p i j", i=2), func=COPY, scale=-1.0
-                )
-            for i in range(2):
-                later[b, 2 * h + i] = neg_melt[:, i]
-
-        def melt_half(b, h, group):
-            neg_melt = held([P, 2, PACK, QUARTER], F32, f"melt{b}{h}")
-            for t in range(PACK):
-                for a in range(2):
+                for a in range(first_pass, 2):
                     melt_pass(b, h, t, a, group[t])
                 nc.scalar.activation(
                     out=neg_melt[:, :, t, :], in_=group[t][:].rearrange("p (i j) -> p i j", i=2), func=COPY, scale=-1.0
@@ -231,17 +232,18 @@ def tile_list_foundry_job_dispatch_kernel(
         h_w = {}
         h_s = {}
 
-        def add_rel_on_vector(b, q):
-            h_bf[b, q] = rotating([P, QUARTER, PACK], BF16, "h_bf", 4)
-            nc.vector.tensor_tensor(
-                h_bf[b, q][:].rearrange("p (c i) t -> p c t i", i=RUN),
-                later[b, q].rearrange("p t (c i) -> p c t i", i=RUN),
-                rel_sb[b, q].rearrange("p t (c i) -> p c t i", i=RUN),
-                ALU.add,
-            )
+        def add_rel_on_vector(b):
+            h_bf[b, 0] = held([P, HALF, PACK], BF16, f"h_first{b}")
+            for q in range(2):
+                nc.vector.tensor_tensor(
+                    h_bf[b, 0][:, q * QUARTER : (q + 1) * QUARTER, :].rearrange("p (c i) t -> p c t i", i=RUN),
+                    later[b, q].rearrange("p t (c i) -> p c t i", i=RUN),
+                    rel_sb[b, q].rearrange("p t (c i) -> p c t i", i=RUN),
+                    ALU.add,
+                )
 
         def add_rel_on_tensor(b, q, group, back_bank):
-            h_bf[b, q] = rotating([P, QUARTER, PACK], BF16, "h_bf", 4)
+            h_bf[b, q] = rotating([P, QUARTER, PACK], BF16, "h_bf", 2)
             turned = []
             for jb in range(QUARTER // P):
                 acc = group[jb][:].rearrange("j (t p) -> j t p", t=PACK)
@@ -267,15 +269,17 @@ def tile_list_foundry_job_dispatch_kernel(
             )
 
         def quantise_h(b, q):
-            h_w[b, q] = rotating([P, QUARTER], U32, "h_w", 8)
-            h_s[b, q] = rotating([P, QUARTER], U8, "h_s", 8)
+            width = h_bf[b, q].shape[1]
+            h_w[b, q] = held([P, width], U32, f"h_w{b}{q}")
+            h_s[b, q] = held([P, width], U8, f"h_s{b}{q}")
             nc.vector.quantize_mx(
                 out=h_w[b, q][:].bitcast(FP8X4), scales=h_s[b, q][:], in_=h_bf[b, q][:].rearrange("p j t -> p (j t)")
             )
 
         def finish(q, blocks, bank):
-            cols = slice(q * QUARTER, (q + 1) * QUARTER)
-            acc = bank[:].rearrange("p (i j) -> p i j", i=2)[:, : len(blocks), :]
+            width = h_w[0, q].shape[1]
+            first = q * QUARTER
+            acc = bank[:].rearrange("p (i j) -> p i j", j=width)[:, : len(blocks), :]
             for i, n in enumerate(blocks):
                 for b in (1, 0):
                     nc.tensor.matmul_mx(
@@ -287,52 +291,48 @@ def tile_list_foundry_job_dispatch_kernel(
                         start=(b == 1),
                         stop=(b == 0),
                     )
-            y = rotating([P, 2, QUARTER], F32, "y", 4)
+            y_bank = rotating([P, HALF], F32, "y", 4)
+            y = y_bank[:].rearrange("p (i j) -> p i j", j=width)
             nc.scalar.activation(out=y[:, : len(blocks), :], in_=acc, func=COPY, scale=-1.0)
             for i, n in enumerate(blocks):
                 nc.vector.tensor_tensor(
-                    page[n][:].indirect(
-                        places[:, q * QUARTER // PER_COLUMN : (q + 1) * QUARTER // PER_COLUMN]
-                    ),
+                    page[n][:].indirect(places[:, first // PER_COLUMN : (first + width) // PER_COLUMN]),
                     y[:, i, :],
-                    gains[:, cols],
+                    gains[:, first : first + width],
                     ALU.mult,
                 )
 
         low, high = banks[:4], banks[4:]
-        melt_open(0, 0, low)
-        melt_open(0, 1, high)
-        melt_close(0, 0, low)
-        melt_close(0, 1, high)
+        for h, group in enumerate((low, high)):
+            open_melt(0, h, group)
+        for h, group in enumerate((low, high)):
+            close_melt(0, h, group, 1)
         for a in range(2):
             round_w1_on_vector(a, 0)
             quantise_w1(a, 0)
         round_w1_on_vector(0, 1)
-        quantise_w1(0, 1)
         round_w1_on_scalar(1, 1)
-        melt_half(1, 0, low)
+        close_melt(1, 0, low, 0)
         mould_and_min(0, 0, high[:2])
+        quantise_w1(0, 1)
         mould_and_min(0, 1, high[2:])
         quantise_w1(1, 1)
         mould_and_min(0, 2, high[:2])
         mould_and_min(0, 3, high[2:])
-        add_rel_on_vector(0, 0)
-        add_rel_on_vector(0, 1)
+
+        add_rel_on_vector(0)
         mould_and_min(1, 0, high[:2])
-        melt_half(1, 1, low)
-        add_rel_on_vector(1, 0)
+        close_melt(1, 1, low, 0)
         quantise_h(0, 0)
         mould_and_min(1, 1, high[2:])
+        add_rel_on_vector(1)
         quantise_h(1, 0)
-        quantise_h(0, 1)
         mould_and_min(1, 2, high[:2])
         mould_and_min(1, 3, high[2:])
-        add_rel_on_vector(1, 1)
-        quantise_h(1, 1)
-        finish(0, (0, 1), banks[5])
-        finish(0, (2, 3), banks[6])
-        finish(1, (0, 1), banks[7])
-        finish(1, (2,), banks[4])
+        finish(0, (0,), high[0])
+        finish(0, (1,), high[2])
+        finish(0, (2,), high[3])
+
         add_rel_on_tensor(0, 2, low[:2], low[1])
         add_rel_on_tensor(0, 3, low[2:], low[3])
         for q in (2, 3):
@@ -346,16 +346,16 @@ def tile_list_foundry_job_dispatch_kernel(
             )
             promised.append(both)
 
-        add_rel_on_tensor(1, 2, low[:2], banks[5])
+        add_rel_on_tensor(1, 2, low[:2], high[1])
         quantise_h(1, 2)
-        finish(1, (3,), banks[5])
-        add_rel_on_tensor(1, 3, low[2:], banks[6])
-        finish(2, (0, 1), banks[7])
-        finish(2, (2,), banks[4])
+        finish(0, (3,), high[1])
+        add_rel_on_tensor(1, 3, low[2:], high[2])
+        finish(2, (0, 1), high[3])
+        finish(2, (2,), high[0])
         quantise_h(1, 3)
-        finish(2, (3,), banks[6])
-        finish(3, (0, 1), banks[5])
-        finish(3, (2, 3), banks[7])
+        finish(2, (3,), high[2])
+        finish(3, (0, 1), high[1])
+        finish(3, (2, 3), high[3])
 
         for n in range(N // P):
             width = S // 2 if n == N // P - 1 else S

@@ -72,20 +72,19 @@ def tile_list_foundry_job_dispatch_kernel(
             out=tab_s[SCALE_ROW:, :].bitcast(I32), in_=tab_scales.rearrange("a q t -> (a q) t").bitcast(I32)
         )
 
-        def load_table(a):
+        def load_table(a, piece):
             words = tab_words[a].rearrange("p t i -> p (t i)").bitcast(I32)
-            piece = T // TABLE_PIECES
-            for c in range(0, T, piece):
-                nc.sync.dma_start(out=tab_w[a][:, c : c + piece], in_=words[:, c : c + piece])
+            cols = slice(piece * T // TABLE_PIECES, (piece + 1) * T // TABLE_PIECES)
+            nc.sync.dma_start(out=tab_w[a][:, cols], in_=words[:, cols])
 
-        load_table(0)
+        load_table(0, 0)
+        load_table(0, 1)
         nc.sync.dma_start(out=w4_raw[:].bitcast(I32), in_=w4_words.rearrange("a p c -> p a c").bitcast(I32))
         for g in range(QUADRANTS):
             nc.scalar.dma_start(
                 out=w4_sraw[32 * g : 32 * g + 4, :, :].bitcast(I32),
                 in_=w4_scales[:, 4 * g : 4 * g + 4, :].rearrange("a r c -> r a c").bitcast(I32),
             )
-        load_table(1)
         nc.vector.tensor_copy(picked_s[:], tab_s[:].indirect(picks[:]))
 
         def move_plane(a, queue):
@@ -95,7 +94,10 @@ def tile_list_foundry_job_dispatch_kernel(
                     out=v_s[32 * g : 32 * g + 4, a, :].bitcast(I32), in_=picked_s[first : first + 4, :].bitcast(I32)
                 )
 
-        move_plane(0, nc.scalar)
+        move_plane(0, nc.sync)
+        load_table(1, 0)
+        load_table(1, 1)
+        move_plane(1, nc.sync)
 
         w1_raw = {}
 
@@ -106,15 +108,16 @@ def tile_list_foundry_job_dispatch_kernel(
                 nc.sync.dma_start(out=w1_raw[a, b][:, j : j + 2, :], in_=rows[:, j : j + 2, :])
 
         load_w1(0, 0)
-        move_plane(1, nc.sync)
         load_w1(1, 0)
         load_w1(0, 1)
         load_w1(1, 1)
 
         rel_sb = {}
+        rel_half = {}
 
         def load_rel(b, h):
             both = held([P, PACK, HALF], F32, f"rel{b}{h}")
+            rel_half[b, h] = both
             nc.sync.dma_start(
                 out=both[:],
                 in_=rel[b * PASS : (b + 1) * PASS, h * HALF : (h + 1) * HALF].rearrange("(p t) j -> p t j", t=PACK),
@@ -171,7 +174,12 @@ def tile_list_foundry_job_dispatch_kernel(
                 melt_pass(b, h, t, 0, group[t])
 
         def close_melt(b, h, group, first_pass):
-            neg_melt = held([P, 2, PACK, QUARTER], F32, f"melt{b}{h}")
+            if (b, h) == (1, 1):
+                neg_melt = w1_raw[1, 1][:].rearrange("p a (b j) -> p (a b) j", j=QUARTER).rearrange(
+                    "p (i t) j -> p i t j", t=PACK
+                )
+            else:
+                neg_melt = held([P, 2, PACK, QUARTER], F32, f"melt{b}{h}")
             for t in range(PACK):
                 for a in range(first_pass, 2):
                     melt_pass(b, h, t, a, group[t])
@@ -181,12 +189,16 @@ def tile_list_foundry_job_dispatch_kernel(
             for i in range(2):
                 later[b, 2 * h + i] = neg_melt[:, i]
 
+        sums = held([P, 2 * S], F32, "sums")
         w1_bf = {}
         w1_w = {}
         w1_s = {}
 
         def w1_views(a, b):
-            w1_bf[a, b] = rotating([P, PACK, P, PACK], BF16, "w1_bf", 3)
+            if (a, b) == (1, 1):
+                w1_bf[a, b] = sums[:, HALF : 3 * HALF].bitcast(BF16).rearrange("p (t m j) -> p t m j", t=PACK, j=PACK)
+            else:
+                w1_bf[a, b] = rotating([P, PACK, P, PACK], BF16, "w1_bf", 2)
             return (
                 w1_bf[a, b][:].rearrange("p t m j -> p m j t"),
                 w1_raw[a, b][:].rearrange("p j (m t) -> p m j t", t=PACK),
@@ -232,18 +244,17 @@ def tile_list_foundry_job_dispatch_kernel(
         h_w = {}
         h_s = {}
 
-        def add_rel_on_vector(b):
-            h_bf[b, 0] = held([P, HALF, PACK], BF16, f"h_first{b}")
-            for q in range(2):
-                nc.vector.tensor_tensor(
-                    h_bf[b, 0][:, q * QUARTER : (q + 1) * QUARTER, :].rearrange("p (c i) t -> p c t i", i=RUN),
-                    later[b, q].rearrange("p t (c i) -> p c t i", i=RUN),
-                    rel_sb[b, q].rearrange("p t (c i) -> p c t i", i=RUN),
-                    ALU.add,
-                )
+        def add_rel_on_vector(b, q):
+            h_bf[b, q] = rel_half[0, 0][:, q, :].bitcast(BF16).rearrange("p (j t) -> p j t", t=PACK)
+            nc.vector.tensor_tensor(
+                h_bf[b, q][:].rearrange("p (c i) t -> p c t i", i=RUN),
+                later[b, q].rearrange("p t (c i) -> p c t i", i=RUN),
+                rel_sb[b, q].rearrange("p t (c i) -> p c t i", i=RUN),
+                ALU.add,
+            )
 
         def add_rel_on_tensor(b, q, group, back_bank):
-            h_bf[b, q] = rotating([P, QUARTER, PACK], BF16, "h_bf", 2)
+            h_bf[b, q] = rotating([P, QUARTER, PACK], BF16, "h_bf", 4)
             turned = []
             for jb in range(QUARTER // P):
                 acc = group[jb][:].rearrange("j (t p) -> j t p", t=PACK)
@@ -268,12 +279,35 @@ def tile_list_foundry_job_dispatch_kernel(
                 in_=back.rearrange("p jb u j -> p jb j u"),
             )
 
+        def add_rel_on_gpsimd(b, q):
+            total = sums[:, q * S : (q + 1) * S].rearrange("p (t j) -> p t j", t=PACK)
+            nc.gpsimd.tensor_tensor(total, later[b, q], rel_sb[b, q], ALU.add)
+            h_bf[b, q] = held([P, QUARTER, PACK], BF16, f"h_first{b}{q}")
+            nc.scalar.copy(
+                out=h_bf[b, q][:].rearrange("p (c i) t -> p c t i", i=PACK),
+                in_=total.rearrange("p t (c i) -> p c t i", i=PACK),
+            )
+
         def quantise_h(b, q):
             width = h_bf[b, q].shape[1]
             h_w[b, q] = held([P, width], U32, f"h_w{b}{q}")
             h_s[b, q] = held([P, width], U8, f"h_s{b}{q}")
             nc.vector.quantize_mx(
                 out=h_w[b, q][:].bitcast(FP8X4), scales=h_s[b, q][:], in_=h_bf[b, q][:].rearrange("p j t -> p (j t)")
+            )
+
+        def store_page(n, width):
+            for c in range(0, S, width):
+                result = promised[n // 2][:, n % 2, c : c + width]
+                nc.vector.tensor_tensor(result, page[n][:, c : c + width], result, ALU.max)
+                nc.sync.dma_start(out=out[n * P : (n + 1) * P, c : c + width], in_=result)
+
+        def scatter(n, y, first, width):
+            nc.vector.tensor_tensor(
+                page[n][:].indirect(places[:, first // PER_COLUMN : (first + width) // PER_COLUMN]),
+                y,
+                gains[:, first : first + width],
+                ALU.mult,
             )
 
         def finish(q, blocks, bank):
@@ -295,12 +329,15 @@ def tile_list_foundry_job_dispatch_kernel(
             y = y_bank[:].rearrange("p (i j) -> p i j", j=width)
             nc.scalar.activation(out=y[:, : len(blocks), :], in_=acc, func=COPY, scale=-1.0)
             for i, n in enumerate(blocks):
-                nc.vector.tensor_tensor(
-                    page[n][:].indirect(places[:, first // PER_COLUMN : (first + width) // PER_COLUMN]),
-                    y[:, i, :],
-                    gains[:, first : first + width],
-                    ALU.mult,
-                )
+                if q < 3:
+                    scatter(n, y[:, i, :], first, width)
+                elif n < 3:
+                    scatter(n, y[:, i, :], first, width)
+                    store_page(n, S)
+                else:
+                    for c in range(0, width, width // 2):
+                        scatter(n, y[:, i, c : c + width // 2], first + c, width // 2)
+                    store_page(n, S // 2)
 
         low, high = banks[:4], banks[4:]
         for h, group in enumerate((low, high)):
@@ -313,31 +350,28 @@ def tile_list_foundry_job_dispatch_kernel(
         round_w1_on_vector(0, 1)
         round_w1_on_scalar(1, 1)
         close_melt(1, 0, low, 0)
-        mould_and_min(0, 0, high[:2])
+        close_melt(1, 1, high, 0)
+        mould_and_min(0, 0, low[:2])
         quantise_w1(0, 1)
-        mould_and_min(0, 1, high[2:])
+        mould_and_min(0, 1, low[2:])
         quantise_w1(1, 1)
-        mould_and_min(0, 2, high[:2])
-        mould_and_min(0, 3, high[2:])
-
-        add_rel_on_vector(0)
-        mould_and_min(1, 0, high[:2])
-        close_melt(1, 1, low, 0)
-        quantise_h(0, 0)
-        mould_and_min(1, 1, high[2:])
-        add_rel_on_vector(1)
-        quantise_h(1, 0)
+        mould_and_min(0, 2, low[:2])
+        mould_and_min(0, 3, low[2:])
+        add_rel_on_gpsimd(0, 0)
+        add_rel_on_gpsimd(0, 1)
+        mould_and_min(1, 0, low[:2])
+        mould_and_min(1, 1, low[2:])
         mould_and_min(1, 2, high[:2])
         mould_and_min(1, 3, high[2:])
+        add_rel_on_vector(1, 0)
+        quantise_h(0, 0)
+        quantise_h(1, 0)
+        add_rel_on_vector(1, 1)
+        quantise_h(0, 1)
+        quantise_h(1, 1)
+        add_rel_on_tensor(0, 2, low[:2], high[2])
         finish(0, (0,), high[0])
-        finish(0, (1,), high[2])
-        finish(0, (2,), high[3])
-
-        add_rel_on_tensor(0, 2, low[:2], low[1])
-        add_rel_on_tensor(0, 3, low[2:], low[3])
-        for q in (2, 3):
-            quantise_h(0, q)
-
+        finish(0, (1,), high[1])
         promised = []
         for pair in range(2):
             both = rotating([P, 2, S], F32, "raw", 4)
@@ -345,21 +379,20 @@ def tile_list_foundry_job_dispatch_kernel(
                 out=both[:], in_=x0[2 * pair * P : 2 * (pair + 1) * P, :].rearrange("(i p) m -> p i m", p=P)
             )
             promised.append(both)
-
-        add_rel_on_tensor(1, 2, low[:2], high[1])
+        add_rel_on_tensor(1, 2, high[:2], high[3])
+        finish(0, (2,), low[2])
+        finish(0, (3,), low[3])
+        add_rel_on_tensor(0, 3, low[2:], high[0])
+        finish(1, (0,), low[0])
+        finish(1, (1,), low[1])
+        add_rel_on_tensor(1, 3, low[:2], high[1])
+        finish(1, (2,), high[2])
+        quantise_h(0, 2)
         quantise_h(1, 2)
-        finish(0, (3,), high[1])
-        add_rel_on_tensor(1, 3, low[2:], high[2])
-        finish(2, (0, 1), high[3])
-        finish(2, (2,), high[0])
+        finish(1, (3,), high[3])
+        quantise_h(0, 3)
         quantise_h(1, 3)
-        finish(2, (3,), high[2])
-        finish(3, (0, 1), high[1])
-        finish(3, (2, 3), high[3])
-
-        for n in range(N // P):
-            width = S // 2 if n == N // P - 1 else S
-            for c in range(0, S, width):
-                result = promised[n // 2][:, n % 2, c : c + width]
-                nc.vector.tensor_tensor(result, page[n][:, c : c + width], result, ALU.max)
-                nc.sync.dma_start(out=out[n * P : (n + 1) * P, c : c + width], in_=result)
+        finish(2, (0, 1), high[1])
+        finish(2, (2, 3), high[0])
+        finish(3, (0, 1), low[2])
+        finish(3, (2, 3), low[3])

@@ -94,10 +94,9 @@ def tile_list_foundry_job_dispatch_kernel(
                     out=v_s[32 * g : 32 * g + 4, a, :].bitcast(I32), in_=picked_s[first : first + 4, :].bitcast(I32)
                 )
 
-        move_plane(0, nc.sync)
         load_table(1, 0)
+        move_plane(0, nc.sync)
         load_table(1, 1)
-        move_plane(1, nc.sync)
 
         w1_raw = {}
 
@@ -106,6 +105,8 @@ def tile_list_foundry_job_dispatch_kernel(
             rows = w1[a * PASS : (a + 1) * PASS, b * PASS : (b + 1) * PASS].rearrange("(p j) c -> p j c", j=PACK)
             for j in range(0, PACK, 2):
                 nc.sync.dma_start(out=w1_raw[a, b][:, j : j + 2, :], in_=rows[:, j : j + 2, :])
+                if (a, b, j) == (0, 0, 0):
+                    move_plane(1, nc.sync)
 
         load_w1(0, 0)
         load_w1(1, 0)

@@ -201,8 +201,8 @@ def tile_list_foundry_job_dispatch_kernel(
             else:
                 w1_bf[a, b] = rotating([P, PACK, P, PACK], BF16, "w1_bf", 2)
             return (
-                w1_bf[a, b][:].rearrange("p t m j -> p m j t"),
-                w1_raw[a, b][:].rearrange("p j (m t) -> p m j t", t=PACK),
+                w1_bf[a, b][:].rearrange("p t m j -> p m t j"),
+                w1_raw[a, b][:].rearrange("p j (m t) -> p m t j", t=PACK),
             )
 
         def round_w1_on_vector(a, b):

@@ -62,15 +62,15 @@ def tile_list_foundry_job_dispatch_kernel(
         ident = held([P, P], F32, "ident")
 
         nc.vector.memset(w4_sraw[:].bitcast(I32), 0)
-        nc.vector.memset(tab_s[:SCALE_ROW, :].bitcast(I32), 0)
+        for a in range(2):
+            nc.vector.memset(tab_s[64 * a : 64 * a + 48, :].bitcast(I32), 0)
         nc.vector.memset(v_s[:].bitcast(I32), 0)
         nc.vector.memset(w8_s[:].bitcast(I32), 0)
         make_identity(nc, ident[:])
 
         nc.sync.dma_start(picks[:], offs)
-        nc.sync.dma_start(
-            out=tab_s[SCALE_ROW:, :].bitcast(I32), in_=tab_scales.rearrange("a q t -> (a q) t").bitcast(I32)
-        )
+        for a in range(2):
+            nc.sync.dma_start(out=tab_s[64 * a + 48 : 64 * a + 64, :].bitcast(I32), in_=tab_scales[a].bitcast(I32))
 
         def load_table(a, piece):
             words = tab_words[a].rearrange("p t i -> p (t i)").bitcast(I32)
@@ -89,7 +89,7 @@ def tile_list_foundry_job_dispatch_kernel(
 
         def move_plane(a, queue):
             for g in range(QUADRANTS):
-                first = SCALE_ROW + 16 * a + 4 * g
+                first = 64 * a + 48 + 4 * g
                 queue.dma_start(
                     out=v_s[32 * g : 32 * g + 4, a, :].bitcast(I32), in_=picked_s[first : first + 4, :].bitcast(I32)
                 )
@@ -338,7 +338,7 @@ def tile_list_foundry_job_dispatch_kernel(
                 else:
                     for c in range(0, width, width // 2):
                         scatter(n, y[:, i, c : c + width // 2], first + c, width // 2)
-                    store_page(n, S // 2)
+                    store_page(n, S // 4)
 
         low, high = banks[:4], banks[4:]
         for h, group in enumerate((low, high)):
@@ -349,8 +349,8 @@ def tile_list_foundry_job_dispatch_kernel(
             round_w1_on_vector(a, 0)
             quantise_w1(a, 0)
         round_w1_on_vector(0, 1)
-        round_w1_on_scalar(1, 1)
         close_melt(1, 0, low, 0)
+        round_w1_on_scalar(1, 1)
         close_melt(1, 1, high, 0)
         mould_and_min(0, 0, low[:2])
         quantise_w1(0, 1)

@@ -24,9 +24,11 @@ QUADRANTS = 4
 HALF = S // 2
 QUARTER = S // 4
 PER_COLUMN = 16
-SCALE_ROW = P - 32
+SCALE_ROWS = 16
+LANDING = 64 - SCALE_ROWS
 RUN = 2
 TABLE_PIECES = 2
+LAST_PIECES = 4
 
 
 def tile_list_foundry_job_dispatch_kernel(
@@ -63,14 +65,16 @@ def tile_list_foundry_job_dispatch_kernel(
 
         nc.vector.memset(w4_sraw[:].bitcast(I32), 0)
         for a in range(2):
-            nc.vector.memset(tab_s[64 * a : 64 * a + 48, :].bitcast(I32), 0)
+            nc.vector.memset(tab_s[64 * a : 64 * a + LANDING, :].bitcast(I32), 0)
         nc.vector.memset(v_s[:].bitcast(I32), 0)
         nc.vector.memset(w8_s[:].bitcast(I32), 0)
         make_identity(nc, ident[:])
 
         nc.sync.dma_start(picks[:], offs)
         for a in range(2):
-            nc.sync.dma_start(out=tab_s[64 * a + 48 : 64 * a + 64, :].bitcast(I32), in_=tab_scales[a].bitcast(I32))
+            nc.sync.dma_start(
+                out=tab_s[64 * a + LANDING : 64 * (a + 1), :].bitcast(I32), in_=tab_scales[a].bitcast(I32)
+            )
 
         def load_table(a, piece):
             words = tab_words[a].rearrange("p t i -> p (t i)").bitcast(I32)
@@ -87,44 +91,39 @@ def tile_list_foundry_job_dispatch_kernel(
             )
         nc.vector.tensor_copy(picked_s[:], tab_s[:].indirect(picks[:]))
 
-        def move_plane(a, queue):
+        def move_plane(a):
             for g in range(QUADRANTS):
-                first = 64 * a + 48 + 4 * g
-                queue.dma_start(
+                first = 64 * a + LANDING + 4 * g
+                nc.sync.dma_start(
                     out=v_s[32 * g : 32 * g + 4, a, :].bitcast(I32), in_=picked_s[first : first + 4, :].bitcast(I32)
                 )
 
         load_table(1, 0)
-        move_plane(0, nc.sync)
+        move_plane(0)
         load_table(1, 1)
 
-        w1_raw = {}
+        w1_raw = {(a, b): rotating([P, PACK, PASS], F32, "raw", 4) for b in range(2) for a in range(2)}
 
-        def load_w1(a, b):
-            w1_raw[a, b] = rotating([P, PACK, PASS], F32, "raw", 4)
-            rows = w1[a * PASS : (a + 1) * PASS, b * PASS : (b + 1) * PASS].rearrange("(p j) c -> p j c", j=PACK)
-            for j in range(0, PACK, 2):
-                nc.sync.dma_start(out=w1_raw[a, b][:, j : j + 2, :], in_=rows[:, j : j + 2, :])
-                if (a, b, j) == (0, 0, 0):
-                    move_plane(1, nc.sync)
+        def w1_rows(a, b):
+            return w1[a * PASS : (a + 1) * PASS, b * PASS : (b + 1) * PASS].rearrange("(p j) c -> p j c", j=PACK)
 
-        load_w1(0, 0)
-        load_w1(1, 0)
-        load_w1(0, 1)
-        load_w1(1, 1)
+        nc.sync.dma_start(out=w1_raw[0, 0][:, :2, :], in_=w1_rows(0, 0)[:, :2, :])
+        move_plane(1)
+        nc.sync.dma_start(out=w1_raw[0, 0][:, 2:, :], in_=w1_rows(0, 0)[:, 2:, :])
+        for a, b in ((1, 0), (0, 1), (1, 1)):
+            nc.sync.dma_start(out=w1_raw[a, b][:], in_=w1_rows(a, b))
 
         rel_sb = {}
         rel_half = {}
 
         def load_rel(b, h):
-            both = held([P, PACK, HALF], F32, f"rel{b}{h}")
-            rel_half[b, h] = both
+            rel_half[b, h] = held([P, PACK, HALF], F32, f"rel{b}{h}")
             nc.sync.dma_start(
-                out=both[:],
+                out=rel_half[b, h][:],
                 in_=rel[b * PASS : (b + 1) * PASS, h * HALF : (h + 1) * HALF].rearrange("(p t) j -> p t j", t=PACK),
             )
             for i in range(2):
-                rel_sb[b, 2 * h + i] = both[:, :, i * QUARTER : (i + 1) * QUARTER]
+                rel_sb[b, 2 * h + i] = rel_half[b, h][:, :, i * QUARTER : (i + 1) * QUARTER]
 
         load_rel(0, 0)
         load_rel(1, 0)
@@ -174,13 +173,7 @@ def tile_list_foundry_job_dispatch_kernel(
             for t in range(PACK):
                 melt_pass(b, h, t, 0, group[t])
 
-        def close_melt(b, h, group, first_pass):
-            if (b, h) == (1, 1):
-                neg_melt = w1_raw[1, 1][:].rearrange("p a (b j) -> p (a b) j", j=QUARTER).rearrange(
-                    "p (i t) j -> p i t j", t=PACK
-                )
-            else:
-                neg_melt = held([P, 2, PACK, QUARTER], F32, f"melt{b}{h}")
+        def close_melt(b, h, group, first_pass, neg_melt):
             for t in range(PACK):
                 for a in range(first_pass, 2):
                     melt_pass(b, h, t, a, group[t])
@@ -190,26 +183,27 @@ def tile_list_foundry_job_dispatch_kernel(
             for i in range(2):
                 later[b, 2 * h + i] = neg_melt[:, i]
 
+        def melt_room(b, h):
+            return held([P, 2, PACK, QUARTER], F32, f"melt{b}{h}")
+
         sums = held([P, 2 * S], F32, "sums")
         w1_bf = {}
         w1_w = {}
         w1_s = {}
 
         def w1_views(a, b):
-            if (a, b) == (1, 1):
-                w1_bf[a, b] = sums[:, HALF : 3 * HALF].bitcast(BF16).rearrange("p (t m j) -> p t m j", t=PACK, j=PACK)
-            else:
-                w1_bf[a, b] = rotating([P, PACK, P, PACK], BF16, "w1_bf", 2)
             return (
                 w1_bf[a, b][:].rearrange("p t m j -> p m t j"),
                 w1_raw[a, b][:].rearrange("p j (m t) -> p m t j", t=PACK),
             )
 
         def round_w1_on_vector(a, b):
+            w1_bf[a, b] = rotating([P, PACK, P, PACK], BF16, "w1_bf", 2)
             dst, src = w1_views(a, b)
             nc.vector.tensor_scalar(dst, src, -1.0, None, ALU.mult)
 
         def round_w1_on_scalar(a, b):
+            w1_bf[a, b] = sums[:, HALF : 3 * HALF].bitcast(BF16).rearrange("p (t m j) -> p t m j", t=PACK, j=PACK)
             dst, src = w1_views(a, b)
             nc.scalar.activation(out=dst, in_=src, func=COPY, scale=-1.0)
 
@@ -241,6 +235,7 @@ def tile_list_foundry_job_dispatch_kernel(
                 dst = later[b, q][:, 2 * pair : 2 * pair + 2, :]
                 nc.vector.tensor_tensor(dst, acc, dst, ALU.min)
 
+        h_pair = {}
         h_bf = {}
         h_w = {}
         h_s = {}
@@ -255,7 +250,9 @@ def tile_list_foundry_job_dispatch_kernel(
             )
 
         def add_rel_on_tensor(b, q, group, back_bank):
-            h_bf[b, q] = rotating([P, QUARTER, PACK], BF16, "h_bf", 4)
+            if b == 0:
+                h_pair[q] = held([P, 2, QUARTER, PACK], BF16, f"h_pair{q}")
+            h_bf[b, q] = h_pair[q][:, b]
             turned = []
             for jb in range(QUARTER // P):
                 acc = group[jb][:].rearrange("j (t p) -> j t p", t=PACK)
@@ -290,31 +287,26 @@ def tile_list_foundry_job_dispatch_kernel(
             )
 
         def quantise_h(b, q):
-            width = h_bf[b, q].shape[1]
-            h_w[b, q] = held([P, width], U32, f"h_w{b}{q}")
-            h_s[b, q] = held([P, width], U8, f"h_s{b}{q}")
+            h_w[b, q] = held([P, QUARTER], U32, f"h_w{b}{q}")
+            h_s[b, q] = held([P, QUARTER], U8, f"h_s{b}{q}")
             nc.vector.quantize_mx(
                 out=h_w[b, q][:].bitcast(FP8X4), scales=h_s[b, q][:], in_=h_bf[b, q][:].rearrange("p j t -> p (j t)")
             )
 
-        def store_page(n, width):
-            for c in range(0, S, width):
-                result = promised[n // 2][:, n % 2, c : c + width]
-                nc.vector.tensor_tensor(result, page[n][:, c : c + width], result, ALU.max)
-                nc.sync.dma_start(out=out[n * P : (n + 1) * P, c : c + width], in_=result)
-
-        def scatter(n, y, first, width):
-            nc.vector.tensor_tensor(
-                page[n][:].indirect(places[:, first // PER_COLUMN : (first + width) // PER_COLUMN]),
-                y,
-                gains[:, first : first + width],
-                ALU.mult,
+        def quantise_pair(q):
+            words = held([P, 2, QUARTER], U32, f"h_w{q}")
+            scales = held([P, 2, QUARTER], U8, f"h_s{q}")
+            nc.vector.quantize_mx(
+                out=words[:].rearrange("p b j -> p (b j)").bitcast(FP8X4),
+                scales=scales[:].rearrange("p b j -> p (b j)"),
+                in_=h_pair[q][:].rearrange("p b j t -> p (b j t)"),
             )
+            for b in range(2):
+                h_w[b, q] = words[:, b, :]
+                h_s[b, q] = scales[:, b, :]
 
-        def finish(q, blocks, bank):
-            width = h_w[0, q].shape[1]
-            first = q * QUARTER
-            acc = bank[:].rearrange("p (i j) -> p i j", j=width)[:, : len(blocks), :]
+        def multiply(q, blocks, bank):
+            acc = bank[:].rearrange("p (i j) -> p i j", j=QUARTER)[:, : len(blocks), :]
             for i, n in enumerate(blocks):
                 for b in (1, 0):
                     nc.tensor.matmul_mx(
@@ -327,52 +319,58 @@ def tile_list_foundry_job_dispatch_kernel(
                         stop=(b == 0),
                     )
             y_bank = rotating([P, HALF], F32, "y", 4)
-            y = y_bank[:].rearrange("p (i j) -> p i j", j=width)
+            y = y_bank[:].rearrange("p (i j) -> p i j", j=QUARTER)
             nc.scalar.activation(out=y[:, : len(blocks), :], in_=acc, func=COPY, scale=-1.0)
-            for i, n in enumerate(blocks):
-                if q < 3:
-                    scatter(n, y[:, i, :], first, width)
-                elif n < 3:
-                    scatter(n, y[:, i, :], first, width)
-                    store_page(n, S)
-                else:
-                    for c in range(0, width, width // 2):
-                        scatter(n, y[:, i, c : c + width // 2], first + c, width // 2)
-                    store_page(n, S // 4)
+            return [y[:, i, :] for i in range(len(blocks))]
+
+        def scatter(n, y, first, width):
+            nc.vector.tensor_tensor(
+                page[n][:].indirect(places[:, first // PER_COLUMN : (first + width) // PER_COLUMN]),
+                y,
+                gains[:, first : first + width],
+                ALU.mult,
+            )
+
+        def finish(q, blocks, bank):
+            for n, y in zip(blocks, multiply(q, blocks, bank)):
+                scatter(n, y, q * QUARTER, QUARTER)
 
         low, high = banks[:4], banks[4:]
         for h, group in enumerate((low, high)):
             open_melt(0, h, group)
         for h, group in enumerate((low, high)):
-            close_melt(0, h, group, 1)
+            close_melt(0, h, group, 1, melt_room(0, h))
         for a in range(2):
             round_w1_on_vector(a, 0)
             quantise_w1(a, 0)
         round_w1_on_vector(0, 1)
-        close_melt(1, 0, low, 0)
+        close_melt(1, 0, low, 0, melt_room(1, 0))
         round_w1_on_scalar(1, 1)
-        close_melt(1, 1, high, 0)
+        close_melt(1, 1, high, 0, w1_raw[1, 1][:].rearrange("p (i u) (v j) -> p i (u v) j", i=2, j=QUARTER))
         mould_and_min(0, 0, low[:2])
         quantise_w1(0, 1)
         mould_and_min(0, 1, low[2:])
         quantise_w1(1, 1)
+
         mould_and_min(0, 2, low[:2])
         mould_and_min(0, 3, low[2:])
-        add_rel_on_gpsimd(0, 0)
-        add_rel_on_gpsimd(0, 1)
+        for q in range(2):
+            add_rel_on_gpsimd(0, q)
         mould_and_min(1, 0, low[:2])
         mould_and_min(1, 1, low[2:])
         mould_and_min(1, 2, high[:2])
         mould_and_min(1, 3, high[2:])
-        add_rel_on_vector(1, 0)
-        quantise_h(0, 0)
-        quantise_h(1, 0)
-        add_rel_on_vector(1, 1)
-        quantise_h(0, 1)
-        quantise_h(1, 1)
+        for q in range(2):
+            add_rel_on_vector(1, q)
+            for b in range(2):
+                quantise_h(b, q)
+
         add_rel_on_tensor(0, 2, low[:2], high[2])
         finish(0, (0,), high[0])
         finish(0, (1,), high[1])
+        finish(0, (2, 3), low[2])
+        finish(1, (0, 1), low[3])
+
         promised = []
         for pair in range(2):
             both = rotating([P, 2, S], F32, "raw", 4)
@@ -380,20 +378,29 @@ def tile_list_foundry_job_dispatch_kernel(
                 out=both[:], in_=x0[2 * pair * P : 2 * (pair + 1) * P, :].rearrange("(i p) m -> p i m", p=P)
             )
             promised.append(both)
-        add_rel_on_tensor(1, 2, high[:2], high[3])
-        finish(0, (2,), low[2])
-        finish(0, (3,), low[3])
-        add_rel_on_tensor(0, 3, low[2:], high[0])
-        finish(1, (0,), low[0])
-        finish(1, (1,), low[1])
-        add_rel_on_tensor(1, 3, low[:2], high[1])
-        finish(1, (2,), high[2])
-        quantise_h(0, 2)
-        quantise_h(1, 2)
-        finish(1, (3,), high[3])
-        quantise_h(0, 3)
-        quantise_h(1, 3)
+
+        add_rel_on_tensor(1, 2, low[2:], high[0])
+        quantise_pair(2)
+        finish(1, (2, 3), high[0])
+        add_rel_on_tensor(0, 3, low[2:], high[1])
+        add_rel_on_tensor(1, 3, low[2:], high[2])
         finish(2, (0, 1), high[1])
-        finish(2, (2, 3), high[0])
-        finish(3, (0, 1), low[2])
-        finish(3, (2, 3), low[3])
+        quantise_pair(3)
+        finish(2, (2, 3), high[2])
+
+        def store_page(n, width):
+            for c in range(0, S, width):
+                result = promised[n // 2][:, n % 2, c : c + width]
+                nc.vector.tensor_tensor(result, page[n][:, c : c + width], result, ALU.max)
+                nc.sync.dma_start(out=out[n * P : (n + 1) * P, c : c + width], in_=result)
+
+        last = 3 * QUARTER
+        for n, y in zip((0, 1), multiply(3, (0, 1), low[0])):
+            scatter(n, y, last, QUARTER)
+            store_page(n, S)
+        y_third, y_fourth = multiply(3, (2, 3), low[1])
+        scatter(2, y_third, last, QUARTER)
+        store_page(2, S)
+        for c in range(0, QUARTER, QUARTER // 2):
+            scatter(3, y_fourth[:, c : c + QUARTER // 2], last + c, QUARTER // 2)
+        store_page(3, S // LAST_PIECES)

@@ -27,7 +27,7 @@ PER_COLUMN = 16
 SCALE_ROWS = 16
 LANDING = 64 - SCALE_ROWS
 RUN = 2
-TABLE_PIECES = 2
+FIRST_PIECE = (T // 2, T // 4)
 LAST_PIECES = 4
 
 
@@ -78,7 +78,7 @@ def tile_list_foundry_job_dispatch_kernel(
 
         def load_table(a, piece):
             words = tab_words[a].rearrange("p t i -> p (t i)").bitcast(I32)
-            cols = slice(piece * T // TABLE_PIECES, (piece + 1) * T // TABLE_PIECES)
+            cols = (slice(0, FIRST_PIECE[a]), slice(FIRST_PIECE[a], T))[piece]
             nc.sync.dma_start(out=tab_w[a][:, cols], in_=words[:, cols])
 
         load_table(0, 0)
@@ -365,11 +365,11 @@ def tile_list_foundry_job_dispatch_kernel(
             for b in range(2):
                 quantise_h(b, q)
 
-        add_rel_on_tensor(0, 2, low[:2], high[2])
         finish(0, (0,), high[0])
         finish(0, (1,), high[1])
         finish(0, (2, 3), low[2])
         finish(1, (0, 1), low[3])
+        add_rel_on_tensor(0, 2, low[:2], high[1])
 
         promised = []
         for pair in range(2):
@@ -383,10 +383,11 @@ def tile_list_foundry_job_dispatch_kernel(
         quantise_pair(2)
         finish(1, (2, 3), high[0])
         add_rel_on_tensor(0, 3, low[2:], high[1])
+        finish(2, (0,), low[2])
+        finish(2, (1, 2), low[3])
         add_rel_on_tensor(1, 3, low[2:], high[2])
-        finish(2, (0, 1), high[1])
         quantise_pair(3)
-        finish(2, (2, 3), high[2])
+        finish(2, (3,), high[2])
 
         def store_page(n, width):
             for c in range(0, S, width):
@@ -395,10 +396,10 @@ def tile_list_foundry_job_dispatch_kernel(
                 nc.sync.dma_start(out=out[n * P : (n + 1) * P, c : c + width], in_=result)
 
         last = 3 * QUARTER
-        for n, y in zip((0, 1), multiply(3, (0, 1), low[0])):
-            scatter(n, y, last, QUARTER)
+        for n in range(2):
+            finish(3, (n,), low[n])
             store_page(n, S)
-        y_third, y_fourth = multiply(3, (2, 3), low[1])
+        y_third, y_fourth = multiply(3, (2, 3), high[3])
         scatter(2, y_third, last, QUARTER)
         store_page(2, S)
         for c in range(0, QUARTER, QUARTER // 2):

@@ -26,6 +26,8 @@ QUARTER = S // 4
 PER_COLUMN = 16
 SCALE_ROWS = 16
 LANDING = 64 - SCALE_ROWS
+LINE = 8
+SPLIT = 80
 RUN = 2
 FIRST_PIECE = (T // 2, T // 4)
 LAST_PIECES = 4
@@ -53,8 +55,8 @@ def tile_list_foundry_job_dispatch_kernel(
         v_w = [held([P, S], U32, f"v_w{a}") for a in range(2)]
         picked_s = held([P, S], U8, "picked_s")
         v_s = held([P, 2, S], U8, "v_s")
-        w4_raw = held([P, 2, 2 * H], U8, "w4_raw")
-        w4_w = held([P, 2, 2 * H], U8, "w4_w")
+        w4_raw = [held([P, 2, 2 * PASS], U8, f"w4_raw{b}") for b in range(2)]
+        w4_w = [held([P, 2, 2 * PASS], U8, f"w4_w{b}") for b in range(2)]
         w4_sraw = held([P, 2, H], U8, "w4_sraw")
         w4_s = held([P, 2, H], U8, "w4_s")
         w8_w = held([P, 2, N], I32, "w8_w")
@@ -83,7 +85,12 @@ def tile_list_foundry_job_dispatch_kernel(
 
         load_table(0, 0)
         load_table(0, 1)
-        nc.sync.dma_start(out=w4_raw[:].bitcast(I32), in_=w4_words.rearrange("a p c -> p a c").bitcast(I32))
+
+        def load_w4(b):
+            words = w4_words[:, :, 2 * b * PASS : 2 * (b + 1) * PASS].rearrange("a p c -> p a c")
+            nc.sync.dma_start(out=w4_raw[b][:].bitcast(I32), in_=words.bitcast(I32))
+
+        load_w4(0)
         for g in range(QUADRANTS):
             nc.scalar.dma_start(
                 out=w4_sraw[32 * g : 32 * g + 4, :, :].bitcast(I32),
@@ -101,17 +108,26 @@ def tile_list_foundry_job_dispatch_kernel(
         load_table(1, 0)
         move_plane(0)
         load_table(1, 1)
+        load_w4(1)
 
-        w1_raw = {(a, b): rotating([P, PACK, PASS], F32, "raw", 4) for b in range(2) for a in range(2)}
+        raw = [rotating([P, 2, PACK, PASS // 2], F32, "raw", 3) for part in range(3)]
+        third_melt = held([P, PACK, 2, QUARTER], F32, "third_melt")
+        w1_raw = {(a, a // 2, u): raw[a][:, u] for a in range(2) for u in range(2)}
+        w1_raw[0, 1, 0] = held([P, PACK, PASS // 2], F32, "w1_raw010")[:]
+        w1_raw[0, 1, 1] = third_melt[:, 2:].rearrange("p t i j -> p (t i) j")
+        for u in range(2):
+            w1_raw[1, 1, u] = raw[2][:, u]
 
-        def w1_rows(a, b):
-            return w1[a * PASS : (a + 1) * PASS, b * PASS : (b + 1) * PASS].rearrange("(p j) c -> p j c", j=PACK)
+        def load_w1(a, b, u):
+            first = b * PASS + u * PASS // 2
+            rows = w1[a * PASS : (a + 1) * PASS, first : first + PASS // 2].rearrange("(p j) c -> p j c", j=PACK)
+            nc.sync.dma_start(out=w1_raw[a, b, u], in_=rows)
 
-        nc.sync.dma_start(out=w1_raw[0, 0][:, :2, :], in_=w1_rows(0, 0)[:, :2, :])
         move_plane(1)
-        nc.sync.dma_start(out=w1_raw[0, 0][:, 2:, :], in_=w1_rows(0, 0)[:, 2:, :])
-        for a, b in ((1, 0), (0, 1), (1, 1)):
-            nc.sync.dma_start(out=w1_raw[a, b][:], in_=w1_rows(a, b))
+        for b in range(2):
+            for a in range(2):
+                for u in range(2):
+                    load_w1(a, b, u)
 
         rel_sb = {}
         rel_half = {}
@@ -138,85 +154,109 @@ def tile_list_foundry_job_dispatch_kernel(
         load_rel(1, 1)
 
         nc.vector.tensor_copy(v_w[0][:], tab_w[0][:].bitcast(U32).indirect(picks[:]))
-        nc.vector.tensor_copy(
-            w4_w[:].bitcast(U16).rearrange("p a (b t m) -> p (a b) t m", t=PACK, m=P),
-            w4_raw[:].bitcast(U16).rearrange("p a (b m t) -> p (a b) t m", t=PACK, m=P),
+
+        def order_w4(b):
+            nc.vector.tensor_copy(
+                w4_w[b][:].bitcast(U16).rearrange("p a (t m) -> p a t m", t=PACK),
+                w4_raw[b][:].bitcast(U16).rearrange("p a (m t) -> p a t m", t=PACK),
+            )
+
+        order_w4(0)
+        nc.scalar.copy(
+            out=w4_w[1][:].bitcast(U16).rearrange("p a (t c i) -> p a c t i", t=PACK, i=LINE),
+            in_=w4_raw[1][:].bitcast(U16).rearrange("p a (c i t) -> p a c t i", t=PACK, i=LINE),
         )
         nc.vector.tensor_copy(
             w4_s[:].rearrange("p a (b t m) -> p (a b) t m", t=PACK, m=P),
             w4_sraw[:].rearrange("p a (b m t) -> p (a b) t m", t=PACK, m=P),
         )
-        for h in range(2):
+        for q in range(4):
             nc.vector.tensor_copy(
-                v_w[1][:, h * HALF : (h + 1) * HALF],
-                tab_w[1][:].bitcast(U32).indirect(picks[:, h * HALF // PER_COLUMN : (h + 1) * HALF // PER_COLUMN]),
+                v_w[1][:, q * QUARTER : (q + 1) * QUARTER],
+                tab_w[1][:].bitcast(U32).indirect(picks[:, q * QUARTER // PER_COLUMN : (q + 1) * QUARTER // PER_COLUMN]),
             )
 
         banks = [psum.tile([P, HALF], F32, name=f"bank{i}") for i in range(8)]
 
         later = {}
 
-        def melt_pass(b, h, t, a, acc):
-            cols = slice(h * HALF, (h + 1) * HALF)
+        def melt_pass(b, h, t, a, acc, first=0, width=HALF):
+            cols = slice(h * HALF + first, h * HALF + first + width)
             c0 = b * PASS + t * P
             nc.tensor.matmul_mx(
-                out=acc[:],
-                lhsT=w4_w[:, a, 2 * c0 : 2 * (c0 + P)].bitcast(FP4X4),
+                out=acc[:, first : first + width],
+                lhsT=w4_w[b][:, a, 2 * t * P : 2 * (t + 1) * P].bitcast(FP4X4),
                 lhsT_scale=w4_s[:, a, c0 : c0 + P],
                 rhs=v_w[a][:, cols].bitcast(FP8X4),
                 rhs_scale=v_s[:, a, cols],
                 start=(a == 0),
-                stop=(a == 1),
+                stop=(a == 1 and first + width == HALF),
             )
 
         def open_melt(b, h, group):
             for t in range(PACK):
                 melt_pass(b, h, t, 0, group[t])
 
-        def close_melt(b, h, group, first_pass, neg_melt):
-            for t in range(PACK):
-                for a in range(first_pass, 2):
-                    melt_pass(b, h, t, a, group[t])
-                nc.scalar.activation(
-                    out=neg_melt[:, :, t, :], in_=group[t][:].rearrange("p (i j) -> p i j", i=2), func=COPY, scale=-1.0
-                )
+        def melt_bank(b, h, t, bank, neg_melt):
+            for a in range(2):
+                melt_pass(b, h, t, a, bank)
+            copy_melt(b, h, t, bank, neg_melt)
+
+        def copy_melt(b, h, t, bank, neg_melt):
+            nc.scalar.activation(
+                out=neg_melt[:, :, t, :], in_=bank[:].rearrange("p (i j) -> p i j", i=2), func=COPY, scale=-1.0
+            )
             for i in range(2):
                 later[b, 2 * h + i] = neg_melt[:, i]
+
+        def close_melt(b, h, group, neg_melt):
+            for t in range(PACK):
+                melt_pass(b, h, t, 1, group[t], 0, QUARTER)
+            for t in range(PACK):
+                melt_pass(b, h, t, 1, group[t], QUARTER, QUARTER)
+                copy_melt(b, h, t, group[t], neg_melt)
 
         def melt_room(b, h):
             return held([P, 2, PACK, QUARTER], F32, f"melt{b}{h}")
 
         sums = held([P, 2 * S], F32, "sums")
+        first_melts = [rotating([P, 2, PACK, QUARTER], F32, "early", 1), melt_room(0, 1)]
         w1_bf = {}
         w1_w = {}
         w1_s = {}
 
-        def w1_views(a, b):
+        def w1_views(a, b, first, last):
+            u = first // (P // 2)
             return (
-                w1_bf[a, b][:].rearrange("p t m j -> p m t j"),
-                w1_raw[a, b][:].rearrange("p j (m t) -> p m t j", t=PACK),
+                w1_bf[a, b][:, :, first:last, :].rearrange("p t m j -> p m t j"),
+                w1_raw[a, b, u].rearrange("p j (m t) -> p m t j", t=PACK)[:, first - u * P // 2 : last - u * P // 2],
             )
 
-        def round_w1_on_vector(a, b):
+        for a, b in ((0, 0), (1, 0), (0, 1)):
             w1_bf[a, b] = rotating([P, PACK, P, PACK], BF16, "w1_bf", 2)
-            dst, src = w1_views(a, b)
+        w1_bf[1, 1] = sums[:, QUARTER : QUARTER + S].bitcast(BF16).rearrange("p (t m j) -> p t m j", t=PACK, j=PACK)
+
+        def round_w1_on_vector(a, b, first, last):
+            dst, src = w1_views(a, b, first, last)
             nc.vector.tensor_scalar(dst, src, -1.0, None, ALU.mult)
 
-        def round_w1_on_scalar(a, b):
-            w1_bf[a, b] = sums[:, HALF : 3 * HALF].bitcast(BF16).rearrange("p (t m j) -> p t m j", t=PACK, j=PACK)
-            dst, src = w1_views(a, b)
+        def round_w1_on_scalar(a, b, first, last):
+            dst, src = w1_views(a, b, first, last)
             nc.scalar.activation(out=dst, in_=src, func=COPY, scale=-1.0)
 
-        def quantise_w1(a, b):
+        def quantise_w1(a, b, pieces=1):
             w1_w[a, b] = held([P, PASS], U32, f"w1_w{a}{b}")
             w1_s[a, b] = held([P, PASS], U8, f"w1_s{a}{b}")
-            nc.vector.quantize_mx(
-                out=w1_w[a, b][:].bitcast(FP8X4),
-                scales=w1_s[a, b][:],
-                in_=w1_bf[a, b][:].rearrange("p t m j -> p (t m j)"),
-            )
+            count = PACK // pieces
+            for first in range(0, PACK, count):
+                cols = slice(first * P, (first + count) * P)
+                nc.vector.quantize_mx(
+                    out=w1_w[a, b][:, cols].bitcast(FP8X4),
+                    scales=w1_s[a, b][:, cols],
+                    in_=w1_bf[a, b][:, first : first + count].rearrange("p t m j -> p (t m j)"),
+                )
 
-        def mould_and_min(b, q, group):
+        def mould_and_min(b, q, group, room=None):
             cols = slice(q * QUARTER, (q + 1) * QUARTER)
             for pair in range(2):
                 acc = group[pair][:].rearrange("p (i j) -> p i j", i=2)
@@ -232,16 +272,19 @@ def tile_list_foundry_job_dispatch_kernel(
                             start=(a == 0),
                             stop=(a == 1),
                         )
-                dst = later[b, q][:, 2 * pair : 2 * pair + 2, :]
-                nc.vector.tensor_tensor(dst, acc, dst, ALU.min)
+                pair_t = slice(2 * pair, 2 * pair + 2)
+                dst = later[b, q] if room is None else room
+                nc.vector.tensor_tensor(dst[:, pair_t, :], acc, later[b, q][:, pair_t, :], ALU.min)
+            if room is not None:
+                later[b, q] = room
 
         h_pair = {}
         h_bf = {}
         h_w = {}
         h_s = {}
 
-        def add_rel_on_vector(b, q):
-            h_bf[b, q] = rel_half[0, 0][:, q, :].bitcast(BF16).rearrange("p (j t) -> p j t", t=PACK)
+        def add_rel_on_vector(b, q, room):
+            h_bf[b, q] = room
             nc.vector.tensor_tensor(
                 h_bf[b, q][:].rearrange("p (c i) t -> p c t i", i=RUN),
                 later[b, q].rearrange("p t (c i) -> p c t i", i=RUN),
@@ -278,7 +321,7 @@ def tile_list_foundry_job_dispatch_kernel(
             )
 
         def add_rel_on_gpsimd(b, q):
-            total = sums[:, q * S : (q + 1) * S].rearrange("p (t j) -> p t j", t=PACK)
+            total = (sums[:, S:].rearrange("p (t j) -> p t j", t=PACK), first_melts[1][:, 1])[q]
             nc.gpsimd.tensor_tensor(total, later[b, q], rel_sb[b, q], ALU.add)
             h_bf[b, q] = held([P, QUARTER, PACK], BF16, f"h_first{b}{q}")
             nc.scalar.copy(
@@ -287,7 +330,7 @@ def tile_list_foundry_job_dispatch_kernel(
             )
 
         def quantise_h(b, q):
-            h_w[b, q] = held([P, QUARTER], U32, f"h_w{b}{q}")
+            h_w[b, q] = early_words[:, 2 * q + b, :]
             h_s[b, q] = held([P, QUARTER], U8, f"h_s{b}{q}")
             nc.vector.quantize_mx(
                 out=h_w[b, q][:].bitcast(FP8X4), scales=h_s[b, q][:], in_=h_bf[b, q][:].rearrange("p j t -> p (j t)")
@@ -339,31 +382,44 @@ def tile_list_foundry_job_dispatch_kernel(
         for h, group in enumerate((low, high)):
             open_melt(0, h, group)
         for h, group in enumerate((low, high)):
-            close_melt(0, h, group, 1, melt_room(0, h))
+            close_melt(0, h, group, first_melts[h])
         for a in range(2):
-            round_w1_on_vector(a, 0)
+            for u in range(2):
+                round_w1_on_vector(a, 0, u * P // 2, (u + 1) * P // 2)
             quantise_w1(a, 0)
-        round_w1_on_vector(0, 1)
-        close_melt(1, 0, low, 0, melt_room(1, 0))
-        round_w1_on_scalar(1, 1)
-        close_melt(1, 1, high, 0, w1_raw[1, 1][:].rearrange("p (i u) (v j) -> p i (u v) j", i=2, j=QUARTER))
-        mould_and_min(0, 0, low[:2])
+        round_w1_on_vector(0, 1, 0, P // 2)
+        round_w1_on_vector(0, 1, P // 2, SPLIT)
+        third, last_melt = third_melt[:].rearrange("p t i j -> p i t j"), raw[2][:]
+        for t in range(2):
+            melt_bank(1, 0, t, low[t], third)
+        round_w1_on_scalar(0, 1, SPLIT, P)
+        for u in range(2):
+            round_w1_on_scalar(1, 1, u * P // 2, (u + 1) * P // 2)
+        mould_and_min(0, 0, (high[3], low[0]))
+        for t in range(2, PACK):
+            melt_bank(1, 0, t, low[t], third)
+        for t in range(3):
+            melt_bank(1, 1, t, high[t], last_melt)
         quantise_w1(0, 1)
-        mould_and_min(0, 1, low[2:])
-        quantise_w1(1, 1)
+        quantise_w1(1, 1, 2)
+        mould_and_min(0, 1, (low[1], high[3]))
 
-        mould_and_min(0, 2, low[:2])
-        mould_and_min(0, 3, low[2:])
+        mould_and_min(0, 2, (low[0], low[1]))
+        mould_and_min(0, 3, (high[3], low[0]), sums[:, :S].rearrange("p (t j) -> p t j", t=PACK))
         for q in range(2):
             add_rel_on_gpsimd(0, q)
-        mould_and_min(1, 0, low[:2])
-        mould_and_min(1, 1, low[2:])
+        mould_and_min(1, 0, low[2:])
+        melt_bank(1, 1, 3, low[1], last_melt)
+        mould_and_min(1, 1, (high[3], low[0]))
         mould_and_min(1, 2, high[:2])
-        mould_and_min(1, 3, high[2:])
-        for q in range(2):
-            add_rel_on_vector(1, q)
-            for b in range(2):
-                quantise_h(b, q)
+        mould_and_min(1, 3, (high[2], high[3]))
+        early_words = rotating([P, 4, QUARTER], U32, "early", 1)
+        add_rel_on_vector(1, 0, rel_half[0, 0][:, 0, :].bitcast(BF16).rearrange("p (j t) -> p j t", t=PACK))
+        for b in range(2):
+            quantise_h(b, 0)
+        add_rel_on_vector(1, 1, h_bf[0, 0])
+        for b in range(2):
+            quantise_h(b, 1)
 
         finish(0, (0,), high[0])
         finish(0, (1,), high[1])
@@ -373,7 +429,7 @@ def tile_list_foundry_job_dispatch_kernel(
 
         promised = []
         for pair in range(2):
-            both = rotating([P, 2, S], F32, "raw", 4)
+            both = rotating([P, 2, S], F32, "raw", 3)
             nc.sync.dma_start(
                 out=both[:], in_=x0[2 * pair * P : 2 * (pair + 1) * P, :].rearrange("(i p) m -> p i m", p=P)
             )

@@ -27,7 +27,6 @@ PER_COLUMN = 16
 SCALE_ROWS = 16
 LANDING = 64 - SCALE_ROWS
 LINE = 8
-SPLIT = 80
 RUN = 2
 FIRST_PIECE = (T // 2, T // 4)
 LAST_PIECES = 4
@@ -50,7 +49,7 @@ def tile_list_foundry_job_dispatch_kernel(
 
         picks = keep.tile([P, S // PER_COLUMN], U16, name="picks")
         places = keep.tile([P, S // PER_COLUMN], U16, name="places")
-        tab_w = [held([P, T], I32, f"tab_w{a}") for a in range(2)]
+        tab_w = [rotating([P, T], I32, f"tab_w{a}", 1) for a in range(2)]
         tab_s = held([P, T], U8, "tab_s")
         v_w = [held([P, S], U32, f"v_w{a}") for a in range(2)]
         picked_s = held([P, S], U8, "picked_s")
@@ -83,14 +82,14 @@ def tile_list_foundry_job_dispatch_kernel(
             cols = (slice(0, FIRST_PIECE[a]), slice(FIRST_PIECE[a], T))[piece]
             nc.sync.dma_start(out=tab_w[a][:, cols], in_=words[:, cols])
 
-        load_table(0, 0)
-        load_table(0, 1)
 
         def load_w4(b):
             words = w4_words[:, :, 2 * b * PASS : 2 * (b + 1) * PASS].rearrange("a p c -> p a c")
             nc.sync.dma_start(out=w4_raw[b][:].bitcast(I32), in_=words.bitcast(I32))
 
+        load_table(0, 0)
         load_w4(0)
+        load_table(0, 1)
         for g in range(QUADRANTS):
             nc.scalar.dma_start(
                 out=w4_sraw[32 * g : 32 * g + 4, :, :].bitcast(I32),
@@ -110,13 +109,11 @@ def tile_list_foundry_job_dispatch_kernel(
         load_table(1, 1)
         load_w4(1)
 
-        raw = [rotating([P, 2, PACK, PASS // 2], F32, "raw", 3) for part in range(3)]
-        third_melt = held([P, PACK, 2, QUARTER], F32, "third_melt")
-        w1_raw = {(a, a // 2, u): raw[a][:, u] for a in range(2) for u in range(2)}
-        w1_raw[0, 1, 0] = held([P, PACK, PASS // 2], F32, "w1_raw010")[:]
-        w1_raw[0, 1, 1] = third_melt[:, 2:].rearrange("p t i j -> p (t i) j")
+        raw = [rotating([P, 2, PACK, PASS // 2], F32, "raw", 2) for a in range(2)]
+        w1_raw = {(a, 0, u): raw[a][:, u] for a in range(2) for u in range(2)}
         for u in range(2):
-            w1_raw[1, 1, u] = raw[2][:, u]
+            w1_raw[0, 1, u] = held([P, PACK, PASS // 2], F32, f"w1_raw01{u}")[:]
+            w1_raw[1, 1, u] = rotating([P, PACK, PASS // 2], F32, f"last{u}", 1)[:]
 
         def load_w1(a, b, u):
             first = b * PASS + u * PASS // 2
@@ -153,7 +150,11 @@ def tile_list_foundry_job_dispatch_kernel(
         nc.sync.dma_start(out=gains[:], in_=wgo)
         load_rel(1, 1)
 
-        nc.vector.tensor_copy(v_w[0][:], tab_w[0][:].bitcast(U32).indirect(picks[:]))
+        for h in range(2):
+            nc.vector.tensor_copy(
+                v_w[0][:, h * HALF : (h + 1) * HALF],
+                tab_w[0][:].bitcast(U32).indirect(picks[:, h * HALF // PER_COLUMN : (h + 1) * HALF // PER_COLUMN]),
+            )
 
         def order_w4(b):
             nc.vector.tensor_copy(
@@ -197,14 +198,17 @@ def tile_list_foundry_job_dispatch_kernel(
             for t in range(PACK):
                 melt_pass(b, h, t, 0, group[t])
 
-        def melt_bank(b, h, t, bank, neg_melt):
+        def melt_bank(b, h, t, bank, neg_melt, room=None):
             for a in range(2):
                 melt_pass(b, h, t, a, bank)
-            copy_melt(b, h, t, bank, neg_melt)
+            copy_melt(b, h, t, bank, neg_melt, room)
 
-        def copy_melt(b, h, t, bank, neg_melt):
+        def copy_melt(b, h, t, bank, neg_melt, room=None):
             nc.scalar.activation(
-                out=neg_melt[:, :, t, :], in_=bank[:].rearrange("p (i j) -> p i j", i=2), func=COPY, scale=-1.0
+                out=neg_melt[:, :, t, :] if room is None else room,
+                in_=bank[:].rearrange("p (i j) -> p i j", i=2),
+                func=COPY,
+                scale=-1.0,
             )
             for i in range(2):
                 later[b, 2 * h + i] = neg_melt[:, i]
@@ -220,7 +224,7 @@ def tile_list_foundry_job_dispatch_kernel(
             return held([P, 2, PACK, QUARTER], F32, f"melt{b}{h}")
 
         sums = held([P, 2 * S], F32, "sums")
-        first_melts = [rotating([P, 2, PACK, QUARTER], F32, "early", 1), melt_room(0, 1)]
+        first_melts = [rotating([P, 2, PACK, QUARTER], F32, "first_melt", 1), melt_room(0, 1)]
         w1_bf = {}
         w1_w = {}
         w1_s = {}
@@ -232,8 +236,9 @@ def tile_list_foundry_job_dispatch_kernel(
                 w1_raw[a, b, u].rearrange("p j (m t) -> p m t j", t=PACK)[:, first - u * P // 2 : last - u * P // 2],
             )
 
-        for a, b in ((0, 0), (1, 0), (0, 1)):
-            w1_bf[a, b] = rotating([P, PACK, P, PACK], BF16, "w1_bf", 2)
+        w1_bf[0, 0] = held([P, PACK, P, PACK], BF16, "w1_bf_first")
+        for a, b in ((1, 0), (0, 1)):
+            w1_bf[a, b] = rotating([P, PACK, P, PACK], BF16, "w1_bf", 1)
         w1_bf[1, 1] = sums[:, QUARTER : QUARTER + S].bitcast(BF16).rearrange("p (t m j) -> p t m j", t=PACK, j=PACK)
 
         def round_w1_on_vector(a, b, first, last):
@@ -245,7 +250,7 @@ def tile_list_foundry_job_dispatch_kernel(
             nc.scalar.activation(out=dst, in_=src, func=COPY, scale=-1.0)
 
         def quantise_w1(a, b, pieces=1):
-            w1_w[a, b] = held([P, PASS], U32, f"w1_w{a}{b}")
+            w1_w[a, b] = late_words[:, a, :] if b == 1 else held([P, PASS], U32, f"w1_w{a}{b}")
             w1_s[a, b] = held([P, PASS], U8, f"w1_s{a}{b}")
             count = PACK // pieces
             for first in range(0, PACK, count):
@@ -256,25 +261,26 @@ def tile_list_foundry_job_dispatch_kernel(
                     in_=w1_bf[a, b][:, first : first + count].rearrange("p t m j -> p (t m j)"),
                 )
 
-        def mould_and_min(b, q, group, room=None):
+        def mould_and_min(b, q, group, room=None, upper=None):
             cols = slice(q * QUARTER, (q + 1) * QUARTER)
             for pair in range(2):
                 acc = group[pair][:].rearrange("p (i j) -> p i j", i=2)
                 for i in range(2):
                     t = 2 * pair + i
-                    for a in range(2):
+                    for a in (1, 0):
                         nc.tensor.matmul_mx(
                             out=acc[:, i, :],
                             lhsT=w1_w[a, b][:, t * P : (t + 1) * P].bitcast(FP8X4),
                             lhsT_scale=w1_s[a, b][:, t * P : (t + 1) * P],
                             rhs=v_w[a][:, cols].bitcast(FP8X4),
                             rhs_scale=v_s[:, a, cols],
-                            start=(a == 0),
-                            stop=(a == 1),
+                            start=(a == 1),
+                            stop=(a == 0),
                         )
                 pair_t = slice(2 * pair, 2 * pair + 2)
                 dst = later[b, q] if room is None else room
-                nc.vector.tensor_tensor(dst[:, pair_t, :], acc, later[b, q][:, pair_t, :], ALU.min)
+                src = upper if pair == 1 and upper is not None else later[b, q][:, pair_t, :]
+                nc.vector.tensor_tensor(dst[:, pair_t, :], acc, src, ALU.min)
             if room is not None:
                 later[b, q] = room
 
@@ -386,35 +392,44 @@ def tile_list_foundry_job_dispatch_kernel(
         for a in range(2):
             for u in range(2):
                 round_w1_on_vector(a, 0, u * P // 2, (u + 1) * P // 2)
-            quantise_w1(a, 0)
-        round_w1_on_vector(0, 1, 0, P // 2)
-        round_w1_on_vector(0, 1, P // 2, SPLIT)
-        third, last_melt = third_melt[:].rearrange("p t i j -> p i t j"), raw[2][:]
+            quantise_w1(a, 0, 1 + a)
+        for a, u in ((0, 0), (0, 1), (1, 0)):
+            nc.gpsimd.tensor_scalar(
+                w1_bf[a, 1][:, :, u * P // 2 : (u + 1) * P // 2, :],
+                w1_raw[a, 1, u].rearrange("p j (m t) -> p t m j", t=PACK),
+                -1.0,
+                0.0,
+                ALU.mult,
+                ALU.add,
+            )
+        third = rotating([P, 2, PACK, QUARTER], F32, "early", 1)
+        for t in range(PACK):
+            melt_bank(1, 0, t, low[t], third)
+        round_w1_on_scalar(1, 1, P // 2, P)
+        mould_and_min(0, 2, high[2:])
+        last_melt = rotating([P, 2, PACK, QUARTER], F32, "last1", 1)
         for t in range(2):
-            melt_bank(1, 0, t, low[t], third)
-        round_w1_on_scalar(0, 1, SPLIT, P)
-        for u in range(2):
-            round_w1_on_scalar(1, 1, u * P // 2, (u + 1) * P // 2)
-        mould_and_min(0, 0, (high[3], low[0]))
-        for t in range(2, PACK):
-            melt_bank(1, 0, t, low[t], third)
-        for t in range(3):
             melt_bank(1, 1, t, high[t], last_melt)
+        first_minima = rotating([P, 2, PACK, QUARTER], F32, "tab_w0", 1)
+        mould_and_min(0, 0, low[:2], first_minima[:, 0])
+
+        mould_and_min(0, 1, low[2:], first_minima[:, 1])
+        late_words = rotating([P, 2, PASS], U32, "first_melt", 1)
         quantise_w1(0, 1)
         quantise_w1(1, 1, 2)
-        mould_and_min(0, 1, (low[1], high[3]))
-
-        mould_and_min(0, 2, (low[0], low[1]))
-        mould_and_min(0, 3, (high[3], low[0]), sums[:, :S].rearrange("p (t j) -> p t j", t=PACK))
+        mould_and_min(0, 3, high[2:], sums[:, :S].rearrange("p (t j) -> p t j", t=PACK))
+        for t in range(2, PACK):
+            melt_bank(1, 1, t, low[t - 2], last_melt)
         for q in range(2):
             add_rel_on_gpsimd(0, q)
         mould_and_min(1, 0, low[2:])
-        melt_bank(1, 1, 3, low[1], last_melt)
-        mould_and_min(1, 1, (high[3], low[0]))
+        mould_and_min(1, 1, high[2:], w1_raw[0, 1, 0])
         mould_and_min(1, 2, high[:2])
-        mould_and_min(1, 3, (high[2], high[3]))
+        mould_and_min(1, 3, low[:2], w1_raw[0, 1, 1])
+        add_rel_on_vector(
+            1, 0, last_melt[:, 1, :2, :].rearrange("p t j -> p (t j)").bitcast(BF16).rearrange("p (j t) -> p j t", t=PACK)
+        )
         early_words = rotating([P, 4, QUARTER], U32, "early", 1)
-        add_rel_on_vector(1, 0, rel_half[0, 0][:, 0, :].bitcast(BF16).rearrange("p (j t) -> p j t", t=PACK))
         for b in range(2):
             quantise_h(b, 0)
         add_rel_on_vector(1, 1, h_bf[0, 0])
@@ -425,11 +440,11 @@ def tile_list_foundry_job_dispatch_kernel(
         finish(0, (1,), high[1])
         finish(0, (2, 3), low[2])
         finish(1, (0, 1), low[3])
-        add_rel_on_tensor(0, 2, low[:2], high[1])
+        add_rel_on_tensor(0, 2, high[2:], high[1])
 
         promised = []
         for pair in range(2):
-            both = rotating([P, 2, S], F32, "raw", 3)
+            both = rotating([P, 2, S], F32, "raw", 2)
             nc.sync.dma_start(
                 out=both[:], in_=x0[2 * pair * P : 2 * (pair + 1) * P, :].rearrange("(i p) m -> p i m", p=P)
             )

@@ -227,6 +227,7 @@ def tile_list_foundry_job_dispatch_kernel(
         first_melts = [rotating([P, 2, PACK, QUARTER], F32, "first_melt", 1), melt_room(0, 1)]
         w1_bf = {}
         w1_w = {}
+        late_words = None
         w1_s = {}
 
         def w1_views(a, b, first, last):
@@ -237,8 +238,9 @@ def tile_list_foundry_job_dispatch_kernel(
             )
 
         w1_bf[0, 0] = held([P, PACK, P, PACK], BF16, "w1_bf_first")
-        for a, b in ((1, 0), (0, 1)):
-            w1_bf[a, b] = rotating([P, PACK, P, PACK], BF16, "w1_bf", 1)
+        shared_bf = held([P, PACK + 2, P, PACK], BF16, "shared_bf")
+        w1_bf[1, 0] = shared_bf[:, 2:]
+        w1_bf[0, 1] = shared_bf[:, :PACK]
         w1_bf[1, 1] = sums[:, QUARTER : QUARTER + S].bitcast(BF16).rearrange("p (t m j) -> p t m j", t=PACK, j=PACK)
 
         def round_w1_on_vector(a, b, first, last):
@@ -250,7 +252,7 @@ def tile_list_foundry_job_dispatch_kernel(
             nc.scalar.activation(out=dst, in_=src, func=COPY, scale=-1.0)
 
         def quantise_w1(a, b, pieces=1):
-            w1_w[a, b] = late_words[:, a, :] if b == 1 else held([P, PASS], U32, f"w1_w{a}{b}")
+            w1_w[a, b] = late_words if a + b == 2 else held([P, PASS], U32, f"w1_w{a}{b}")
             w1_s[a, b] = held([P, PASS], U8, f"w1_s{a}{b}")
             count = PACK // pieces
             for first in range(0, PACK, count):
@@ -261,7 +263,7 @@ def tile_list_foundry_job_dispatch_kernel(
                     in_=w1_bf[a, b][:, first : first + count].rearrange("p t m j -> p (t m j)"),
                 )
 
-        def mould_and_min(b, q, group, room=None, upper=None):
+        def mould_and_min(b, q, group, room=None, sources=None):
             cols = slice(q * QUARTER, (q + 1) * QUARTER)
             for pair in range(2):
                 acc = group[pair][:].rearrange("p (i j) -> p i j", i=2)
@@ -279,7 +281,7 @@ def tile_list_foundry_job_dispatch_kernel(
                         )
                 pair_t = slice(2 * pair, 2 * pair + 2)
                 dst = later[b, q] if room is None else room
-                src = upper if pair == 1 and upper is not None else later[b, q][:, pair_t, :]
+                src = later[b, q][:, pair_t, :] if sources is None else sources[pair]
                 nc.vector.tensor_tensor(dst[:, pair_t, :], acc, src, ALU.min)
             if room is not None:
                 later[b, q] = room
@@ -393,43 +395,36 @@ def tile_list_foundry_job_dispatch_kernel(
             for u in range(2):
                 round_w1_on_vector(a, 0, u * P // 2, (u + 1) * P // 2)
             quantise_w1(a, 0, 1 + a)
-        for a, u in ((0, 0), (0, 1), (1, 0)):
-            nc.gpsimd.tensor_scalar(
-                w1_bf[a, 1][:, :, u * P // 2 : (u + 1) * P // 2, :],
-                w1_raw[a, 1, u].rearrange("p j (m t) -> p t m j", t=PACK),
-                -1.0,
-                0.0,
-                ALU.mult,
-                ALU.add,
-            )
-        third = rotating([P, 2, PACK, QUARTER], F32, "early", 1)
+        for u in range(2):
+            round_w1_on_vector(0, 1, u * P // 2, (u + 1) * P // 2)
+        third = melt_room(1, 0)
         for t in range(PACK):
             melt_bank(1, 0, t, low[t], third)
-        round_w1_on_scalar(1, 1, P // 2, P)
-        mould_and_min(0, 2, high[2:])
-        last_melt = rotating([P, 2, PACK, QUARTER], F32, "last1", 1)
-        for t in range(2):
-            melt_bank(1, 1, t, high[t], last_melt)
+        for u in range(2):
+            round_w1_on_scalar(1, 1, u * P // 2, (u + 1) * P // 2)
         first_minima = rotating([P, 2, PACK, QUARTER], F32, "tab_w0", 1)
-        mould_and_min(0, 0, low[:2], first_minima[:, 0])
-
-        mould_and_min(0, 1, low[2:], first_minima[:, 1])
-        late_words = rotating([P, 2, PASS], U32, "first_melt", 1)
+        mould_and_min(0, 0, high[2:], first_minima[:, 0])
+        last_melt = [rotating([P, 2, 2, QUARTER], F32, f"last{pair}", 1) for pair in range(2)]
+        late_minima = rotating([P, 2, PACK, QUARTER], F32, "tab_w1", 1)
+        for t in range(2):
+            melt_bank(1, 1, t, high[t], late_minima, last_melt[0][:, :, t, :])
         quantise_w1(0, 1)
+        mould_and_min(0, 1, low[:2], first_minima[:, 1])
+
+        mould_and_min(0, 2, low[2:])
+        late_words = rotating([P, PASS], U32, "first_melt", 1)
         quantise_w1(1, 1, 2)
         mould_and_min(0, 3, high[2:], sums[:, :S].rearrange("p (t j) -> p t j", t=PACK))
         for t in range(2, PACK):
-            melt_bank(1, 1, t, low[t - 2], last_melt)
+            melt_bank(1, 1, t, low[t - 2], late_minima, last_melt[1][:, :, t - 2, :])
         for q in range(2):
             add_rel_on_gpsimd(0, q)
         mould_and_min(1, 0, low[2:])
-        mould_and_min(1, 1, high[2:], w1_raw[0, 1, 0])
-        mould_and_min(1, 2, high[:2])
-        mould_and_min(1, 3, low[:2], w1_raw[0, 1, 1])
-        add_rel_on_vector(
-            1, 0, last_melt[:, 1, :2, :].rearrange("p t j -> p (t j)").bitcast(BF16).rearrange("p (j t) -> p j t", t=PACK)
-        )
-        early_words = rotating([P, 4, QUARTER], U32, "early", 1)
+        mould_and_min(1, 1, high[2:])
+        mould_and_min(1, 2, high[:2], None, [part[:, 0] for part in last_melt])
+        mould_and_min(1, 3, low[:2], None, [part[:, 1] for part in last_melt])
+        add_rel_on_vector(1, 0, rotating([P, QUARTER, PACK], BF16, "last0", 1))
+        early_words = rotating([P, 4, QUARTER], U32, "last1", 1)
         for b in range(2):
             quantise_h(b, 0)
         add_rel_on_vector(1, 1, h_bf[0, 0])

@@ -47,9 +47,12 @@ def tile_list_foundry_job_dispatch_kernel(
         def rotating(shape, dtype, name, bufs):
             return ring.tile(shape, dtype, name=name, bufs=bufs, align_bytes=64)
 
+        def taking_over(shape, dtype, name):
+            return rotating(shape, dtype, name, 1)
+
         picks = keep.tile([P, S // PER_COLUMN], U16, name="picks")
         places = keep.tile([P, S // PER_COLUMN], U16, name="places")
-        tab_w = [rotating([P, T], I32, f"tab_w{a}", 1) for a in range(2)]
+        tab_w = [taking_over([P, T], I32, f"tab_w{a}") for a in range(2)]
         tab_s = held([P, T], U8, "tab_s")
         v_w = [held([P, S], U32, f"v_w{a}") for a in range(2)]
         picked_s = held([P, S], U8, "picked_s")
@@ -82,7 +85,6 @@ def tile_list_foundry_job_dispatch_kernel(
             cols = (slice(0, FIRST_PIECE[a]), slice(FIRST_PIECE[a], T))[piece]
             nc.sync.dma_start(out=tab_w[a][:, cols], in_=words[:, cols])
 
-
         def load_w4(b):
             words = w4_words[:, :, 2 * b * PASS : 2 * (b + 1) * PASS].rearrange("a p c -> p a c")
             nc.sync.dma_start(out=w4_raw[b][:].bitcast(I32), in_=words.bitcast(I32))
@@ -113,7 +115,7 @@ def tile_list_foundry_job_dispatch_kernel(
         w1_raw = {(a, 0, u): raw[a][:, u] for a in range(2) for u in range(2)}
         for u in range(2):
             w1_raw[0, 1, u] = held([P, PACK, PASS // 2], F32, f"w1_raw01{u}")[:]
-            w1_raw[1, 1, u] = rotating([P, PACK, PASS // 2], F32, f"last{u}", 1)[:]
+            w1_raw[1, 1, u] = taking_over([P, PACK, PASS // 2], F32, f"last{u}")[:]
 
         def load_w1(a, b, u):
             first = b * PASS + u * PASS // 2
@@ -150,19 +152,18 @@ def tile_list_foundry_job_dispatch_kernel(
         nc.sync.dma_start(out=gains[:], in_=wgo)
         load_rel(1, 1)
 
-        for h in range(2):
-            nc.vector.tensor_copy(
-                v_w[0][:, h * HALF : (h + 1) * HALF],
-                tab_w[0][:].bitcast(U32).indirect(picks[:, h * HALF // PER_COLUMN : (h + 1) * HALF // PER_COLUMN]),
-            )
+        def gather_words(a, width):
+            for first in range(0, S, width):
+                nc.vector.tensor_copy(
+                    v_w[a][:, first : first + width],
+                    tab_w[a][:].bitcast(U32).indirect(picks[:, first // PER_COLUMN : (first + width) // PER_COLUMN]),
+                )
 
-        def order_w4(b):
-            nc.vector.tensor_copy(
-                w4_w[b][:].bitcast(U16).rearrange("p a (t m) -> p a t m", t=PACK),
-                w4_raw[b][:].bitcast(U16).rearrange("p a (m t) -> p a t m", t=PACK),
-            )
-
-        order_w4(0)
+        gather_words(0, HALF)
+        nc.vector.tensor_copy(
+            w4_w[0][:].bitcast(U16).rearrange("p a (t m) -> p a t m", t=PACK),
+            w4_raw[0][:].bitcast(U16).rearrange("p a (m t) -> p a t m", t=PACK),
+        )
         nc.scalar.copy(
             out=w4_w[1][:].bitcast(U16).rearrange("p a (t c i) -> p a c t i", t=PACK, i=LINE),
             in_=w4_raw[1][:].bitcast(U16).rearrange("p a (c i t) -> p a c t i", t=PACK, i=LINE),
@@ -171,100 +172,95 @@ def tile_list_foundry_job_dispatch_kernel(
             w4_s[:].rearrange("p a (b t m) -> p (a b) t m", t=PACK, m=P),
             w4_sraw[:].rearrange("p a (b m t) -> p (a b) t m", t=PACK, m=P),
         )
-        for q in range(4):
-            nc.vector.tensor_copy(
-                v_w[1][:, q * QUARTER : (q + 1) * QUARTER],
-                tab_w[1][:].bitcast(U32).indirect(picks[:, q * QUARTER // PER_COLUMN : (q + 1) * QUARTER // PER_COLUMN]),
-            )
+        gather_words(1, QUARTER)
 
         banks = [psum.tile([P, HALF], F32, name=f"bank{i}") for i in range(8)]
 
+        neg_melt = {}
         later = {}
 
-        def melt_pass(b, h, t, a, acc, first=0, width=HALF):
-            cols = slice(h * HALF + first, h * HALF + first + width)
-            c0 = b * PASS + t * P
+        def by_pairs(values):
+            return [values[:, 2 * pair : 2 * pair + 2, :] for pair in range(2)]
+
+        def as_t_j(values):
+            return values.rearrange("p (t j) -> p t j", t=PACK)
+
+        def melt_pass(b, t, a, cols, acc, start, stop):
             nc.tensor.matmul_mx(
-                out=acc[:, first : first + width],
+                out=acc,
                 lhsT=w4_w[b][:, a, 2 * t * P : 2 * (t + 1) * P].bitcast(FP4X4),
-                lhsT_scale=w4_s[:, a, c0 : c0 + P],
+                lhsT_scale=w4_s[:, a, b * PASS + t * P : b * PASS + (t + 1) * P],
                 rhs=v_w[a][:, cols].bitcast(FP8X4),
                 rhs_scale=v_s[:, a, cols],
-                start=(a == 0),
-                stop=(a == 1 and first + width == HALF),
+                start=start,
+                stop=stop,
             )
 
-        def open_melt(b, h, group):
-            for t in range(PACK):
-                melt_pass(b, h, t, 0, group[t])
+        def copy_negated(dst, bank):
+            nc.scalar.activation(out=dst, in_=bank[:].rearrange("p (i j) -> p i j", i=2), func=COPY, scale=-1.0)
 
-        def melt_bank(b, h, t, bank, neg_melt, room=None):
+        def early_melt_pass(q, a):
+            cols = slice(q * QUARTER, (q + 1) * QUARTER)
+            for pair in range(2):
+                bank = banks[2 * q + pair]
+                for i in range(2):
+                    acc = bank[:, i * QUARTER : (i + 1) * QUARTER]
+                    melt_pass(0, 2 * pair + i, a, cols, acc, start=(a == 0 and i == 0), stop=(a == 1 and i == 1))
+                if a == 1:
+                    copy_negated(neg_melt[0, q][pair], bank)
+
+        def late_melt(h, t, bank, dst):
             for a in range(2):
-                melt_pass(b, h, t, a, bank)
-            copy_melt(b, h, t, bank, neg_melt, room)
+                melt_pass(1, t, a, slice(h * HALF, (h + 1) * HALF), bank[:], start=(a == 0), stop=(a == 1))
+            copy_negated(dst, bank)
 
-        def copy_melt(b, h, t, bank, neg_melt, room=None):
-            nc.scalar.activation(
-                out=neg_melt[:, :, t, :] if room is None else room,
-                in_=bank[:].rearrange("p (i j) -> p i j", i=2),
-                func=COPY,
-                scale=-1.0,
-            )
-            for i in range(2):
-                later[b, 2 * h + i] = neg_melt[:, i]
+        after_w1 = held([P, 2 * S], F32, "after_w1")
+        early_melt = [
+            taking_over([P, 2, PACK, QUARTER], F32, "first_melt"),
+            held([P, 2, PACK, QUARTER], F32, "second_melt"),
+        ]
+        for q in range(4):
+            neg_melt[0, q] = by_pairs(early_melt[q // 2][:, q % 2])
 
-        def close_melt(b, h, group, neg_melt):
-            for t in range(PACK):
-                melt_pass(b, h, t, 1, group[t], 0, QUARTER)
-            for t in range(PACK):
-                melt_pass(b, h, t, 1, group[t], QUARTER, QUARTER)
-                copy_melt(b, h, t, group[t], neg_melt)
-
-        def melt_room(b, h):
-            return held([P, 2, PACK, QUARTER], F32, f"melt{b}{h}")
-
-        sums = held([P, 2 * S], F32, "sums")
-        first_melts = [rotating([P, 2, PACK, QUARTER], F32, "first_melt", 1), melt_room(0, 1)]
-        w1_bf = {}
-        w1_w = {}
-        late_words = None
-        w1_s = {}
-
-        def w1_views(a, b, first, last):
-            u = first // (P // 2)
-            return (
-                w1_bf[a, b][:, :, first:last, :].rearrange("p t m j -> p m t j"),
-                w1_raw[a, b, u].rearrange("p j (m t) -> p m t j", t=PACK)[:, first - u * P // 2 : last - u * P // 2],
-            )
-
-        w1_bf[0, 0] = held([P, PACK, P, PACK], BF16, "w1_bf_first")
+        w1_bf = {(0, 0): held([P, PACK, P, PACK], BF16, "w1_bf_first")}
         shared_bf = held([P, PACK + 2, P, PACK], BF16, "shared_bf")
         w1_bf[1, 0] = shared_bf[:, 2:]
         w1_bf[0, 1] = shared_bf[:, :PACK]
-        w1_bf[1, 1] = sums[:, QUARTER : QUARTER + S].bitcast(BF16).rearrange("p (t m j) -> p t m j", t=PACK, j=PACK)
+        w1_bf[1, 1] = after_w1[:, QUARTER : QUARTER + S].bitcast(BF16).rearrange("p (t m j) -> p t m j", t=PACK, j=PACK)
+        w1_w = {}
+        w1_s = {}
 
-        def round_w1_on_vector(a, b, first, last):
-            dst, src = w1_views(a, b, first, last)
-            nc.vector.tensor_scalar(dst, src, -1.0, None, ALU.mult)
+        def w1_views(a, b, u):
+            return (
+                w1_bf[a, b][:, :, u * P // 2 : (u + 1) * P // 2, :].rearrange("p t m j -> p m t j"),
+                w1_raw[a, b, u].rearrange("p j (m t) -> p m t j", t=PACK),
+            )
 
-        def round_w1_on_scalar(a, b, first, last):
-            dst, src = w1_views(a, b, first, last)
+        def round_w1_on_vector(a, b, u, pieces):
+            dst, src = w1_views(a, b, u)
+            count = PACK // pieces
+            for t in range(0, PACK, count):
+                nc.vector.tensor_scalar(dst[:, :, t : t + count, :], src[:, :, t : t + count, :], -1.0, None, ALU.mult)
+
+        def round_w1_on_scalar(a, b, u):
+            dst, src = w1_views(a, b, u)
             nc.scalar.activation(out=dst, in_=src, func=COPY, scale=-1.0)
 
-        def quantise_w1(a, b, pieces=1):
-            w1_w[a, b] = late_words if a + b == 2 else held([P, PASS], U32, f"w1_w{a}{b}")
+        def quantise_w1(a, b, pieces, words):
+            w1_w[a, b] = words
             w1_s[a, b] = held([P, PASS], U8, f"w1_s{a}{b}")
             count = PACK // pieces
-            for first in range(0, PACK, count):
-                cols = slice(first * P, (first + count) * P)
+            for t in range(0, PACK, count):
+                cols = slice(t * P, (t + count) * P)
                 nc.vector.quantize_mx(
                     out=w1_w[a, b][:, cols].bitcast(FP8X4),
                     scales=w1_s[a, b][:, cols],
-                    in_=w1_bf[a, b][:, first : first + count].rearrange("p t m j -> p (t m j)"),
+                    in_=w1_bf[a, b][:, t : t + count].rearrange("p t m j -> p (t m j)"),
                 )
 
-        def mould_and_min(b, q, group, room=None, sources=None):
+        def mould_and_min(b, q, group, dst):
             cols = slice(q * QUARTER, (q + 1) * QUARTER)
+            later[b, q] = dst
             for pair in range(2):
                 acc = group[pair][:].rearrange("p (i j) -> p i j", i=2)
                 for i in range(2):
@@ -279,20 +275,15 @@ def tile_list_foundry_job_dispatch_kernel(
                             start=(a == 1),
                             stop=(a == 0),
                         )
-                pair_t = slice(2 * pair, 2 * pair + 2)
-                dst = later[b, q] if room is None else room
-                src = later[b, q][:, pair_t, :] if sources is None else sources[pair]
-                nc.vector.tensor_tensor(dst[:, pair_t, :], acc, src, ALU.min)
-            if room is not None:
-                later[b, q] = room
+                nc.vector.tensor_tensor(by_pairs(dst)[pair], acc, neg_melt[b, q][pair], ALU.min)
 
         h_pair = {}
         h_bf = {}
         h_w = {}
         h_s = {}
 
-        def add_rel_on_vector(b, q, room):
-            h_bf[b, q] = room
+        def add_rel_on_vector(b, q, dst):
+            h_bf[b, q] = dst
             nc.vector.tensor_tensor(
                 h_bf[b, q][:].rearrange("p (c i) t -> p c t i", i=RUN),
                 later[b, q].rearrange("p t (c i) -> p c t i", i=RUN),
@@ -328,8 +319,7 @@ def tile_list_foundry_job_dispatch_kernel(
                 in_=back.rearrange("p jb u j -> p jb j u"),
             )
 
-        def add_rel_on_gpsimd(b, q):
-            total = (sums[:, S:].rearrange("p (t j) -> p t j", t=PACK), first_melts[1][:, 1])[q]
+        def add_rel_on_gpsimd(b, q, total):
             nc.gpsimd.tensor_tensor(total, later[b, q], rel_sb[b, q], ALU.add)
             h_bf[b, q] = held([P, QUARTER, PACK], BF16, f"h_first{b}{q}")
             nc.scalar.copy(
@@ -337,8 +327,8 @@ def tile_list_foundry_job_dispatch_kernel(
                 in_=total.rearrange("p t (c i) -> p c t i", i=PACK),
             )
 
-        def quantise_h(b, q):
-            h_w[b, q] = early_words[:, 2 * q + b, :]
+        def quantise_h(b, q, words):
+            h_w[b, q] = words
             h_s[b, q] = held([P, QUARTER], U8, f"h_s{b}{q}")
             nc.vector.quantize_mx(
                 out=h_w[b, q][:].bitcast(FP8X4), scales=h_s[b, q][:], in_=h_bf[b, q][:].rearrange("p j t -> p (j t)")
@@ -387,49 +377,50 @@ def tile_list_foundry_job_dispatch_kernel(
                 scatter(n, y, q * QUARTER, QUARTER)
 
         low, high = banks[:4], banks[4:]
-        for h, group in enumerate((low, high)):
-            open_melt(0, h, group)
-        for h, group in enumerate((low, high)):
-            close_melt(0, h, group, first_melts[h])
         for a in range(2):
-            for u in range(2):
-                round_w1_on_vector(a, 0, u * P // 2, (u + 1) * P // 2)
-            quantise_w1(a, 0, 1 + a)
+            for q in range(4):
+                early_melt_pass(q, a)
+        for a in range(2):
+            round_w1_on_vector(a, 0, 0, pieces=1)
+            round_w1_on_vector(a, 0, 1, pieces=2)
+            quantise_w1(a, 0, 2, held([P, PASS], U32, f"w1_w{a}0"))
         for u in range(2):
-            round_w1_on_vector(0, 1, u * P // 2, (u + 1) * P // 2)
-        third = melt_room(1, 0)
+            round_w1_on_vector(0, 1, u, pieces=1)
+        third_melt = held([P, 2, PACK, QUARTER], F32, "third_melt")
         for t in range(PACK):
-            melt_bank(1, 0, t, low[t], third)
+            late_melt(0, t, low[t], third_melt[:, :, t, :])
         for u in range(2):
-            round_w1_on_scalar(1, 1, u * P // 2, (u + 1) * P // 2)
-        first_minima = rotating([P, 2, PACK, QUARTER], F32, "tab_w0", 1)
-        mould_and_min(0, 0, high[2:], first_minima[:, 0])
-        last_melt = [rotating([P, 2, 2, QUARTER], F32, f"last{pair}", 1) for pair in range(2)]
-        late_minima = rotating([P, 2, PACK, QUARTER], F32, "tab_w1", 1)
-        for t in range(2):
-            melt_bank(1, 1, t, high[t], late_minima, last_melt[0][:, :, t, :])
-        quantise_w1(0, 1)
-        mould_and_min(0, 1, low[:2], first_minima[:, 1])
+            round_w1_on_scalar(1, 1, u)
 
-        mould_and_min(0, 2, low[2:])
-        late_words = rotating([P, PASS], U32, "first_melt", 1)
-        quantise_w1(1, 1, 2)
-        mould_and_min(0, 3, high[2:], sums[:, :S].rearrange("p (t j) -> p t j", t=PACK))
-        for t in range(2, PACK):
-            melt_bank(1, 1, t, low[t - 2], late_minima, last_melt[1][:, :, t - 2, :])
-        for q in range(2):
-            add_rel_on_gpsimd(0, q)
-        mould_and_min(1, 0, low[2:])
-        mould_and_min(1, 1, high[2:])
-        mould_and_min(1, 2, high[:2], None, [part[:, 0] for part in last_melt])
-        mould_and_min(1, 3, low[:2], None, [part[:, 1] for part in last_melt])
-        add_rel_on_vector(1, 0, rotating([P, QUARTER, PACK], BF16, "last0", 1))
-        early_words = rotating([P, 4, QUARTER], U32, "last1", 1)
+        first_minima = taking_over([P, 2, PACK, QUARTER], F32, "tab_w0")
+        mould_and_min(0, 0, high[2:], first_minima[:, 0])
+        last_melt = [taking_over([P, 2, 2, QUARTER], F32, f"last{pair}") for pair in range(2)]
+        last_minima = taking_over([P, 2, PACK, QUARTER], F32, "tab_w1")
+        for i in range(2):
+            neg_melt[1, i] = by_pairs(third_melt[:, i])
+            neg_melt[1, 2 + i] = [last_melt[pair][:, i] for pair in range(2)]
+            late_melt(1, i, high[i], last_melt[0][:, :, i, :])
+        quantise_w1(0, 1, 1, held([P, PASS], U32, "w1_w01"))
+        mould_and_min(0, 1, low[:2], first_minima[:, 1])
+        mould_and_min(0, 2, low[2:], early_melt[1][:, 0])
+        quantise_w1(1, 1, 2, taking_over([P, PASS], U32, "first_melt"))
+        mould_and_min(0, 3, high[2:], as_t_j(after_w1[:, :S]))
+        for i in range(2):
+            late_melt(1, 2 + i, low[i], last_melt[1][:, :, i, :])
+
+        add_rel_on_gpsimd(0, 0, as_t_j(after_w1[:, S:]))
+        add_rel_on_gpsimd(0, 1, early_melt[1][:, 1])
+        mould_and_min(1, 0, low[2:], third_melt[:, 0])
+        mould_and_min(1, 1, high[2:], third_melt[:, 1])
+        mould_and_min(1, 2, high[:2], last_minima[:, 0])
+        mould_and_min(1, 3, low[:2], last_minima[:, 1])
+        add_rel_on_vector(1, 0, taking_over([P, QUARTER, PACK], BF16, "last0"))
+        first_words = taking_over([P, 2, 2, QUARTER], U32, "last1")
         for b in range(2):
-            quantise_h(b, 0)
+            quantise_h(b, 0, first_words[:, 0, b, :])
         add_rel_on_vector(1, 1, h_bf[0, 0])
         for b in range(2):
-            quantise_h(b, 1)
+            quantise_h(b, 1, first_words[:, 1, b, :])
 
         finish(0, (0,), high[0])
         finish(0, (1,), high[1])

@@ -24,11 +24,10 @@ QUADRANTS = 4
 HALF = S // 2
 QUARTER = S // 4
 PER_COLUMN = 16
-SCALE_ROWS = 16
-LANDING = 64 - SCALE_ROWS
+LANDING_STEP = 4
 LINE = 8
 RUN = 2
-FIRST_PIECE = (T // 2, T // 4)
+FIRST_PIECE = (T // 4, T // 4)
 LAST_PIECES = 4
 
 
@@ -68,17 +67,12 @@ def tile_list_foundry_job_dispatch_kernel(
         ident = held([P, P], F32, "ident")
 
         nc.vector.memset(w4_sraw[:].bitcast(I32), 0)
-        for a in range(2):
-            nc.vector.memset(tab_s[64 * a : 64 * a + LANDING, :].bitcast(I32), 0)
+        nc.vector.memset(tab_s[:].bitcast(I32), 0)
         nc.vector.memset(v_s[:].bitcast(I32), 0)
         nc.vector.memset(w8_s[:].bitcast(I32), 0)
         make_identity(nc, ident[:])
 
         nc.sync.dma_start(picks[:], offs)
-        for a in range(2):
-            nc.sync.dma_start(
-                out=tab_s[64 * a + LANDING : 64 * (a + 1), :].bitcast(I32), in_=tab_scales[a].bitcast(I32)
-            )
 
         def load_table(a, piece):
             words = tab_words[a].rearrange("p t i -> p (t i)").bitcast(I32)
@@ -90,20 +84,23 @@ def tile_list_foundry_job_dispatch_kernel(
             nc.sync.dma_start(out=w4_raw[b][:].bitcast(I32), in_=words.bitcast(I32))
 
         load_table(0, 0)
+        nc.sync.dma_start(
+            out=tab_s[0:P:LANDING_STEP, :].bitcast(I32), in_=tab_scales.rearrange("a q t -> (a q) t").bitcast(I32)
+        )
         load_w4(0)
         load_table(0, 1)
-        for g in range(QUADRANTS):
+        for r in range(QUADRANTS):
             nc.scalar.dma_start(
-                out=w4_sraw[32 * g : 32 * g + 4, :, :].bitcast(I32),
-                in_=w4_scales[:, 4 * g : 4 * g + 4, :].rearrange("a r c -> r a c").bitcast(I32),
+                out=w4_sraw[r:P:32, :, :].bitcast(I32),
+                in_=w4_scales[:, r::4, :].rearrange("a g c -> g a c").bitcast(I32),
             )
         nc.vector.tensor_copy(picked_s[:], tab_s[:].indirect(picks[:]))
 
         def move_plane(a):
-            for g in range(QUADRANTS):
-                first = 64 * a + LANDING + 4 * g
+            for r in range(4):
+                first = 64 * a + LANDING_STEP * r
                 nc.sync.dma_start(
-                    out=v_s[32 * g : 32 * g + 4, a, :].bitcast(I32), in_=picked_s[first : first + 4, :].bitcast(I32)
+                    out=v_s[r:P:32, a, :].bitcast(I32), in_=picked_s[first : 64 * (a + 1) : 16, :].bitcast(I32)
                 )
 
         load_table(1, 0)

from contextlib import ExitStack

import concourse.mybir as mybir
from concourse.masks import make_identity

T, S, K, H, N = 4096, 1024, 1024, 1024, 512
FLOPS = 2 * S * (2 * K * H + H * N)

F32 = mybir.dt.float32
BF16 = mybir.dt.bfloat16
I32 = mybir.dt.int32
U32 = mybir.dt.uint32
U16 = mybir.dt.uint16
U8 = mybir.dt.uint8
FP8X4 = mybir.dt.float8_e4m3fn_x4
FP4X4 = mybir.dt.float4_e2m1fn_x4
ALU = mybir.AluOpType
COPY = mybir.ActivationFunctionType.Copy

P = 128
PACK = 4
PASS = P * PACK
QUADRANTS = 4
HALF = S // 2
QUARTER = S // 4
PER_COLUMN = 16
LANDING_STEP = 4
LINE = 8
RUN = 2
FIRST_PIECE = (T // 4, T // 4)
LAST_PIECES = 4


def tile_list_foundry_job_dispatch_kernel(
    tc, tab_words, tab_scales, offs, w1, w4_words, w4_scales, rel, w8_words, w8_scales, offs2, wgo, x0, out
):
    nc = tc.nc
    with ExitStack() as ctx:
        keep = ctx.enter_context(tc.tile_pool(name="keep", bufs=1))
        ring = ctx.enter_context(tc.tile_pool(name="ring", bufs=2))
        psum = ctx.enter_context(tc.psum_pool(name="psum", bufs=1))

        def held(shape, dtype, name):
            return keep.tile(shape, dtype, name=name, align_bytes=64)

        def rotating(shape, dtype, name, bufs):
            return ring.tile(shape, dtype, name=name, bufs=bufs, align_bytes=64)

        def taking_over(shape, dtype, name):
            return rotating(shape, dtype, name, 1)

        picks = keep.tile([P, S // PER_COLUMN], U16, name="picks")
        places = keep.tile([P, S // PER_COLUMN], U16, name="places")
        tab_w = [taking_over([P, T], I32, f"tab_w{a}") for a in range(2)]
        tab_s = held([P, T], U8, "tab_s")
        v_w = [held([P, S], U32, f"v_w{a}") for a in range(2)]
        picked_s = held([P, S], U8, "picked_s")
        v_s = held([P, 2, S], U8, "v_s")
        w4_raw = [held([P, 2, 2 * PASS], U8, f"w4_raw{b}") for b in range(2)]
        w4_w = [held([P, 2, 2 * PASS], U8, f"w4_w{b}") for b in range(2)]
        w4_sraw = held([P, 2, H], U8, "w4_sraw")
        w4_s = held([P, 2, H], U8, "w4_s")
        w8_w = held([P, 2, N], I32, "w8_w")
        w8_s = held([P, N], U8, "w8_s")
        gains = held([P, S], F32, "gains")
        page = [held([P, S], F32, f"page{n}") for n in range(N // P)]
        ident = held([P, P], F32, "ident")

        nc.vector.memset(w4_sraw[:].bitcast(I32), 0)
        nc.vector.memset(tab_s[:].bitcast(I32), 0)
        nc.vector.memset(v_s[:].bitcast(I32), 0)
        nc.vector.memset(w8_s[:].bitcast(I32), 0)
        make_identity(nc, ident[:])

        nc.sync.dma_start(picks[:], offs)

        def load_table(a, piece):
            words = tab_words[a].rearrange("p t i -> p (t i)").bitcast(I32)
            cols = (slice(0, FIRST_PIECE[a]), slice(FIRST_PIECE[a], T))[piece]
            nc.sync.dma_start(out=tab_w[a][:, cols], in_=words[:, cols])

        def load_w4(b):
            words = w4_words[:, :, 2 * b * PASS : 2 * (b + 1) * PASS].rearrange("a p c -> p a c")
            nc.sync.dma_start(out=w4_raw[b][:].bitcast(I32), in_=words.bitcast(I32))

        load_table(0, 0)
        nc.sync.dma_start(
            out=tab_s[0:P:LANDING_STEP, :].bitcast(I32), in_=tab_scales.rearrange("a q t -> (a q) t").bitcast(I32)
        )
        load_w4(0)
        load_table(0, 1)
        for r in range(QUADRANTS):
            nc.scalar.dma_start(
                out=w4_sraw[r:P:32, :, :].bitcast(I32),
                in_=w4_scales[:, r::4, :].rearrange("a g c -> g a c").bitcast(I32),
            )
        nc.vector.tensor_copy(picked_s[:], tab_s[:].indirect(picks[:]))

        def move_plane(a):
            for r in range(4):
                first = 64 * a + LANDING_STEP * r
                nc.sync.dma_start(
                    out=v_s[r:P:32, a, :].bitcast(I32), in_=picked_s[first : 64 * (a + 1) : 16, :].bitcast(I32)
                )

        load_table(1, 0)
        move_plane(0)
        load_table(1, 1)
        load_w4(1)

        raw = [rotating([P, 2, PACK, PASS // 2], F32, "raw", 2) for a in range(2)]
        w1_raw = {(a, 0, u): raw[a][:, u] for a in range(2) for u in range(2)}
        for u in range(2):
            w1_raw[0, 1, u] = held([P, PACK, PASS // 2], F32, f"w1_raw01{u}")[:]
            w1_raw[1, 1, u] = taking_over([P, PACK, PASS // 2], F32, f"last{u}")[:]

        def load_w1(a, b, u):
            first = b * PASS + u * PASS // 2
            rows = w1[a * PASS : (a + 1) * PASS, first : first + PASS // 2].rearrange("(p j) c -> p j c", j=PACK)
            nc.sync.dma_start(out=w1_raw[a, b, u], in_=rows)

        move_plane(1)
        for b in range(2):
            for a in range(2):
                for u in range(2):
                    load_w1(a, b, u)

        rel_sb = {}
        rel_half = {}

        def load_rel(b, h):
            rel_half[b, h] = held([P, PACK, HALF], F32, f"rel{b}{h}")
            nc.sync.dma_start(
                out=rel_half[b, h][:],
                in_=rel[b * PASS : (b + 1) * PASS, h * HALF : (h + 1) * HALF].rearrange("(p t) j -> p t j", t=PACK),
            )
            for i in range(2):
                rel_sb[b, 2 * h + i] = rel_half[b, h][:, :, i * QUARTER : (i + 1) * QUARTER]

        load_rel(0, 0)
        load_rel(1, 0)
        load_rel(0, 1)
        for g in range(QUADRANTS):
            nc.sync.dma_start(
                out=w8_s[32 * g : 32 * g + 8, :].bitcast(I32), in_=w8_scales[:, 4 * g : 4 * g + 4, :].bitcast(I32)
            )
        nc.sync.dma_start(out=w8_w[:], in_=w8_words.rearrange("a p c i -> p a (c i)").bitcast(I32))
        nc.sync.dma_start(places[:], offs2)
        nc.sync.dma_start(out=gains[:], in_=wgo)
        load_rel(1, 1)

        def gather_words(a, width):
            for first in range(0, S, width):
                nc.vector.tensor_copy(
                    v_w[a][:, first : first + width],
                    tab_w[a][:].bitcast(U32).indirect(picks[:, first // PER_COLUMN : (first + width) // PER_COLUMN]),
                )

        gather_words(0, HALF)
        nc.vector.tensor_copy(
            w4_w[0][:].bitcast(U16).rearrange("p a (t m) -> p a t m", t=PACK),
            w4_raw[0][:].bitcast(U16).rearrange("p a (m t) -> p a t m", t=PACK),
        )
        nc.scalar.copy(
            out=w4_w[1][:].bitcast(U16).rearrange("p a (t c i) -> p a c t i", t=PACK, i=LINE),
            in_=w4_raw[1][:].bitcast(U16).rearrange("p a (c i t) -> p a c t i", t=PACK, i=LINE),
        )
        nc.vector.tensor_copy(
            w4_s[:].rearrange("p a (b t m) -> p (a b) t m", t=PACK, m=P),
            w4_sraw[:].rearrange("p a (b m t) -> p (a b) t m", t=PACK, m=P),
        )
        gather_words(1, QUARTER)

        banks = [psum.tile([P, HALF], F32, name=f"bank{i}") for i in range(8)]

        neg_melt = {}
        later = {}

        def by_pairs(values):
            return [values[:, 2 * pair : 2 * pair + 2, :] for pair in range(2)]

        def as_t_j(values):
            return values.rearrange("p (t j) -> p t j", t=PACK)

        def melt_pass(b, t, a, cols, acc, start, stop):
            nc.tensor.matmul_mx(
                out=acc,
                lhsT=w4_w[b][:, a, 2 * t * P : 2 * (t + 1) * P].bitcast(FP4X4),
                lhsT_scale=w4_s[:, a, b * PASS + t * P : b * PASS + (t + 1) * P],
                rhs=v_w[a][:, cols].bitcast(FP8X4),
                rhs_scale=v_s[:, a, cols],
                start=start,
                stop=stop,
            )

        def copy_negated(dst, bank):
            nc.scalar.activation(out=dst, in_=bank[:].rearrange("p (i j) -> p i j", i=2), func=COPY, scale=-1.0)

        def early_melt_pass(q, a):
            cols = slice(q * QUARTER, (q + 1) * QUARTER)
            for pair in range(2):
                bank = banks[2 * q + pair]
                for i in range(2):
                    acc = bank[:, i * QUARTER : (i + 1) * QUARTER]
                    melt_pass(0, 2 * pair + i, a, cols, acc, start=(a == 0 and i == 0), stop=(a == 1 and i == 1))
                if a == 1:
                    copy_negated(neg_melt[0, q][pair], bank)

        def late_melt(h, t, bank, dst):
            for a in range(2):
                melt_pass(1, t, a, slice(h * HALF, (h + 1) * HALF), bank[:], start=(a == 0), stop=(a == 1))
            copy_negated(dst, bank)

        after_w1 = held([P, 2 * S], F32, "after_w1")
        early_melt = [
            taking_over([P, 2, PACK, QUARTER], F32, "first_melt"),
            held([P, 2, PACK, QUARTER], F32, "second_melt"),
        ]
        for q in range(4):
            neg_melt[0, q] = by_pairs(early_melt[q // 2][:, q % 2])

        w1_bf = {(0, 0): held([P, PACK, P, PACK], BF16, "w1_bf_first")}
        shared_bf = held([P, PACK + 2, P, PACK], BF16, "shared_bf")
        w1_bf[1, 0] = shared_bf[:, 2:]
        w1_bf[0, 1] = shared_bf[:, :PACK]
        w1_bf[1, 1] = after_w1[:, QUARTER : QUARTER + S].bitcast(BF16).rearrange("p (t m j) -> p t m j", t=PACK, j=PACK)
        w1_w = {}
        w1_s = {}

        def w1_views(a, b, u):
            return (
                w1_bf[a, b][:, :, u * P // 2 : (u + 1) * P // 2, :].rearrange("p t m j -> p m t j"),
                w1_raw[a, b, u].rearrange("p j (m t) -> p m t j", t=PACK),
            )

        def round_w1_on_vector(a, b, u, pieces):
            dst, src = w1_views(a, b, u)
            count = PACK // pieces
            for t in range(0, PACK, count):
                nc.vector.tensor_scalar(dst[:, :, t : t + count, :], src[:, :, t : t + count, :], -1.0, None, ALU.mult)

        def round_w1_on_scalar(a, b, u):
            dst, src = w1_views(a, b, u)
            nc.scalar.activation(out=dst, in_=src, func=COPY, scale=-1.0)

        def quantise_w1(a, b, pieces, words):
            w1_w[a, b] = words
            w1_s[a, b] = held([P, PASS], U8, f"w1_s{a}{b}")
            count = PACK // pieces
            for t in range(0, PACK, count):
                cols = slice(t * P, (t + count) * P)
                nc.vector.quantize_mx(
                    out=w1_w[a, b][:, cols].bitcast(FP8X4),
                    scales=w1_s[a, b][:, cols],
                    in_=w1_bf[a, b][:, t : t + count].rearrange("p t m j -> p (t m j)"),
                )

        def mould_and_min(b, q, group, dst):
            cols = slice(q * QUARTER, (q + 1) * QUARTER)
            later[b, q] = dst
            for pair in range(2):
                acc = group[pair][:].rearrange("p (i j) -> p i j", i=2)
                for i in range(2):
                    t = 2 * pair + i
                    for a in (1, 0):
                        nc.tensor.matmul_mx(
                            out=acc[:, i, :],
                            lhsT=w1_w[a, b][:, t * P : (t + 1) * P].bitcast(FP8X4),
                            lhsT_scale=w1_s[a, b][:, t * P : (t + 1) * P],
                            rhs=v_w[a][:, cols].bitcast(FP8X4),
                            rhs_scale=v_s[:, a, cols],
                            start=(a == 1),
                            stop=(a == 0),
                        )
                nc.vector.tensor_tensor(by_pairs(dst)[pair], acc, neg_melt[b, q][pair], ALU.min)

        h_pair = {}
        h_bf = {}
        h_w = {}
        h_s = {}

        def add_rel_on_vector(b, q, dst):
            h_bf[b, q] = dst
            nc.vector.tensor_tensor(
                h_bf[b, q][:].rearrange("p (c i) t -> p c t i", i=RUN),
                later[b, q].rearrange("p t (c i) -> p c t i", i=RUN),
                rel_sb[b, q].rearrange("p t (c i) -> p c t i", i=RUN),
                ALU.add,
            )

        def add_rel_on_tensor(b, q, group, back_bank):
            if b == 0:
                h_pair[q] = held([P, 2, QUARTER, PACK], BF16, f"h_pair{q}")
            h_bf[b, q] = h_pair[q][:, b]
            turned = []
            for jb in range(QUARTER // P):
                acc = group[jb][:].rearrange("j (t p) -> j t p", t=PACK)
                jcols = slice(jb * P, (jb + 1) * P)
                for t in range(PACK):
                    nc.tensor.matmul(
                        acc[:, t, :], later[b, q][:, t, jcols], ident[:], start=True, stop=False, is_transpose=True
                    )
                    nc.tensor.matmul(
                        acc[:, t, :], rel_sb[b, q][:, t, jcols], ident[:], start=False, stop=True, is_transpose=True
                    )
                rows = rotating([P, 2, P, 2], BF16, "h_rows", 5)
                nc.scalar.copy(out=rows[:], in_=acc.rearrange("j (u e) p -> j u p e", e=2))
                turned.append(rows)
            back = back_bank[:].rearrange("p (jb u j) -> p jb u j", u=2, j=P)
            for jb in range(QUARTER // P):
                words = turned[jb][:].rearrange("j u p e -> j u (p e)").bitcast(F32)
                for u in range(2):
                    nc.tensor.transpose(back[:, jb, u, :], words[:, u, :], ident[:])
            nc.scalar.copy(
                out=h_bf[b, q][:].bitcast(F32).rearrange("p (jb j) u -> p jb j u", j=P),
                in_=back.rearrange("p jb u j -> p jb j u"),
            )

        def add_rel_on_gpsimd(b, q, total):
            nc.gpsimd.tensor_tensor(total, later[b, q], rel_sb[b, q], ALU.add)
            h_bf[b, q] = held([P, QUARTER, PACK], BF16, f"h_first{b}{q}")
            nc.scalar.copy(
                out=h_bf[b, q][:].rearrange("p (c i) t -> p c t i", i=PACK),
                in_=total.rearrange("p t (c i) -> p c t i", i=PACK),
            )

        def quantise_h(b, q, words):
            h_w[b, q] = words
            h_s[b, q] = held([P, QUARTER], U8, f"h_s{b}{q}")
            nc.vector.quantize_mx(
                out=h_w[b, q][:].bitcast(FP8X4), scales=h_s[b, q][:], in_=h_bf[b, q][:].rearrange("p j t -> p (j t)")
            )

        def quantise_pair(q):
            words = held([P, 2, QUARTER], U32, f"h_w{q}")
            scales = held([P, 2, QUARTER], U8, f"h_s{q}")
            nc.vector.quantize_mx(
                out=words[:].rearrange("p b j -> p (b j)").bitcast(FP8X4),
                scales=scales[:].rearrange("p b j -> p (b j)"),
                in_=h_pair[q][:].rearrange("p b j t -> p (b j t)"),
            )
            for b in range(2):
                h_w[b, q] = words[:, b, :]
                h_s[b, q] = scales[:, b, :]

        def multiply(q, blocks, bank):
            acc = bank[:].rearrange("p (i j) -> p i j", j=QUARTER)[:, : len(blocks), :]
            for i, n in enumerate(blocks):
                for b in (1, 0):
                    nc.tensor.matmul_mx(
                        out=acc[:, i, :],
                        lhsT=w8_w[:, b, n * P : (n + 1) * P].bitcast(FP8X4),
                        lhsT_scale=w8_s[4 * b :, n * P : (n + 1) * P],
                        rhs=h_w[b, q][:].bitcast(FP8X4),
                        rhs_scale=h_s[b, q][:],
                        start=(b == 1),
                        stop=(b == 0),
                    )
            y_bank = rotating([P, HALF], F32, "y", 4)
            y = y_bank[:].rearrange("p (i j) -> p i j", j=QUARTER)
            nc.scalar.activation(out=y[:, : len(blocks), :], in_=acc, func=COPY, scale=-1.0)
            return [y[:, i, :] for i in range(len(blocks))]

        def scatter(n, y, first, width):
            nc.vector.tensor_tensor(
                page[n][:].indirect(places[:, first // PER_COLUMN : (first + width) // PER_COLUMN]),
                y,
                gains[:, first : first + width],
                ALU.mult,
            )

        def finish(q, blocks, bank):
            for n, y in zip(blocks, multiply(q, blocks, bank)):
                scatter(n, y, q * QUARTER, QUARTER)

        low, high = banks[:4], banks[4:]
        for a in range(2):
            for q in range(4):
                early_melt_pass(q, a)
        for a in range(2):
            round_w1_on_vector(a, 0, 0, pieces=1)
            round_w1_on_vector(a, 0, 1, pieces=2)
            quantise_w1(a, 0, 2, held([P, PASS], U32, f"w1_w{a}0"))
        for u in range(2):
            round_w1_on_vector(0, 1, u, pieces=1)
        third_melt = held([P, 2, PACK, QUARTER], F32, "third_melt")
        for t in range(PACK):
            late_melt(0, t, low[t], third_melt[:, :, t, :])
        for u in range(2):
            round_w1_on_scalar(1, 1, u)

        first_minima = taking_over([P, 2, PACK, QUARTER], F32, "tab_w0")
        mould_and_min(0, 0, high[2:], first_minima[:, 0])
        last_melt = [taking_over([P, 2, 2, QUARTER], F32, f"last{pair}") for pair in range(2)]
        last_minima = taking_over([P, 2, PACK, QUARTER], F32, "tab_w1")
        for i in range(2):
            neg_melt[1, i] = by_pairs(third_melt[:, i])
            neg_melt[1, 2 + i] = [last_melt[pair][:, i] for pair in range(2)]
            late_melt(1, i, high[i], last_melt[0][:, :, i, :])
        quantise_w1(0, 1, 1, held([P, PASS], U32, "w1_w01"))
        mould_and_min(0, 1, low[:2], first_minima[:, 1])
        mould_and_min(0, 2, low[2:], early_melt[1][:, 0])
        quantise_w1(1, 1, 2, taking_over([P, PASS], U32, "first_melt"))
        mould_and_min(0, 3, high[2:], as_t_j(after_w1[:, :S]))
        for i in range(2):
            late_melt(1, 2 + i, low[i], last_melt[1][:, :, i, :])

        add_rel_on_gpsimd(0, 0, as_t_j(after_w1[:, S:]))
        add_rel_on_gpsimd(0, 1, early_melt[1][:, 1])
        mould_and_min(1, 0, low[2:], third_melt[:, 0])
        mould_and_min(1, 1, high[2:], third_melt[:, 1])
        mould_and_min(1, 2, high[:2], last_minima[:, 0])
        mould_and_min(1, 3, low[:2], last_minima[:, 1])
        add_rel_on_vector(1, 0, taking_over([P, QUARTER, PACK], BF16, "last0"))
        first_words = taking_over([P, 2, 2, QUARTER], U32, "last1")
        for b in range(2):
            quantise_h(b, 0, first_words[:, 0, b, :])
        add_rel_on_vector(1, 1, h_bf[0, 0])
        for b in range(2):
            quantise_h(b, 1, first_words[:, 1, b, :])

        finish(0, (0,), high[0])
        finish(0, (1,), high[1])
        finish(0, (2, 3), low[2])
        finish(1, (0, 1), low[3])
        add_rel_on_tensor(0, 2, high[2:], high[1])

        promised = []
        for pair in range(2):
            both = rotating([P, 2, S], F32, "raw", 2)
            nc.sync.dma_start(
                out=both[:], in_=x0[2 * pair * P : 2 * (pair + 1) * P, :].rearrange("(i p) m -> p i m", p=P)
            )
            promised.append(both)

        add_rel_on_tensor(1, 2, low[2:], high[0])
        quantise_pair(2)
        finish(1, (2, 3), high[0])
        add_rel_on_tensor(0, 3, low[2:], high[1])
        finish(2, (0,), low[2])
        finish(2, (1, 2), low[3])
        add_rel_on_tensor(1, 3, low[2:], high[2])
        quantise_pair(3)
        finish(2, (3,), high[2])

        def store_page(n, width):
            for c in range(0, S, width):
                result = promised[n // 2][:, n % 2, c : c + width]
                nc.vector.tensor_tensor(result, page[n][:, c : c + width], result, ALU.max)
                nc.sync.dma_start(out=out[n * P : (n + 1) * P, c : c + width], in_=result)

        last = 3 * QUARTER
        for n in range(2):
            finish(3, (n,), low[n])
            store_page(n, S)
        y_third, y_fourth = multiply(3, (2, 3), high[3])
        scatter(2, y_third, last, QUARTER)
        store_page(2, S)
        for c in range(0, QUARTER, QUARTER // 2):
            scatter(3, y_fourth[:, c : c + QUARTER // 2], last + c, QUARTER // 2)
        store_page(3, S // LAST_PIECES)
